import numpy as np, ml_dtypes
CORES = [16,17,18,19,32,33,34,35]
N = 8
import mx_ref
BF = ml_dtypes.bfloat16
def tile(rs):
    return np.stack(rs, axis=2).reshape(128, -1).astype(BF)
def pick(q, e):
    c = np.concatenate([q[0].reshape(128, -1, 4), np.zeros((128, 1, 4), np.uint8)], axis=1); s = np.concatenate([q[1], np.ones((16, 1), np.uint8)], axis=1)
    return (np.ascontiguousarray(c[:, e].reshape(128, -1)), np.ascontiguousarray(s[:, e]))
def join(*qs):
    return (np.concatenate([q[0] for q in qs], axis=1), np.concatenate([q[1] for q in qs], axis=1))
def put(q, e, v):
    c, s = q[0].reshape(128, -1, 4).copy(), q[1].copy(); c[:, e] = v[0].reshape(128, -1, 4); s[:, e] = v[1]
    return (c.reshape(128, -1), s)
def pk(c, s):
    return (np.ascontiguousarray(c), mx_ref.live(s))
def emit(q):
    return q[0], q[1]
def packed(v, rng):
    q = [mx_ref.quantize(np.ascontiguousarray(v[r])) for r in range(N)]
    return np.stack([a for a, b in q]), np.stack([mx_ref.plane(b, rng) for a, b in q])
def values_of_codes():
    e, c = np.zeros((128, 128, 4), np.float32), np.zeros((128, 2, 4), np.uint8)
    e[np.arange(128), np.arange(128), 0] = 1
    c[:127, :, 0] = np.arange(256).reshape(2, 128).T[:127]
    return mx_ref.matmul(mx_ref.quantize(e.reshape(128, 512).astype(BF)), (c.reshape(128, 8), np.full((16, 2), 127, np.uint8))).T.reshape(-1).astype(np.float64)
CODE_VALUE, SCALE_VALUE = values_of_codes(), 2.0 ** (np.arange(256) - 127.0)
def decode(q):
    return (CODE_VALUE[q[0]].reshape(16, 8, -1, 4) * SCALE_VALUE[q[1]][:, None, :, None] + 0.0).reshape(128, -1).astype(np.float32)
def f(rng, *shape):
    return mx_ref.flush((rng.standard_normal(shape, dtype=np.float32) * np.exp2(rng.integers(-2, 3, shape[:-1] + (1,)))).astype(BF))
def wide(rng, *shape, cols=0):
    v = rng.standard_normal(shape, dtype=np.float32) * np.exp2(rng.integers(-12, 13, shape)).astype(np.float32)
    if cols: v *= np.repeat(np.exp2(rng.integers(-cols, cols + 1, shape[:-2] + (1, shape[-1] // 4))) * (rng.random(shape[:-2] + (1, shape[-1] // 4)) > 0.0625), 4, axis=-1).astype(np.float32)
    return mx_ref.flush(v.astype(BF))
C, H, E = 256, 64, 320
STEP = [1, 2, 4]
def parts(t, h, n):
    return np.ascontiguousarray(t.reshape(8, 16, -1, 4)[h, :, n].transpose(0, 2, 1, 3)).reshape(128, -1)
def big(v):
    v = v.astype(np.float32)
    v[np.abs(v) < np.float32(2.0 ** -16)] = 0
    return v.astype(BF)
def numbers_of(rng):
    return {"x": big(f(rng, N, 128, 4 * C)), "u": np.array(f(rng, N, 128, 512)), "v": np.array(f(rng, N, 128, 512))}
def edges(rng):
    return {"nb": rng.integers(0, E, (N, 4, C)).astype(np.int32), "e": rng.integers(0, 8, (N, 4, C)).astype(np.int32)}
def layers(rng):
    return big(f(rng, N, 128, 2048)).reshape(N, 8, 16, 4, 8, 16, 4)
def weights(rng, w):
    c, p = packed(np.ascontiguousarray(w).reshape(N, 128, 2048), rng)
    return {"wc": c, "ws": p}
def bare(u):
    u = u.reshape(N, 128, 128, 4)
    u[:, :, ::16] = 0
    u[:, :, 1::16] = 0
    u[:, :, 2] = 0
    return u
def setup_inputs(rng):
    return {**numbers_of(rng), **edges(rng), **weights(rng, layers(rng))}
def setup_inputs_ties(rng):
    d = numbers_of(rng)
    x = d["x"].reshape(N, 8, 16, C, 4)
    x[:, :, :3] = 0
    x[:, :, :3, :, 0] = rng.integers(1, 4, (N, 8, 3, C)).astype(np.float32).astype(BF)
    u = bare(d["u"])
    o = rng.permutation(N)
    for r in range(N):
        k = 0.0 if r == o[0] else -1.0 if r == o[1] else 1.0
        u[r, 2, 2, 0] = k
        for h in range(0, 128, 16):
            u[r, h, h, 0] = k
            u[r, h + 1, h + 1, 0] = k
    w = layers(rng)
    w[:, :, :, :, :, :3] = 0
    return {"x": x.reshape(N, 128, 4 * C), "u": u.reshape(N, 128, 512), "v": d["v"], **edges(rng), **weights(rng, w)}
def setup_inputs_near(rng):
    d = numbers_of(rng)
    x = d["x"].astype(np.float32).reshape(N, 8, 16, C, 4)
    u = bare(d["u"])
    o = rng.permutation(N) % 4
    x[:, :, 0] = 0
    x[:, :, 8:] = 0
    s = rng.integers(0, 16, (N, 8, 3, C))
    x[:, :, 8:11] = ((s[..., None] >> np.arange(4)) & 1) * np.exp2(np.arange(4) - 23.0)
    x[:, :, 11, :, 0] = 2.0 ** -10
    for r in range(N):
        x[r, :, 0, :, 0] = -1.0 if o[r] == 1 else 1.0
        if o[r] == 3:
            x[r, :, 8:] = 0
            x[r, :, 8:11, :, 0] = rng.choice([0.0, 1.0, 1.125], (8, 3, C)) * 2.0 ** -29
            x[r, :, 12, :, 0] = 2.0 ** -29
            for g in np.append(0, 1 + rng.permutation(7)[:3]): x[r, int(g), 8:11, int(rng.integers(C)), 0] = 2.0 ** 29
        k = 1.0 if o[r] == 0 else 2.0 ** -30
        for h, i, j in [(h, 8 + i, h + i) for h in range(0, 128, 16) for i in (0, 1)] + [(0, 10, 2)]:
            u[r, h + i, j] = k if o[r] < 3 or j == 2 else k * 1.25 if h < 64 else k * 1.125
            if o[r] < 2:
                u[r, h, j, 0] = k
                u[r, h + 11, j, 0] = k
        if o[r] == 2:
            a, b = [16 * int(h) for h in rng.permutation(8)[:2]]
            u[r, a, a, 0] = 1.0
            u[r, b, b, 0] = -1.0
            u[r, b, b + 1, 0] = -1.0
            m, n = [int(h) for h in rng.permutation(C)[:2]]
            x[r, :, 0, m, 1] = 1.0
            x[r, :, 0, n, 1] = -1.0
            u[r, 0, 2, 1] = 1.0
        if o[r] == 3: u[r, 12, 2, 0] = -k
    w = layers(rng)
    for i in [0] + [8 + k for k in range(8)]:
        w[:, :, i] = 0
        w[:, :, :, :, :, i] = 0
    return {"x": x.reshape(N, 128, 4 * C).astype(BF), "u": u.reshape(N, 128, 512), "v": d["v"], **edges(rng), **weights(rng, w)}
def setup_inputs_huge(rng):
    d = numbers_of(rng)
    o = rng.permutation(N)
    c = rng.integers(0, 2, (N, C)) * 2.0 - 1.0
    a = 2.0 ** 29 * (1.0 - 0.1 * rng.random((N, 8, 16, 17, 4)))
    for g in range(8):
        a[:, g, :, g] *= 2.0
        a[:, g, :, 8 + g] *= 2.0
    for r in range(N):
        if o[r] < 2: c[r] = -1.0
        if o[r] == 0:
            c[r, rng.permutation(C)[:H // 2]] = 1.0
            a[r] = 2.0 ** 30
            for g in range(8):
                a[r, 0, :7 - g, g] *= 0.5
                a[r, 0, :7 - g, 8 + g] *= 0.5
        if o[r] >= N // 2: a[r, :, :, 8:16] *= (rng.permutation(8) % 2 * 2.0 - 1.0)[:, None]
    x = (0.6 + 0.09 * rng.random((N, 8, 16, C, 4))) * c[:, None, None, :, None]
    x[o == 0] = 0.875 * np.sign(x[o == 0])
    u = bare(d["u"])
    u[:, :, [16 * h for h in range(8)] + [16 * h + 1 for h in range(8)] + [2]] = a.reshape(N, 128, 17, 4).astype(np.float32).astype(BF)
    w = np.zeros((N, 128, 4, 128, 4), np.float32)
    i = np.arange(128)
    for b in range(4): w[:, i, b, i, b] = 1
    return {"x": (2.0 ** 30 * x).astype(np.float32).reshape(N, 128, 4 * C).astype(BF), "u": u.reshape(N, 128, 512), "v": d["v"], **edges(rng), **weights(rng, w.astype(BF))}
def setup_inputs_few(rng):
    d = numbers_of(rng)
    x = (129 + 2 * rng.integers(0, 64, (N, 8, 16, C, 4))) * np.exp2(rng.integers(-14, -7, (N, 8, 16, C, 4)) - 7.0) * (rng.integers(0, 2, (N, 8, 16, C, 4)) * 2.0 - 1.0)
    x[:, :, ::8, :, 0] = 1.96875
    u = d["u"].reshape(N, 8, 16, 128, 4)
    u[:, :, ::8] = 0
    t = edges(rng)
    o = rng.permutation(N)
    t["nb"][o[0]] = E - 1
    t["nb"][o[1]] = np.arange(C)
    t["e"][o[1]] = 7
    t["nb"][o[2]] = C + rng.integers(0, H, (4, C))
    t["nb"][o[3]] = 0
    t["e"][o[3]] = 0
    w = layers(rng)
    w[:, :, :, :, :, 8:] = 0
    return {"x": (16.0 * x).astype(np.float32).reshape(N, 128, 4 * C).astype(BF), "u": u.reshape(N, 128, 512), "v": d["v"], **t, **weights(rng, w)}
def setup_inputs_spread(rng):
    d = setup_inputs(rng)
    d["x"] = big(wide(rng, N, 128, 4 * C, cols=6))
    return d
def check_inputs(d):
    b = []
    for k in ("x", "u", "v"):
        a = np.abs(d[k].astype(np.float32))
        if not (np.isfinite(a).all() and ((a == 0) | (a >= 2.0 ** -30) & (a <= 2.0 ** 30)).all()): b.append("a value of " + k)
    if not ((d["nb"] >= 0) & (d["nb"] < E)).all(): b.append("an entry of nb")
    if not ((d["e"] >= 0) & (d["e"] < 8)).all(): b.append("an entry of e")
    none, least, most = [emit(mx_ref.quantize(np.full((128, 16), k, np.float32).astype(BF)))[1][0, 0] for k in (0.0, 2.0 ** -30, 2.0 ** 30)]
    for r in range(N):
        if ((d["wc"][r] == 0x7F) | (d["wc"][r] == 0xFF)).any(): b.append("wc: a code that is no number")
        s = mx_ref.live(d["ws"][r])
        if ((s != none) & ((s < least) | (s > most))).any(): b.append("ws: a scale out of range")
    return b
def reference(x, u, v, nb, e, wc, ws):
    qu = [mx_ref.quantize(u[r]) for r in range(N)]
    lay = [pk(wc[r], ws[r]) for r in range(N)]
    now = [x[r] for r in range(N)]
    shift = e.astype(np.int64)
    g, i = np.arange(8), np.arange(C)
    for d in STEP:
        q = [mx_ref.quantize(now[r]) for r in range(N)]
        own = [mx_ref.matmul(qu[r], q[r]) + np.float32(0.0) for r in range(N)]
        border = [pick(q[r], np.argsort(-own[r][2], kind="stable")[:H]) for r in range(N)]
        made = []
        for r in range(N):
            came = border[(r + d) % N]
            p = np.concatenate([own[r], mx_ref.matmul(qu[r], came) + np.float32(0.0)], axis=1)
            val = decode(join(q[r], came))
            k = np.argmax(p[1::16], axis=0)
            shift[r] = (shift[r] + k[nb[r]] - k[:C]) % 8
            src = (g[:, None, None] + shift[r]) % 8
            c = np.argmax(p[::16][src, nb[r]], axis=1)
            a = parts(val, (g[:, None] + k[:C]) % 8, i)
            b = parts(val, np.take_along_axis(src, c[:, None], axis=1)[:, 0], nb[r][c, i])
            z = mx_ref.quantize(((a + b) * np.float32(0.5)).astype(BF))
            made.append(tile([np.maximum(mx_ref.matmul(pick(lay[r], np.arange(128 * t, 128 * t + 128)), z), np.float32(0.0)) * np.float32(0.03125) + a[:, t::4] for t in range(4)]))
        now = made
    y, oe = np.zeros((N, 128, C), np.float32), np.zeros((N, 4, C), np.float32)
    oc, osc = np.zeros((N, 128, 4 * C), np.uint8), np.zeros((N, 16, C), np.uint8)
    for r in range(N):
        q = mx_ref.quantize(now[r])
        y[r] = mx_ref.matmul(mx_ref.quantize(v[r]), q)
        oe[r] = shift[r]
        oc[r], osc[r] = emit(q)
    return {"y": y, "oe": oe, "oc": oc, "osc": osc}

@@ -1,0 +1,538 @@
+from concourse.mybir import dt, AluOpType as ALU, ActivationFunctionType as ACT
+
+F32, BF, I32, U16, MX, U8 = "float32", "bfloat16", "int32", "uint16", "float8_e4m3fn_x4", "uint8"
+STEP = [1, 2, 4]
+C, H = 256, 64
+FAR, MASK, PL = 4096, 4096 + 2047, 6144
+NPE = [4, 5, 5]
+NV = [1, 3, 3]
+EARLY = 6
+N1 = 9
+NS = 1
+POS = [0, 1, 4, 2, 5, 3, 6, 7, 8, 9, 10]
+
+
+def _s(n, d):
+    return ("sbuf", [128, n], d)
+
+
+SCRATCH = {
+    "ps": ("psum", [128, 4096], F32),
+    "xin": _s(1024, BF), "uin": _s(512, BF), "vin": _s(512, BF),
+    "wq": _s(512, MX), "wsc": _s(512, U8), "uq": _s(128, MX), "us": _s(128, U8), "vq": _s(128, MX), "vs": _s(128, U8),
+    "u2q": _s(128, MX), "u2s": _s(128, U8), "uaq": _s(400, MX), "uas": _s(400, U8),
+    "et": _s(1040, BF), "eq": _s(1024, MX), "es": _s(1024, U8),
+    "wt": _s(1536, BF), "cq": _s(384, MX), "cs": _s(384, U8),
+    "jm": _s(256, BF), "tri": _s(128, BF), "cn": _s(128, BF), "ch": _s(128, BF), "keep": _s(256, BF),
+    "fi": _s(352, F32), "ft": _s(352, F32), "rows": _s(64, F32), "col": _s(8, F32), "wa": _s(128, BF), "wb": _s(128, BF),
+    "l2": _s(8, U16), "lf": _s(64, F32), "ls": _s(64, U16), "lk": _s(16, U16),
+    "ia": _s(16, F32), "ni": _s(32, I32), "n0": _s(32, F32), "nf": _s(64, F32), "nt": _s(64, F32), "n16": _s(16, F32), "tmp": _s(48, F32),
+    "sc": _s(8, F32),
+    "dd": _s(256, BF), "fo": _s(256, BF), "fd": _s(256, BF), "rk": _s(256, BF), "oh": _s(512, BF), "ohq": _s(128, MX), "ohs": _s(128, U8),
+    "lt": _s(128, F32), "lb": _s(4, U16),
+    "f2": _s(256, F32), "ff": _s(1024, BF), "ffq": _s(256, MX), "ffs": _s(256, U8), "fb": _s(512, BF), "fbq": _s(128, MX), "fbs": _s(128, U8),
+    "kl": _s(320, BF), "ga": _s(256, BF), "ta": _s(256, BF), "sa": _s(256, BF), "gk": _s(256, BF), "tk": _s(256, BF), "sk": _s(256, BF),
+    "oa": _s(16, F32), "offa": _s(16, U16), "pre": _s(16, F32), "preu": _s(16, F32), "wi": _s(16, I32), "wr": _s(16, I32), "wx": _s(64, F32),
+    "ui": _s(16, I32), "uj": _s(16, I32), "offm": _s(16, U16), "sj": _s(32, I32), "ci": _s(64, I32),
+    "cand": _s(64, I32), "dc": _s(32, F32), "gm": _s(256, F32), "tm": _s(256, F32),
+    "e1": _s(32, F32), "e2": _s(32, F32), "e3": _s(32, F32), "e4": _s(16, F32), "e5": _s(32, F32), "e6": _s(16, F32), "e7": _s(16, F32), "e8": _s(16, F32),
+    "offb": _s(16, U16),
+    "win": _s(4 * PL, BF), "mk": _s(PL, F32),
+    "ah": _s(1024, BF), "af": _s(1024, BF), "z": _s(1024, BF), "zq": _s(256, MX), "zs": _s(256, U8), "rl": _s(1024, F32), "xn": _s(1024, BF),
+    "og": _s(32, F32), "ot": _s(32, F32), "yb": _s(256, F32),
+}
+for _r in range(4):
+    SCRATCH["q%d" % _r] = _s(256, MX)
+    SCRATCH["s%d" % _r] = _s(256, U8)
+for _r in range(3):
+    SCRATCH["bq%d" % _r] = _s(64, MX)
+    SCRATCH["bs%d" % _r] = _s(64, U8)
+    SCRATCH["lq%d" % _r] = _s(192, MX)
+    SCRATCH["lsc%d" % _r] = _s(192, U8)
+
+SEMAPHORES = ["V", "S", "P", "G", "dx", "du", "dw", "dv", "dn", "sw0", "sw1", "sw2", "sw3", "arr0", "arr1", "arr2", "sent", "out", "outa", "oute"]
+
+
+def width(name):
+    return SCRATCH[name][1][1]
+
+
+def R(name, c0=0, c1=None, step=1, p0=0, p1=128, pstep=1):
+    return (name, c0, width(name) if c1 is None else c1, step, p0, p1, pstep)
+
+
+def meets(a, b):
+    if a[0] != b[0] or a[5] <= b[4] or b[5] <= a[4] or a[2] <= b[1] or b[2] <= a[1]:
+        return False
+    if a[3] == b[3]:
+        return (a[1] - b[1]) % a[3] == 0
+    if a[3] == 1 or b[3] == 1:
+        return True
+    return bool(set(range(a[1], a[2], a[3])) & set(range(b[1], b[2], b[3])))
+
+
+def rank_program(g, core, T, topo):
+    rank = T.rank_of(core)
+    if rank is None:
+        return
+    n = len(T.cores)
+    Q = {"V": g.vector, "S": g.scalar, "P": g.tensor, "G": g, "Y": g.sync}
+    count = {k: 0 for k in SEMAPHORES}
+    known = {k: {} for k in Q}
+    clock = {}
+    log = {}
+
+    def ap(r):
+        if r[6] != 1:
+            return T[r[0]][r[4]:r[5]:r[6], r[1]:r[2]]
+        if r[3] != 1:
+            return T[r[0]][r[4]:r[5], r[1]:r[2]:r[3]]
+        return T[r[0]][r[4]:r[5], r[1]:r[2]]
+
+    def wait(q, sem, val):
+        if known[q].get(sem, 0) >= val:
+            return
+        Q[q].wait_ge(T.sem[sem], val)
+        known[q][sem] = val
+        for s, v in clock.get((sem, val), {}).items():
+            if known[q].get(s, 0) < v:
+                known[q][s] = v
+
+    def order(q, reads, writes):
+        need = {}
+        for regs, w in ((reads, False), (writes, True)):
+            for r in regs:
+                for (o, ow, oq, sem, val) in log.get(r[0], []):
+                    if oq == "P" and q == "P":
+                        continue
+                    hit = (w or ow) and meets(r, o)
+                    if r[0] == "ps" and oq != q and r[1] // 512 == o[1] // 512:
+                        hit = True
+                    if hit and need.get(sem, 0) < val:
+                        need[sem] = val
+        for sem in sorted(need, key=lambda s: (s == q, s)):
+            wait(q, sem, need[sem])
+
+    def note(q, reads, writes, sem, val):
+        clock[(sem, val)] = dict(known[q])
+        for regs, w in ((reads, False), (writes, True)):
+            for r in regs:
+                old = log.setdefault(r[0], [])
+                if w:
+                    old[:] = [e for e in old if e[0] != r]
+                old.append((r, w, q, sem, val))
+
+    def op(q, fn, reads, writes):
+        order(q, reads, writes)
+        fn().then_inc(T.sem[q], 1)
+        count[q] += 1
+        note(q, reads, writes, q, count[q])
+
+    def dmas(q, sem, items):
+        for (o, i, rd, wr) in items:
+            order(q, rd, wr)
+            Q[q].dma_start(o, i).then_inc(T.sem[sem], 16)
+            count[sem] += 16
+        for (o, i, rd, wr) in items:
+            note(q, rd, wr, sem, count[sem])
+
+    def src(a):
+        if len(a) == 2:
+            return ap(a[0]).indirect(ap(a[1])), [a[0], a[1]]
+        return ap(a), [a]
+
+    def copy(o, a):
+        v, rd = src(a)
+        op("V", lambda: g.vector.tensor_copy(ap(o), v), rd, [o])
+
+    def tt(o, a, b, alu):
+        v, rd = src(a)
+        op("V", lambda: g.vector.tensor_tensor(ap(o), v, ap(b), alu), rd + [b], [o])
+
+    def ts(o, a, s1, op0, s2=None, op1=None):
+        v, rd = src(a)
+        rd = rd + [s for s in (s1, s2) if isinstance(s, tuple)]
+        a1 = ap(s1) if isinstance(s1, tuple) else s1
+        a2 = ap(s2) if isinstance(s2, tuple) else s2
+        if op1 is None:
+            op("V", lambda: g.vector.tensor_scalar(ap(o), v, a1, None, op0), rd, [o])
+        else:
+            op("V", lambda: g.vector.tensor_scalar(ap(o), v, a1, a2, op0, op1), rd, [o])
+
+    def fill(o, c):
+        op("V", lambda: g.vector.memset(ap(o), c), [], [o])
+
+    def turn(o, a):
+        op("V", lambda: g.vector.transpose(ap(o), ap(a)), [a], [o])
+
+    def scan(o, a, b, op0, op1):
+        op("V", lambda: g.vector.tensor_tensor_scan(ap(o), ap(a), ap(b), 0.0, op0, op1), [a, b], [o])
+
+    def quant(oq, osc, a):
+        op("V", lambda: g.vector.quantize_mx(ap(oq), ap(osc), ap(a)), [a], [oq, osc])
+
+    def act(o, a, func=ACT.Copy, scale=None, bias=None):
+        v, rd = src(a)
+        kw = {}
+        if scale is not None:
+            kw["scale"] = scale
+        if bias is not None:
+            kw["bias"] = ap(bias) if isinstance(bias, tuple) else bias
+            rd = rd + ([bias] if isinstance(bias, tuple) else [])
+        op("S", lambda: g.scalar.activation(ap(o), v, func, **kw), rd, [o])
+
+    def lin(o, a, scale=None, bias=None):
+        act(o, a, ACT.Identity, scale, bias)
+
+    def pick_codes(o, w, off):
+        op("V", lambda: g.vector.tensor_copy(ap(o).bitcast(dt.uint32), ap(w).bitcast(dt.uint32).indirect(ap(off))), [w, off], [o])
+
+    def mm(bank, w, x, start=True, stop=True):
+        rs = [R(w[0], w[2], w[2] + w[3]), R(w[1], w[2], w[2] + w[3]), R(x[0], x[2], x[2] + x[3]), R(x[1], x[2], x[2] + x[3])]
+        o = R("ps", 512 * bank, 512 * bank + x[3])
+        op("P", lambda: g.tensor.matmul_mx(ap(o), ap(rs[0]), ap(rs[1]), ap(rs[2]), ap(rs[3]), start, stop), rs, [o])
+
+    def ps(bank, c0, c1):
+        return R("ps", 512 * bank + c0, 512 * bank + c1)
+
+    def iota(o, pattern, base, cm):
+        op("G", lambda: g.iota(ap(o), pattern, base, cm, allow_small_or_imprecise_dtypes=True), [], [o])
+
+    def F(f):
+        return R("ft", 32 * POS[f], 32 * POS[f] + 1)
+
+    def field(f, pattern, base=0, cm=0, c0=0, c1=32):
+        iota(R("fi", 32 * POS[f] + c0, 32 * POS[f] + c1), pattern, base, cm)
+
+    def col(k):
+        return R("col", k, k + 1)
+
+    def zeros(k):
+        return R("et", 0, 4 * k, 4)
+
+    U2, UF1, UF2 = ("u2q", "u2s", 0, 128), ("uaq", "uas", 0, 128), ("uaq", "uas", 128, 128)
+    WHI, WLO, WLOSS = ("cq", "cs", 0, 128), ("cq", "cs", 128, 128), ("cq", "cs", 256, 128)
+    LU, LKI, LU2, LU1, LNB, LEX, LOE, LA, LX7 = [R("ls", a, b) for a, b in
+                                                 ((0, 25), (26, 27), (28, 29), (30, 31), (32, 33), (34, 38), (38, 40), (40, 56), (56, 60))]
+
+    def scores(r, k, tile):
+        h = ("q%d" % r, "s%d" % r, 128 * k, 128)
+        quant(R(h[0], 128 * k, 128 * k + 128), R(h[1], 128 * k, 128 * k + 128), R(tile, 512 * k, 512 * k + 512))
+        if r == len(STEP):
+            return
+        mm(1 + 2 * k, h, U2)
+        mm(2 * k, U2, h)
+        act(R("sc", 4 * k, 4 * k + 1), ps(1 + 2 * k, 0, 1))
+        if k == 1:
+            mm(1, U2, h)
+        lin(R("dd", 128 * k, 128 * k + 128), ps(2 * k, 0, 128), -1.0, R("sc", 4 * k, 4 * k + 1))
+
+    def unit(b):
+        quant(R("eq", 256 * b, 256 * b + 240), R("es", 256 * b, 256 * b + 240), R("et", 3 - b, 963 - b))
+
+    dmas("Y", "dx", [(T.xin[:], T.x[:], [], [R("xin")])])
+    dmas("S", "du", [(T.uin[:], T.u[:], [], [R("uin")])])
+    iota(R("jm"), [[0, 2], [1, 128]], 0, -1)
+    field(0, [[0, 2], [1, 16]])
+    field(1, [[16, 2], [0, 16]], 0, 1)
+    field(3, [[0, 4], [1, 8]])
+    field(5, [[8, 4], [0, 8]], 0, 1)
+    iota(R("ch"), [[0, 16], [8, 8]], 0, 0)
+    iota(R("cn"), [[16, 4], [0, 2], [1, 16]], 0, 0)
+    field(2, [[0, 2], [16, 2], [0, 8]], 1)
+    field(4, [[0, 2], [1, 4], [0, 4]])
+    field(6, [[0, 8], [16, 4]], 7, 2)
+    field(7, [[0, 2], [2, 8], [0, 2]])
+    field(8, [[1, 32]])
+    for k in range(2):
+        field(9, [[1, 2], [2, 2], [8, 4]], 0, 0, 16 * k, 16 * k + 16)
+        field(10, [[1, 2], [4, 4], [8, 2]], 0, 0, 16 * k, 16 * k + 16)
+    iota(R("rows", 0, 8), [[0, 2], [32, 4]], 0, 0)
+    iota(R("rows", 8, 12), [[4, 4]], 0, 0)
+    iota(R("rows", 16, 32), [[32, 8], [0, 2]], 0, 0)
+    iota(R("rows", 32, 48), [[16, 16]], 0, 0)
+    iota(R("rows", 48, 64), [[0, 8], [256, 2]], 0, 0)
+    fill(R("ni"), 0)
+    fill(R("et"), 0.0)
+    fill(R("l2"), 2)
+    dmas("Y", "dn", [(ap(R("ni", 0, 16, 1, c, 128, 8)), T.nb[c, :], [], [R("ni")]) for c in range(4)]
+         + [(ap(R("ni", 16, 32, 1, c, 128, 8)), T.e[c, :], [], [R("ni")]) for c in range(4)])
+    dmas("Y", "dw", [(T.wq[:].bitcast(dt.uint8), T.wc[:], [], [R("wq")]), (T.wsc[:], T.ws[:], [], [R("wsc")])])
+    dmas("Y", "dv", [(T.vin[:], T.v[:], [], [R("vin")])])
+    for k in range(1, 4):
+        lin(R("ff", k, 1024, 4), zeros(256))
+    fill(R("oh"), 0.0)
+    ts(R("et", 3, 1024, 4), R("jm"), 0.0, ALU.is_equal)
+    ts(R("tri"), R("jm", 0, 128), 0.0, ALU.is_lt, 2.0 ** -100, ALU.mult)
+    lin(R("keep"), zeros(256), None, 1.0)
+    unit(0)
+    unit(1)
+    turn(R("ft", 0, 128), R("fi", 0, 128))
+    lin(col(2), F(3), 8.0)
+    lin(col(6), F(1), None, 128.0)
+    lin(R("wt", 0, 512, 2), zeros(256), None, F(1))
+    lin(R("wt", 1, 512, 2), zeros(256), None, col(6))
+    lin(R("wt", 512, 1024, 2), zeros(256), None, F(0))
+    lin(R("wt", 513, 1024, 2), zeros(256), None, F(0))
+    unit(2)
+    unit(3)
+    lin(R("keep", 0, 256, 16), zeros(16))
+    fill(R("wt", 1024, 1536), 0.0)
+    fill(R("fb"), 0.0)
+    fill(R("sj"), 0)
+    tt(col(3), col(2), F(5), ALU.is_gt)
+    quant(R("uq"), R("us"), R("uin"))
+    ts(R("wa"), R("ch"), F(5), ALU.is_equal, col(3), ALU.mult)
+    ts(R("wb"), R("ch"), col(2), ALU.is_equal, col(3), ALU.mult)
+    pick_codes(R("u2q"), R("uq"), R("l2"))
+    act(R("u2s"), (R("us"), R("l2")))
+    tt(R("wt", 1024, 1536, 4), R("wa"), R("wb"), ALU.subtract)
+    scores(0, 0, "xin")
+    scores(0, 1, "xin")
+    quant(R("cq"), R("cs"), R("wt"))
+    turn(R("ft", 128, 352), R("fi", 128, 352))
+
+    def lists():
+        lin(R("lf"), zeros(64))
+        lin(col(0), F(3), 16.0, 1.0)
+        lin(col(1), F(7), 8.0)
+        lin(R("lf", 0, 8), R("rows", 0, 8), None, F(2))
+        lin(R("lf", 8, 16), zeros(8), None, col(0))
+        lin(R("lf", 16, 25), zeros(9), None, col(1))
+        lin(col(7), F(8), 0.0625, F(7))
+        lin(R("lf", 26, 27), F(6))
+        lin(R("lf", 28, 29), F(0), -0.0625, col(7))
+        lin(R("lf", 32, 33), F(9))
+        lin(R("lf", 34, 38), R("rows", 8, 12), None, F(4))
+        lin(R("lf", 38, 39), F(10))
+        lin(R("lf", 39, 40), F(10), None, 2.0)
+        lin(R("lf", 30, 31), R("lf", 28, 29), 16.0, 7.0)
+        lin(R("lf", 40, 56), R("rows", 16, 32), None, F(8))
+        lin(R("lf", 56, 60), R("lf", 34, 38), 16.0, 7.0)
+        lin(col(4), F(3), -1.0)
+        lin(col(5), F(3), 256.0)
+        lin(R("ia"), R("rows", 32, 48), None, F(0))
+
+    def later_constants():
+        copy(R("ls"), R("lf"))
+        copy(R("n0"), R("ni"))
+        pick_codes(R("uaq"), R("uq"), LU)
+        act(R("uas"), (R("us"), LU))
+        for k in range(4):
+            act(R("nf", 16 * k, 16 * k + 16), R("n0", 16 * (k // 2), 16 * (k // 2) + 16))
+
+    def edges():
+        turn(R("nt"), R("nf"))
+        copy(R("n16"), (R("nt", 0, 32), LNB))
+        ts(R("tmp", 0, 16), (R("nt", 32, 64), LNB), 256.0, ALU.mult)
+        ts(R("tmp", 16, 32), R("n16"), float(C), ALU.is_ge, float(FAR - C), ALU.mult)
+        tt(R("tmp", 32, 48), R("tmp", 0, 16), R("n16"), ALU.add)
+        copy(R("lk"), (R("n16"), LU2))
+        tt(R("cand", 0, 64, 4), R("tmp", 32, 48), R("tmp", 16, 32), ALU.add)
+
+    def engines(k):
+        each = [set(topo.engines(T.cores[k], T.cores[(k - d) % n])) for d in STEP]
+        return sorted(each[0] & each[1] & each[2])
+
+    ring = [0]
+
+    def ring_bank():
+        ring[0] += 1
+        return 4 + (ring[0] - 1) % 4
+
+    def side(b, h):
+        if b == "m":
+            return ("uaq", "uas", 256 + 2 * h, 128)
+        return ("eq", "es", 256 * b + 16 * h, 128)
+
+    def unpack_half(r, b, h, k):
+        bank = ring_bank()
+        lo = PL * b + C * h + 128 * k
+        mm(bank, side(b, h), ("q%d" % r, "s%d" % r, 128 * k, 128))
+        act(R("win", lo, lo + 128), ps(bank, 0, 128), ACT.Copy, 0.5)
+
+    first = [(b, h) for b in range(4) for h in (1, 2, 3)] + [(b, 0) for b in range(4)]
+
+    for r, d in enumerate(STEP):
+        qn, sn, bq, bs, lq, lsc = "q%d" % r, "s%d" % r, "bq%d" % r, "bs%d" % r, "lq%d" % r, "lsc%d" % r
+        own, came = (qn, sn, 0, C), (lq, lsc, 0, 128)
+        npe = NPE[r]
+        todo = first + [("m", h) for h in range(8)] + [(b, h) for h in range(4, npe) for b in range(4)]
+        begun = first[:EARLY] if r else []
+
+        def place(b, h):
+            return R("mk", C * h, C * h + C) if b == "m" else R("win", PL * b + C * h, PL * b + C * h + C)
+
+        def unpack_own(k):
+            for _ in range(k):
+                b, h = todo.pop(0)
+                if (b, h) in begun:
+                    unpack_half(r, b, h, 1)
+                    continue
+                bank = ring_bank()
+                mm(bank, side(b, h), own)
+                act(place(b, h), ps(bank, 0, C), ACT.Copy, None if b == "m" else 0.5)
+
+        def exchange(b):
+            dmas("Y", "sw%d" % b, [(ap(o), ap(i), [i], [o]) for (o, i) in
+                                   [(R("win", PL * b + C * npe, PL * b + 2048, 1, 64 * k, 64 * k + 64),
+                                     R("win", PL * b + C * (npe - 4), PL * b + 1024, 1, 64 - 64 * k, 128 - 64 * k))
+                                    for k in range(2)]])
+
+        if r == 0:
+            lists()
+        unpack_own(4 if r == 0 else N1)
+        for b in range(NS if r else 0):
+            exchange(b)
+        tt(R("fd", 0, 128), R("dd", 0, 128), R("tri"), ALU.is_lt)
+        ts(R("fo", 0, 128), ps(1, 0, 128), R("sc", 0, 1), ALU.is_gt)
+        ts(R("fo", 128, 256), ps(0, 0, 128), R("sc", 4, 5), ALU.is_ge)
+        scan(R("rk", 0, 128), R("fd", 0, 128), R("fo", 0, 128), ALU.add, ALU.add)
+        tt(R("fd", 128, 256), R("dd", 128, 256), R("tri"), ALU.is_lt)
+        ts(R("oh", 0, 512, 4), R("cn"), R("rk", 127, 128), ALU.is_equal)
+        scan(R("rk", 128, 256), R("fd", 128, 256), R("fo", 128, 256), ALU.add, ALU.add)
+        ts(R("oh", 1, 512, 4), R("cn"), R("rk", 255, 256), ALU.is_equal)
+        quant(R("ohq"), R("ohs"), R("oh"))
+        mm(0, WHI, ("ohq", "ohs", 0, 128), True, False)
+        mm(0, WLO, ("ohq", "ohs", 0, 128), False, True)
+        turn(R("lt"), ps(0, 0, 128))
+        copy(R("lb"), R("lt", 0, 128, 32))
+        pick_codes(R(bq), R(qn), R("lb"))
+        copy(R(bs), (R(sn), R("lb")))
+        rid, pid, _ = topo.addr(T.cores[(rank - d) % n])
+        for (a, o, rg) in ((T[bq][:].bitcast(dt.uint8), T[lq][:, 0:H].bitcast(dt.uint8), R(bq)), (T[bs][:], T[lsc][:, 0:H], R(bs))):
+            order("G", [rg], [])
+            g.remote_dma(o, a, T.sem["arr%d" % r], T.sem.sent, pid, rid, sum(1 << e for e in engines(rank)))
+            count["sent"] += len(engines(rank))
+        count["arr%d" % r] = 2 * len(engines((rank + d) % n))
+        note("G", [], [R(lq, 0, H), R(lsc, 0, H)], "arr%d" % r, count["arr%d" % r])
+        clock[("arr%d" % r, count["arr%d" % r])] = {}
+        if r == 0:
+            later_constants()
+            unpack_own(4)
+
+        mm(1, UF1, own)
+        mm(2, UF2, own)
+        unpack_own(6)
+        copy(R("f2"), ps(1, 0, C))
+        tt(R("ff", 0, 1024, 4), ps(2, 0, C), R("f2"), ALU.is_gt)
+        quant(R("ffq"), R("ffs"), R("ff"))
+        mm(3, WLOSS, ("ffq", "ffs", 0, C))
+        quant(R(lq, 64, 192), R(lsc, 64, 192), R("xn" if r else "xin", 0, 512))
+        if r == 0:
+            edges()
+        unpack_own(3)
+        ts(R("kl", 0, C), ps(3, 0, C), col(4), ALU.is_equal, col(5), ALU.mult)
+        mine = [todo.pop() for _ in range(NV[r])]
+        for k, (b, h) in enumerate(mine[:3]):
+            mm(k, side(b, h), own)
+        unpack_own(min(4, len(todo)))
+        wait("Y", "sent", count["sent"])
+        for b in range(NS if r else 0, 4):
+            exchange(b)
+        copy(R("ga"), (R("kl", 0, C), LA))
+        turn(R("ta"), R("ga"))
+        scan(R("sa"), R("keep"), R("ta"), ALU.mult, ALU.add)
+        ts(R("pre"), (R("sa"), LKI), -1.0, ALU.mult, 2048.0, ALU.add)
+        tt(R("oa"), R("sa", 7, 256, 16), R("ia"), ALU.add)
+        tt(R("wi"), R("pre"), R("cand", 0, 64, 4), ALU.add)
+        copy(R("offa"), R("oa"))
+        ts(R("wr"), R("wi"), MASK, ALU.bitwise_and)
+        tt(R("preu"), (R("wr"), LU2), R("rows", 48, 64), ALU.add)
+        copy(R("wx"), (R("wr"), LEX))
+        for k, (b, h) in enumerate(mine):
+            if k >= 3:
+                unpack_own(min(2, len(todo)))
+                mm(k % 3, side(b, h), own)
+            if b == "m":
+                copy(place(b, h), ps(k % 3, 0, C))
+            else:
+                ts(place(b, h), ps(k % 3, 0, C), 0.5, ALU.mult)
+        unpack_own(len(todo))
+        if r == 1:
+            quant(R("vq"), R("vs"), R("vin"))
+
+        mm(1, UF1, came)
+        mm(2, UF2, came)
+        late = [("m", h) for h in range(8)] + [(b, h) for b in range(4) for h in range(8)]
+
+        def unpack_came(k):
+            for _ in range(k):
+                b, h = late.pop(0)
+                bank = ring_bank()
+                mm(bank, side(b, h), came)
+                if b == "m":
+                    act(R("mk", FAR + C * h, FAR + C * h + H), ps(bank, 0, H))
+                else:
+                    act(R("win", PL * b + FAR + C * h, PL * b + FAR + C * h + H), ps(bank, 0, H), ACT.Copy, 0.5)
+
+        unpack_came(6)
+        copy(R("f2", 0, H), ps(1, 0, H))
+        tt(R("fb", 0, 4 * H, 4), ps(2, 0, H), R("f2", 0, H), ALU.is_gt)
+        quant(R("fbq"), R("fbs"), R("fb"))
+        mm(3, WLOSS, ("fbq", "fbs", 0, 128))
+        unpack_came(34)
+        ts(R("kl", C, C + H), ps(3, 0, H), col(4), ALU.is_equal, col(5), ALU.mult)
+        copy(R("gk"), (R("kl"), R("lk")))
+        turn(R("tk"), R("gk"))
+        scan(R("sk"), R("keep"), R("tk"), ALU.mult, ALU.add)
+        tt(R("ui"), (R("sk"), LU1), R("preu"), ALU.add)
+        tt(R("ci"), (R("sk"), LX7), R("wx"), ALU.add)
+        ts(R("uj"), R("ui"), MASK, ALU.bitwise_and)
+        ts(R("cand"), R("ci"), MASK, ALU.bitwise_and)
+        copy(R("offm"), R("uj"))
+        tt(R("dc"), R("cand", 32, 64), R("cand", 0, 32), ALU.subtract)
+        copy(R("gm"), (R("mk"), R("offm")))
+        turn(R("tm"), R("gm"))
+        even, odd = R("tm", 0, 128, 4), R("tm", 128, 256, 4)
+        tt(R("e1"), odd, even, ALU.is_gt)
+        tt(R("e2"), odd, even, ALU.max)
+        tt(R("e3"), R("e1"), R("dc"), ALU.mult)
+        tt(R("e4"), R("e2", 16, 32), R("e2", 0, 16), ALU.is_gt)
+        tt(R("e5"), R("e3"), R("cand", 0, 32), ALU.add)
+        tt(R("e6"), R("e5", 16, 32), R("e5", 0, 16), ALU.subtract)
+        tt(R("e7"), R("e6"), R("e4"), ALU.mult)
+        tt(R("e8"), R("e7"), R("e5", 0, 16), ALU.add)
+        for b in range(4):
+            act(R("ah", 256 * b, 256 * b + 256), (R("win", PL * b, PL * b + 2048), R("offa")))
+        for a in range(4):
+            for k in range(4):
+                copy(R("offb", 4 * a, 4 * a + 4, 1, 32 * k, 32 * k + 32), R("e8", k, 16, 4, 32 * a, 32 * a + 32))
+        for k in range(2):
+            for b in range(4):
+                tt(R("z", 512 * k + b, 512 * k + 512, 4), (R("win", PL * b, PL * b + PL), R("offb", 8 * k, 8 * k + 8)),
+                   R("ah", 256 * b + 128 * k, 256 * b + 128 * k + 128), ALU.add)
+            quant(R("zq", 128 * k, 128 * k + 128), R("zs", 128 * k, 128 * k + 128), R("z", 512 * k, 512 * k + 512))
+            for b in range(4):
+                mm(4 * k + b, ("wq", "wsc", 128 * b, 128), ("zq", "zs", 128 * k, 128))
+            if k == 0:
+                act(R("af"), R("ah"), ACT.Copy, 2.0)
+            for b in range(4):
+                act(R("rl", 256 * b + 128 * k, 256 * b + 128 * k + 128), ps(4 * k + b, 0, 128), ACT.Relu, 0.03125)
+        if r == 2:
+            ts(R("sj", 0, 16), R("cand", 0, 64, 4), 8, ALU.arith_shift_right, 7, ALU.bitwise_and)
+            copy(R("og"), (R("sj"), LOE))
+            turn(R("ot"), R("og"))
+            dmas("Y", "oute", [(T.oe[c, :], ap(R("ot", 0, 16, 1, c, 128, 8)), [R("ot")], []) for c in range(4)])
+        for k in range(2):
+            for b in range(4):
+                lo = 256 * b + 128 * k
+                tt(R("xn", 512 * k + b, 512 * k + 512, 4), R("rl", lo, lo + 128), R("af", lo, lo + 128), ALU.add)
+            scores(r + 1, k, "xn")
+            if k == 0 and r < 2:
+                for (b, h) in first[:EARLY]:
+                    unpack_half(r + 1, b, h, 0)
+            if r == 2:
+                mm(k, ("vq", "vs", 0, 128), ("q3", "s3", 128 * k, 128))
+                act(R("yb", 128 * k, 128 * k + 128), ps(k, 0, 128))
+                if k == 0:
+                    dmas("Y", "outa", [(T.oc[:, 0:512], T.q3[:, 0:128].bitcast(dt.uint8), [R("q3", 0, 128)], []),
+                                       (T.y[:, 0:128], T.yb[:, 0:128], [R("yb", 0, 128)], [])])
+
+    dmas("S", "out", [(T.y[:, 128:256], T.yb[:, 128:256], [R("yb", 128, 256)], [])])
+    dmas("Y", "out", [(T.oc[:, 512:1024], T.q3[:, 128:256].bitcast(dt.uint8), [R("q3")], [])]
+         + [(T.osc[4 * k:4 * k + 4, :], T.s3[32 * k:32 * k + 4, :], [R("s3")], []) for k in range(4)])
+    for sem in SEMAPHORES:
+        if count[sem]:
+            known["G"].pop(sem, None)
+            wait("G", sem, count[sem])

@@ -8,7 +8,7 @@ NPE = [4, 5, 5]
 NV = [1, 3, 3]
 EARLY = 6
 N1 = 9
-NS = 1
+NS = 2
 POS = [0, 1, 4, 2, 5, 3, 6, 7, 8, 9, 10]
 
 
@@ -35,8 +35,8 @@ SCRATCH = {
     "oa": _s(16, F32), "offa": _s(16, U16), "pre": _s(16, F32), "preu": _s(16, F32), "wi": _s(16, I32), "wr": _s(16, I32), "wx": _s(64, F32),
     "ui": _s(16, I32), "uj": _s(16, I32), "offm": _s(16, U16), "sj": _s(32, I32), "ci": _s(64, I32),
     "cand": _s(64, I32), "dc": _s(32, F32), "gm": _s(256, F32), "tm": _s(256, F32),
-    "e1": _s(32, F32), "e2": _s(32, F32), "e3": _s(32, F32), "e4": _s(16, F32), "e5": _s(32, F32), "e6": _s(16, F32), "e7": _s(16, F32), "e8": _s(16, F32),
-    "offb": _s(16, U16),
+    "e1": _s(32, F32), "e2": _s(32, F32), "e3": _s(32, F32), "e4": _s(32, F32), "e5": _s(32, F32), "e6": _s(32, F32), "e8": _s(16, F32),
+    "offb": _s(16, U16), "ob": _s(8, F32),
     "win": _s(4 * PL, BF), "mk": _s(PL, F32),
     "ah": _s(1024, BF), "af": _s(1024, BF), "z": _s(1024, BF), "zq": _s(256, MX), "zs": _s(256, U8), "rl": _s(1024, F32), "xn": _s(1024, BF),
     "og": _s(32, F32), "ot": _s(32, F32), "yb": _s(256, F32),
@@ -222,10 +222,9 @@ def rank_program(g, core, T, topo):
             return
         mm(1 + 2 * k, h, U2)
         mm(2 * k, U2, h)
-        act(R("sc", 4 * k, 4 * k + 1), ps(1 + 2 * k, 0, 1))
-        if k == 1:
-            mm(1, U2, h)
-        lin(R("dd", 128 * k, 128 * k + 128), ps(2 * k, 0, 128), -1.0, R("sc", 4 * k, 4 * k + 1))
+        if k == 0:
+            act(R("sc", 0, 1), ps(1, 0, 1))
+            lin(R("dd", 0, 128), ps(0, 0, 128), -1.0, R("sc", 0, 1))
 
     def unit(b):
         quant(R("eq", 256 * b, 256 * b + 240), R("es", 256 * b, 256 * b + 240), R("et", 3 - b, 963 - b))
@@ -301,13 +300,13 @@ def rank_program(g, core, T, topo):
         lin(R("lf", 16, 25), zeros(9), None, col(1))
         lin(col(7), F(8), 0.0625, F(7))
         lin(R("lf", 26, 27), F(6))
-        lin(R("lf", 28, 29), F(0), -0.0625, col(7))
         lin(R("lf", 32, 33), F(9))
         lin(R("lf", 34, 38), R("rows", 8, 12), None, F(4))
+        lin(R("lf", 28, 29), F(0), -0.0625, col(7))
         lin(R("lf", 38, 39), F(10))
         lin(R("lf", 39, 40), F(10), None, 2.0)
-        lin(R("lf", 30, 31), R("lf", 28, 29), 16.0, 7.0)
         lin(R("lf", 40, 56), R("rows", 16, 32), None, F(8))
+        lin(R("lf", 30, 31), R("lf", 28, 29), 16.0, 7.0)
         lin(R("lf", 56, 60), R("lf", 34, 38), 16.0, 7.0)
         lin(col(4), F(3), -1.0)
         lin(col(5), F(3), 256.0)
@@ -385,12 +384,13 @@ def rank_program(g, core, T, topo):
         for b in range(NS if r else 0):
             exchange(b)
         tt(R("fd", 0, 128), R("dd", 0, 128), R("tri"), ALU.is_lt)
-        ts(R("fo", 0, 128), ps(1, 0, 128), R("sc", 0, 1), ALU.is_gt)
-        ts(R("fo", 128, 256), ps(0, 0, 128), R("sc", 4, 5), ALU.is_ge)
-        scan(R("rk", 0, 128), R("fd", 0, 128), R("fo", 0, 128), ALU.add, ALU.add)
+        ts(R("dd", 128, 256), ps(2, 0, 128), ps(3, 0, 1), ALU.subtract, -1.0, ALU.mult)
+        ts(R("fo", 0, 128), ps(2, 0, 128), R("sc", 0, 1), ALU.is_gt)
+        ts(R("fo", 128, 256), ps(0, 0, 128), ps(3, 0, 1), ALU.is_ge)
         tt(R("fd", 128, 256), R("dd", 128, 256), R("tri"), ALU.is_lt)
-        ts(R("oh", 0, 512, 4), R("cn"), R("rk", 127, 128), ALU.is_equal)
+        scan(R("rk", 0, 128), R("fd", 0, 128), R("fo", 0, 128), ALU.add, ALU.add)
         scan(R("rk", 128, 256), R("fd", 128, 256), R("fo", 128, 256), ALU.add, ALU.add)
+        ts(R("oh", 0, 512, 4), R("cn"), R("rk", 127, 128), ALU.is_equal)
         ts(R("oh", 1, 512, 4), R("cn"), R("rk", 255, 256), ALU.is_equal)
         quant(R("ohq"), R("ohs"), R("oh"))
         mm(0, WHI, ("ohq", "ohs", 0, 128), True, False)
@@ -424,15 +424,27 @@ def rank_program(g, core, T, topo):
         unpack_own(3)
         ts(R("kl", 0, C), ps(3, 0, C), col(4), ALU.is_equal, col(5), ALU.mult)
         mine = [todo.pop() for _ in range(NV[r])]
-        for k, (b, h) in enumerate(mine[:3]):
+        for k, (b, h) in enumerate(mine):
             mm(k, side(b, h), own)
         unpack_own(min(4, len(todo)))
         wait("Y", "sent", count["sent"])
         for b in range(NS if r else 0, 4):
             exchange(b)
+
+        def take(k):
+            if k < len(mine):
+                b, h = mine[k]
+                if b == "m":
+                    copy(place(b, h), ps(k, 0, C))
+                else:
+                    ts(place(b, h), ps(k, 0, C), 0.5, ALU.mult)
+
         copy(R("ga"), (R("kl", 0, C), LA))
+        take(0)
         turn(R("ta"), R("ga"))
+        take(1)
         scan(R("sa"), R("keep"), R("ta"), ALU.mult, ALU.add)
+        take(2)
         ts(R("pre"), (R("sa"), LKI), -1.0, ALU.mult, 2048.0, ALU.add)
         tt(R("oa"), R("sa", 7, 256, 16), R("ia"), ALU.add)
         tt(R("wi"), R("pre"), R("cand", 0, 64, 4), ALU.add)
@@ -440,14 +452,6 @@ def rank_program(g, core, T, topo):
         ts(R("wr"), R("wi"), MASK, ALU.bitwise_and)
         tt(R("preu"), (R("wr"), LU2), R("rows", 48, 64), ALU.add)
         copy(R("wx"), (R("wr"), LEX))
-        for k, (b, h) in enumerate(mine):
-            if k >= 3:
-                unpack_own(min(2, len(todo)))
-                mm(k % 3, side(b, h), own)
-            if b == "m":
-                copy(place(b, h), ps(k % 3, 0, C))
-            else:
-                ts(place(b, h), ps(k % 3, 0, C), 0.5, ALU.mult)
         unpack_own(len(todo))
         if r == 1:
             quant(R("vq"), R("vs"), R("vin"))
@@ -455,11 +459,13 @@ def rank_program(g, core, T, topo):
         mm(1, UF1, came)
         mm(2, UF2, came)
         late = [("m", h) for h in range(8)] + [(b, h) for b in range(4) for h in range(8)]
+        wide = [0, 4, 5, 6, 7]
 
         def unpack_came(k):
             for _ in range(k):
                 b, h = late.pop(0)
-                bank = ring_bank()
+                bank = wide.pop(0)
+                wide.append(bank)
                 mm(bank, side(b, h), came)
                 if b == "m":
                     act(R("mk", FAR + C * h, FAR + C * h + H), ps(bank, 0, H))
@@ -471,37 +477,50 @@ def rank_program(g, core, T, topo):
         tt(R("fb", 0, 4 * H, 4), ps(2, 0, H), R("f2", 0, H), ALU.is_gt)
         quant(R("fbq"), R("fbs"), R("fb"))
         mm(3, WLOSS, ("fbq", "fbs", 0, 128))
-        unpack_came(34)
+        wide[:0] = [1, 2]
+        unpack_came(2)
         ts(R("kl", C, C + H), ps(3, 0, H), col(4), ALU.is_equal, col(5), ALU.mult)
-        copy(R("gk"), (R("kl"), R("lk")))
-        turn(R("tk"), R("gk"))
-        scan(R("sk"), R("keep"), R("tk"), ALU.mult, ALU.add)
+        copy(R("gk", 0, 128), (R("kl"), R("lk", 0, 8)))
+        act(R("gk", 128, 256), (R("kl"), R("lk", 8, 16)))
+        unpack_came(len(late))
+        for k in range(2):
+            turn(R("tk", 128 * k, 128 * k + 128), R("gk", 128 * k, 128 * k + 128))
+        for k in range(2):
+            scan(R("sk", 128 * k, 128 * k + 128), R("keep", 0, 128), R("tk", 128 * k, 128 * k + 128), ALU.mult, ALU.add)
         tt(R("ui"), (R("sk"), LU1), R("preu"), ALU.add)
         tt(R("ci"), (R("sk"), LX7), R("wx"), ALU.add)
         ts(R("uj"), R("ui"), MASK, ALU.bitwise_and)
         ts(R("cand"), R("ci"), MASK, ALU.bitwise_and)
         copy(R("offm"), R("uj"))
         tt(R("dc"), R("cand", 32, 64), R("cand", 0, 32), ALU.subtract)
-        copy(R("gm"), (R("mk"), R("offm")))
-        turn(R("tm"), R("gm"))
+        for k in range(2):
+            copy(R("gm", 128 * k, 128 * k + 128), (R("mk"), R("offm", 8 * k, 8 * k + 8)))
+        for k in range(2):
+            turn(R("tm", 128 * k, 128 * k + 128), R("gm", 128 * k, 128 * k + 128))
         even, odd = R("tm", 0, 128, 4), R("tm", 128, 256, 4)
         tt(R("e1"), odd, even, ALU.is_gt)
         tt(R("e2"), odd, even, ALU.max)
         tt(R("e3"), R("e1"), R("dc"), ALU.mult)
-        tt(R("e4"), R("e2", 16, 32), R("e2", 0, 16), ALU.is_gt)
+        tt(R("e4", 0, 16), R("e2", 16, 32), R("e2", 0, 16), ALU.is_le)
+        tt(R("e4", 16, 32), R("e2", 16, 32), R("e2", 0, 16), ALU.is_gt)
         tt(R("e5"), R("e3"), R("cand", 0, 32), ALU.add)
-        tt(R("e6"), R("e5", 16, 32), R("e5", 0, 16), ALU.subtract)
-        tt(R("e7"), R("e6"), R("e4"), ALU.mult)
-        tt(R("e8"), R("e7"), R("e5", 0, 16), ALU.add)
+        tt(R("e6"), R("e5"), R("e4"), ALU.mult)
+        tt(R("e8"), R("e6", 0, 16), R("e6", 16, 32), ALU.add)
         for b in range(4):
             act(R("ah", 256 * b, 256 * b + 256), (R("win", PL * b, PL * b + 2048), R("offa")))
         for a in range(4):
             for k in range(4):
-                copy(R("offb", 4 * a, 4 * a + 4, 1, 32 * k, 32 * k + 32), R("e8", k, 16, 4, 32 * a, 32 * a + 32))
+                i = R("e8", k, 16, 4, 32 * a, 32 * a + 32)
+                if a == 3:
+                    act(R("ob", 4, 8, 1, 32 * k, 32 * k + 32), i)
+                else:
+                    copy(R("offb", 4 * a, 4 * a + 4, 1, 32 * k, 32 * k + 32), i)
         for k in range(2):
             for b in range(4):
                 tt(R("z", 512 * k + b, 512 * k + 512, 4), (R("win", PL * b, PL * b + PL), R("offb", 8 * k, 8 * k + 8)),
                    R("ah", 256 * b + 128 * k, 256 * b + 128 * k + 128), ALU.add)
+            if k == 0:
+                copy(R("offb", 12, 16), R("ob", 4, 8))
             quant(R("zq", 128 * k, 128 * k + 128), R("zs", 128 * k, 128 * k + 128), R("z", 512 * k, 512 * k + 512))
             for b in range(4):
                 mm(4 * k + b, ("wq", "wsc", 128 * b, 128), ("zq", "zs", 128 * k, 128))

@@ -4,10 +4,9 @@ F32, BF, I32, U16, MX, U8 = "float32", "bfloat16", "int32", "uint16", "float8_e4
 STEP = [1, 2, 4]
 C, H = 256, 64
 FAR, MASK, PL = 4096, 4096 + 2047, 6144
-NPE = [4, 5, 5]
-NV = [1, 3, 3]
+NPE = 5
+NV = [2, 3, 3]
 EARLY = 6
-N1 = 9
 NS = 2
 POS = [0, 1, 4, 2, 5, 3, 6, 7, 8, 9, 10]
 
@@ -34,8 +33,8 @@ SCRATCH = {
     "kl": _s(320, BF), "ga": _s(256, BF), "ta": _s(256, BF), "sa": _s(256, BF), "gk": _s(256, BF), "tk": _s(256, BF), "sk": _s(256, BF),
     "oa": _s(16, F32), "offa": _s(16, U16), "pre": _s(16, F32), "preu": _s(16, F32), "wi": _s(16, I32), "wr": _s(16, I32), "wx": _s(64, F32),
     "ui": _s(16, I32), "uj": _s(16, I32), "offm": _s(16, U16), "sj": _s(32, I32), "ci": _s(64, I32),
-    "cand": _s(64, I32), "dc": _s(32, F32), "gm": _s(256, F32), "tm": _s(256, F32),
-    "e1": _s(32, F32), "e2": _s(32, F32), "e3": _s(32, F32), "e4": _s(32, F32), "e5": _s(32, F32), "e6": _s(32, F32), "e8": _s(16, F32),
+    "cand": _s(64, I32), "gm": _s(256, F32), "tm": _s(256, F32),
+    "e2": _s(32, F32), "e5": _s(96, F32), "d0": _s(96, F32), "d1": _s(96, F32), "e8": _s(16, F32),
     "offb": _s(16, U16), "ob": _s(8, F32),
     "win": _s(4 * PL, BF), "mk": _s(PL, F32),
     "ah": _s(1024, BF), "af": _s(1024, BF), "z": _s(1024, BF), "zq": _s(256, MX), "zs": _s(256, U8), "rl": _s(1024, F32), "xn": _s(1024, BF),
@@ -279,6 +278,8 @@ def rank_program(g, core, T, topo):
     fill(R("wt", 1024, 1536), 0.0)
     fill(R("fb"), 0.0)
     fill(R("sj"), 0)
+    lin(R("d0"), zeros(96))
+    lin(R("d1"), zeros(96))
     tt(col(3), col(2), F(5), ALU.is_gt)
     quant(R("uq"), R("us"), R("uin"))
     ts(R("wa"), R("ch"), F(5), ALU.is_equal, col(3), ALU.mult)
@@ -321,7 +322,6 @@ def rank_program(g, core, T, topo):
             act(R("nf", 16 * k, 16 * k + 16), R("n0", 16 * (k // 2), 16 * (k // 2) + 16))
 
     def edges():
-        turn(R("nt"), R("nf"))
         copy(R("n16"), (R("nt", 0, 32), LNB))
         ts(R("tmp", 0, 16), (R("nt", 32, 64), LNB), 256.0, ALU.mult)
         ts(R("tmp", 16, 32), R("n16"), float(C), ALU.is_ge, float(FAR - C), ALU.mult)
@@ -350,17 +350,31 @@ def rank_program(g, core, T, topo):
         mm(bank, side(b, h), ("q%d" % r, "s%d" % r, 128 * k, 128))
         act(R("win", lo, lo + 128), ps(bank, 0, 128), ACT.Copy, 0.5)
 
+    def exchange(b):
+        dmas("Y", "sw%d" % b, [(ap(o), ap(i), [i], [o]) for (o, i) in
+                               [(R("win", PL * b + C * NPE, PL * b + 2048, 1, 64 * k, 64 * k + 64),
+                                 R("win", PL * b + C * (NPE - 4), PL * b + 1024, 1, 64 - 64 * k, 128 - 64 * k))
+                                for k in range(2)]])
+
+    def place(b, h):
+        return R("mk", C * h, C * h + C) if b == "m" else R("win", PL * b + C * h, PL * b + C * h + C)
+
+    def mean(k, b):
+        tt(R("z", 512 * k + b, 512 * k + 512, 4), (R("win", PL * b, PL * b + PL), R("offb", 8 * k, 8 * k + 8)),
+           R("ah", 256 * b + 128 * k, 256 * b + 128 * k + 128), ALU.add)
+
+    def state(k, b):
+        lo = 256 * b + 128 * k
+        tt(R("xn", 512 * k + b, 512 * k + 512, 4), R("rl", lo, lo + 128), R("af", lo, lo + 128), ALU.add)
+
     first = [(b, h) for b in range(4) for h in (1, 2, 3)] + [(b, 0) for b in range(4)]
+    more = [(b, h) for h in range(4, NPE) for b in range(4)]
 
     for r, d in enumerate(STEP):
         qn, sn, bq, bs, lq, lsc = "q%d" % r, "s%d" % r, "bq%d" % r, "bs%d" % r, "lq%d" % r, "lsc%d" % r
         own, came = (qn, sn, 0, C), (lq, lsc, 0, 128)
-        npe = NPE[r]
-        todo = first + [("m", h) for h in range(8)] + [(b, h) for h in range(4, npe) for b in range(4)]
+        todo = first + more[:2] + [("m", h) for h in range(8)] + more[2:]
         begun = first[:EARLY] if r else []
-
-        def place(b, h):
-            return R("mk", C * h, C * h + C) if b == "m" else R("win", PL * b + C * h, PL * b + C * h + C)
 
         def unpack_own(k):
             for _ in range(k):
@@ -372,21 +386,22 @@ def rank_program(g, core, T, topo):
                 mm(bank, side(b, h), own)
                 act(place(b, h), ps(bank, 0, C), ACT.Copy, None if b == "m" else 0.5)
 
-        def exchange(b):
-            dmas("Y", "sw%d" % b, [(ap(o), ap(i), [i], [o]) for (o, i) in
-                                   [(R("win", PL * b + C * npe, PL * b + 2048, 1, 64 * k, 64 * k + 64),
-                                     R("win", PL * b + C * (npe - 4), PL * b + 1024, 1, 64 - 64 * k, 128 - 64 * k))
-                                    for k in range(2)]])
-
         if r == 0:
             lists()
-        unpack_own(4 if r == 0 else N1)
-        for b in range(NS if r else 0):
-            exchange(b)
+            unpack_own(4)
+        else:
+            mm(1, UF1, own)
+            act(R("f2"), ps(1, 0, C))
+            unpack_own(6)
+            for b in range(NS):
+                exchange(b)
         tt(R("fd", 0, 128), R("dd", 0, 128), R("tri"), ALU.is_lt)
         ts(R("dd", 128, 256), ps(2, 0, 128), ps(3, 0, 1), ALU.subtract, -1.0, ALU.mult)
         ts(R("fo", 0, 128), ps(2, 0, 128), R("sc", 0, 1), ALU.is_gt)
         ts(R("fo", 128, 256), ps(0, 0, 128), ps(3, 0, 1), ALU.is_ge)
+        if r:
+            mm(2, UF2, own)
+            unpack_own(3)
         tt(R("fd", 128, 256), R("dd", 128, 256), R("tri"), ALU.is_lt)
         scan(R("rk", 0, 128), R("fd", 0, 128), R("fo", 0, 128), ALU.add, ALU.add)
         scan(R("rk", 128, 256), R("fd", 128, 256), R("fo", 128, 256), ALU.add, ALU.add)
@@ -395,8 +410,19 @@ def rank_program(g, core, T, topo):
         quant(R("ohq"), R("ohs"), R("oh"))
         mm(0, WHI, ("ohq", "ohs", 0, 128), True, False)
         mm(0, WLO, ("ohq", "ohs", 0, 128), False, True)
+        if r:
+            tt(R("ff", 0, 1024, 4), ps(2, 0, C), R("f2"), ALU.is_gt)
+            quant(R(lq, 64, 192), R(lsc, 64, 192), R("xn", 0, 512))
+            unpack_own(4)
+        else:
+            later_constants()
         turn(R("lt"), ps(0, 0, 128))
+        if r:
+            quant(R("ffq", 0, 128), R("ffs", 0, 128), R("ff", 0, 512))
         copy(R("lb"), R("lt", 0, 128, 32))
+        if r:
+            quant(R("ffq", 128, 256), R("ffs", 128, 256), R("ff", 512, 1024))
+            mm(3, WLOSS, ("ffq", "ffs", 0, C))
         pick_codes(R(bq), R(qn), R("lb"))
         copy(R(bs), (R(sn), R("lb")))
         rid, pid, _ = topo.addr(T.cores[(rank - d) % n])
@@ -408,18 +434,16 @@ def rank_program(g, core, T, topo):
         note("G", [], [R(lq, 0, H), R(lsc, 0, H)], "arr%d" % r, count["arr%d" % r])
         clock[("arr%d" % r, count["arr%d" % r])] = {}
         if r == 0:
-            later_constants()
             unpack_own(4)
-
-        mm(1, UF1, own)
-        mm(2, UF2, own)
-        unpack_own(6)
-        copy(R("f2"), ps(1, 0, C))
-        tt(R("ff", 0, 1024, 4), ps(2, 0, C), R("f2"), ALU.is_gt)
-        quant(R("ffq"), R("ffs"), R("ff"))
-        mm(3, WLOSS, ("ffq", "ffs", 0, C))
-        quant(R(lq, 64, 192), R(lsc, 64, 192), R("xn" if r else "xin", 0, 512))
-        if r == 0:
+            mm(1, UF1, own)
+            mm(2, UF2, own)
+            unpack_own(6)
+            copy(R("f2"), ps(1, 0, C))
+            quant(R(lq, 64, 192), R(lsc, 64, 192), R("xin", 0, 512))
+            tt(R("ff", 0, 1024, 4), ps(2, 0, C), R("f2"), ALU.is_gt)
+            turn(R("nt"), R("nf"))
+            quant(R("ffq"), R("ffs"), R("ff"))
+            mm(3, WLOSS, ("ffq", "ffs", 0, C))
             edges()
         unpack_own(3)
         ts(R("kl", 0, C), ps(3, 0, C), col(4), ALU.is_equal, col(5), ALU.mult)
@@ -452,6 +476,8 @@ def rank_program(g, core, T, topo):
         ts(R("wr"), R("wi"), MASK, ALU.bitwise_and)
         tt(R("preu"), (R("wr"), LU2), R("rows", 48, 64), ALU.add)
         copy(R("wx"), (R("wr"), LEX))
+        if r:
+            copy(R("ah", 0, 256), (R("win", 0, 2048), R("offa")))
         unpack_own(len(todo))
         if r == 1:
             quant(R("vq"), R("vs"), R("vin"))
@@ -492,21 +518,20 @@ def rank_program(g, core, T, topo):
         ts(R("uj"), R("ui"), MASK, ALU.bitwise_and)
         ts(R("cand"), R("ci"), MASK, ALU.bitwise_and)
         copy(R("offm"), R("uj"))
-        tt(R("dc"), R("cand", 32, 64), R("cand", 0, 32), ALU.subtract)
+        tt(R("d1", 0, 96, 3), R("cand", 32, 64), R("cand", 0, 32), ALU.subtract)
         for k in range(2):
             copy(R("gm", 128 * k, 128 * k + 128), (R("mk"), R("offm", 8 * k, 8 * k + 8)))
+        copy(R("d1", 1, 96, 3), R("cand", 0, 32))
         for k in range(2):
             turn(R("tm", 128 * k, 128 * k + 128), R("gm", 128 * k, 128 * k + 128))
         even, odd = R("tm", 0, 128, 4), R("tm", 128, 256, 4)
-        tt(R("e1"), odd, even, ALU.is_gt)
         tt(R("e2"), odd, even, ALU.max)
-        tt(R("e3"), R("e1"), R("dc"), ALU.mult)
-        tt(R("e4", 0, 16), R("e2", 16, 32), R("e2", 0, 16), ALU.is_le)
-        tt(R("e4", 16, 32), R("e2", 16, 32), R("e2", 0, 16), ALU.is_gt)
-        tt(R("e5"), R("e3"), R("cand", 0, 32), ALU.add)
-        tt(R("e6"), R("e5"), R("e4"), ALU.mult)
-        tt(R("e8"), R("e6", 0, 16), R("e6", 16, 32), ALU.add)
-        for b in range(4):
+        tt(R("d0", 1, 96, 3), odd, even, ALU.is_gt)
+        tt(R("d0", 2, 48, 3), R("e2", 16, 32), R("e2", 0, 16), ALU.is_le)
+        tt(R("d0", 50, 96, 3), R("e2", 16, 32), R("e2", 0, 16), ALU.is_gt)
+        scan(R("e5"), R("d0"), R("d1"), ALU.mult, ALU.add)
+        tt(R("e8"), R("e5", 2, 48, 3), R("e5", 50, 96, 3), ALU.add)
+        for b in range(1 if r else 0, 4):
             act(R("ah", 256 * b, 256 * b + 256), (R("win", PL * b, PL * b + 2048), R("offa")))
         for a in range(4):
             for k in range(4):
@@ -516,11 +541,12 @@ def rank_program(g, core, T, topo):
                 else:
                     copy(R("offb", 4 * a, 4 * a + 4, 1, 32 * k, 32 * k + 32), i)
         for k in range(2):
-            for b in range(4):
-                tt(R("z", 512 * k + b, 512 * k + 512, 4), (R("win", PL * b, PL * b + PL), R("offb", 8 * k, 8 * k + 8)),
-                   R("ah", 256 * b + 128 * k, 256 * b + 128 * k + 128), ALU.add)
+            for b in range(k, 4):
+                if k == 0 and b == 3:
+                    copy(R("offb", 12, 16), R("ob", 4, 8))
+                mean(k, b)
             if k == 0:
-                copy(R("offb", 12, 16), R("ob", 4, 8))
+                mean(1, 0)
             quant(R("zq", 128 * k, 128 * k + 128), R("zs", 128 * k, 128 * k + 128), R("z", 512 * k, 512 * k + 512))
             for b in range(4):
                 mm(4 * k + b, ("wq", "wsc", 128 * b, 128), ("zq", "zs", 128 * k, 128))
@@ -534,9 +560,10 @@ def rank_program(g, core, T, topo):
             turn(R("ot"), R("og"))
             dmas("Y", "oute", [(T.oe[c, :], ap(R("ot", 0, 16, 1, c, 128, 8)), [R("ot")], []) for c in range(4)])
         for k in range(2):
-            for b in range(4):
-                lo = 256 * b + 128 * k
-                tt(R("xn", 512 * k + b, 512 * k + 512, 4), R("rl", lo, lo + 128), R("af", lo, lo + 128), ALU.add)
+            for b in range(k, 4):
+                state(k, b)
+            if k == 0:
+                state(1, 0)
             scores(r + 1, k, "xn")
             if k == 0 and r < 2:
                 for (b, h) in first[:EARLY]:

@@ -5,10 +5,12 @@ STEP = [1, 2, 4]
 C, H = 256, 64
 FAR, MASK, PL = 4096, 4096 + 2047, 6144
 NPE = 5
-NV = [2, 3, 3]
 EARLY = 6
-NS = 2
-POS = [0, 1, 4, 2, 5, 3, 6, 7, 8, 9, 10]
+NS = 0
+WHOLE = [True, True, False]
+BULK = 4
+BITS = [(0, 15), (0, 112), (0, 7), (0, 120), (3, 1), (2, 3), (0, 14), (0, 31), (0, 1), (4, 1)]
+CYC, HOP, PECYC, LOCAL, REMOTE, PASSES = 0.83e-3, 0.2, 0.6e-3, 1.2, 1.2, 4
 
 
 def _s(n, d):
@@ -21,22 +23,24 @@ SCRATCH = {
     "wq": _s(512, MX), "wsc": _s(512, U8), "uq": _s(128, MX), "us": _s(128, U8), "vq": _s(128, MX), "vs": _s(128, U8),
     "u2q": _s(128, MX), "u2s": _s(128, U8), "uaq": _s(400, MX), "uas": _s(400, U8),
     "et": _s(1040, BF), "eq": _s(1024, MX), "es": _s(1024, U8),
-    "wt": _s(1536, BF), "cq": _s(384, MX), "cs": _s(384, U8),
-    "jm": _s(256, BF), "tri": _s(128, BF), "cn": _s(128, BF), "ch": _s(128, BF), "keep": _s(256, BF),
-    "fi": _s(352, F32), "ft": _s(352, F32), "rows": _s(64, F32), "col": _s(8, F32), "wa": _s(128, BF), "wb": _s(128, BF),
-    "l2": _s(8, U16), "lf": _s(64, F32), "ls": _s(64, U16), "lk": _s(16, U16),
+    "wt": _s(1540, BF), "cq": _s(512, MX), "cs": _s(512, U8),
+    "jm": _s(128, BF), "tri": _s(128, BF), "cn": _s(128, BF), "ch": _s(128, BF), "keep": _s(256, BF),
+    "pi": _s(16, I32), "pf": _s(16, F32),
+    "fi": _s(96, F32), "ft": _s(96, F32), "rows": _s(32, F32), "col": _s(16, F32), "wa": _s(128, BF), "wb": _s(128, BF),
+    "l2": _s(8, U16), "ls": _s(64, U16), "lk": _s(16, U16),
     "ia": _s(16, F32), "ni": _s(32, I32), "n0": _s(32, F32), "nf": _s(64, F32), "nt": _s(64, F32), "n16": _s(16, F32), "tmp": _s(48, F32),
     "sc": _s(8, F32),
     "dd": _s(256, BF), "fo": _s(256, BF), "fd": _s(256, BF), "rk": _s(256, BF), "oh": _s(512, BF), "ohq": _s(128, MX), "ohs": _s(128, U8),
-    "lt": _s(128, F32), "lb": _s(4, U16),
-    "f2": _s(256, F32), "ff": _s(1024, BF), "ffq": _s(256, MX), "ffs": _s(256, U8), "fb": _s(512, BF), "fbq": _s(128, MX), "fbs": _s(128, U8),
-    "kl": _s(320, BF), "ga": _s(256, BF), "ta": _s(256, BF), "sa": _s(256, BF), "gk": _s(256, BF), "tk": _s(256, BF), "sk": _s(256, BF),
+    "lt": _s(128, F32),
+    "f2": _s(512, F32), "ff": _s(1024, BF), "ffq": _s(256, MX), "ffs": _s(256, U8),
+    "kl": _s(320, BF), "kr": _s(256, BF), "ga": _s(256, BF), "ta": _s(256, BF), "sa": _s(256, BF), "gk": _s(256, BF), "tk": _s(256, BF), "sk": _s(256, BF),
     "oa": _s(16, F32), "offa": _s(16, U16), "pre": _s(16, F32), "preu": _s(16, F32), "wi": _s(16, I32), "wr": _s(16, I32), "wx": _s(64, F32),
     "ui": _s(16, I32), "uj": _s(16, I32), "offm": _s(16, U16), "sj": _s(32, I32), "ci": _s(64, I32),
     "cand": _s(64, I32), "gm": _s(256, F32), "tm": _s(256, F32),
-    "e2": _s(32, F32), "e5": _s(96, F32), "d0": _s(96, F32), "d1": _s(96, F32), "e8": _s(16, F32),
-    "offb": _s(16, U16), "ob": _s(8, F32),
-    "win": _s(4 * PL, BF), "mk": _s(PL, F32),
+    "e2": _s(32, F32), "fl": _s(32, F32), "dc": _s(64, F32), "e5": _s(128, F32), "d0": _s(128, F32), "d1": _s(128, F32),
+    "offb": _s(16, U16), "ob": _s(16, F32),
+    "win": ("sbuf", [128, 4, PL], BF), "mk": _s(PL, F32),
+    "bq": _s(320, MX), "bs": _s(320, U8),
     "ah": _s(1024, BF), "af": _s(1024, BF), "z": _s(1024, BF), "zq": _s(256, MX), "zs": _s(256, U8), "rl": _s(1024, F32), "xn": _s(1024, BF),
     "og": _s(32, F32), "ot": _s(32, F32), "yb": _s(256, F32),
 }
@@ -44,20 +48,28 @@ for _r in range(4):
     SCRATCH["q%d" % _r] = _s(256, MX)
     SCRATCH["s%d" % _r] = _s(256, U8)
 for _r in range(3):
-    SCRATCH["bq%d" % _r] = _s(64, MX)
-    SCRATCH["bs%d" % _r] = _s(64, U8)
-    SCRATCH["lq%d" % _r] = _s(192, MX)
-    SCRATCH["lsc%d" % _r] = _s(192, U8)
+    SCRATCH["lq%d" % _r] = _s(256, MX)
+    SCRATCH["lsc%d" % _r] = _s(256, U8)
+    SCRATCH["lb%d" % _r] = _s(4, U16)
+    SCRATCH["ll%d" % _r] = _s(4, U16)
+SIZE = {F32: 4, BF: 2, I32: 4, U16: 2, MX: 4, U8: 1}
 
-SEMAPHORES = ["V", "S", "P", "G", "dx", "du", "dw", "dv", "dn", "sw0", "sw1", "sw2", "sw3", "arr0", "arr1", "arr2", "sent", "out", "outa", "oute"]
+SEMAPHORES = (["V", "S", "P", "G", "dx0", "dx1", "du", "dw", "dv", "dn", "sent", "out", "outa", "outy", "oute"]
+              + ["sw%d%d" % (r, b) for r in range(3) for b in range(4)]
+              + ["%s%d" % (a, r) for r in range(3) for a in ("arra", "arrb", "arrl")])
 
 
 def width(name):
-    return SCRATCH[name][1][1]
+    shape = SCRATCH[name][1]
+    return shape[1] * (shape[2] if len(shape) == 3 else 1)
 
 
 def R(name, c0=0, c1=None, step=1, p0=0, p1=128, pstep=1):
     return (name, c0, width(name) if c1 is None else c1, step, p0, p1, pstep)
+
+
+def size(r):
+    return len(range(r[1], r[2], r[3]))
 
 
 def meets(a, b):
@@ -70,18 +82,165 @@ def meets(a, b):
     return bool(set(range(a[1], a[2], a[3])) & set(range(b[1], b[2], b[3])))
 
 
+def link(calls):
+    log = {}
+    for i, c in enumerate(calls):
+        c["pred"] = dict(c["after"])
+        for regs, w in ((c["reads"], False), (c["writes"], True)):
+            for r in regs:
+                for (o, ow, j) in log.get(r[0] if r[0] != "ps" else r[1] // 512, []):
+                    other = list(calls[j]["ways"])
+                    if j != i and (((w or ow) and meets(r, o)) or (r[0] == "ps" and (other != list(c["ways"]) or len(other) > 1))):
+                        c["pred"][j] = 0.0 if other == ["P"] == list(c["ways"]) else HOP
+        for regs, w in ((c["reads"], False), (c["writes"], True)):
+            for r in regs:
+                old = log.setdefault(r[0] if r[0] != "ps" else r[1] // 512, [])
+                if w:
+                    old[:] = [e for e in old if e[0] != r]
+                old.append((r, w, i))
+
+
+def arrange(calls):
+    link(calls)
+    n = len(calls)
+    span = [max(c["ways"].values()) + c["lat"] for c in calls]
+    users = {}
+    for i, c in enumerate(calls):
+        c["bank"] = sorted({r[1] // 512 for r in c["reads"] + c["writes"] if r[0] == "ps"})
+        for v in c["bank"]:
+            users.setdefault(v, []).append(i)
+    succ = [[] for _ in calls]
+    for i, c in enumerate(calls):
+        for j, d in c["pred"].items():
+            succ[j].append((i, d))
+    best, behind, chain = None, {}, None
+    for _ in range(PASSES):
+        new, line = [0.0] * n, {}
+        for i in reversed(range(n)):
+            new[i] = span[i] + max([0.0] + [d + new[k] for k, d in succ[i]])
+            if i in behind:
+                new[i] = max(new[i], calls[i]["ways"][way[i]] + chain[behind[i]])
+            if calls[i]["line"]:
+                new[i] = line[calls[i]["line"]] = max(new[i], span[i] + line.get(calls[i]["line"], 0.0))
+        chain = new if chain is None else [(a + b) / 2 for a, b in zip(chain, new)]
+        start, way, end = {}, {}, {}
+        free = {q: 0.0 for q in "VSPGYA"}
+        waiting = [len(c["pred"]) for c in calls]
+        ready = {i: 0.0 for i in range(n) if not waiting[i]}
+        todo = {q: [i for i in range(n) if q in calls[i]["ways"]] for q in free}
+        banks, held, left, last = {b: 0.0 for b in range(8)}, {}, {v: len(u) for v, u in users.items()}, {}
+        bulk, place, seq, engines = set(), {}, [], 0.0
+
+        def opens(i):
+            return [v for v in calls[i]["bank"] if v not in place]
+
+        def when(i):
+            if opens(i):
+                if not banks or (calls[i]["bulk"] and len(bulk) >= BULK):
+                    return None
+                return max(ready[i], min(banks.values()))
+            return ready[i]
+
+        def guess(i, depth, memo):
+            if i in ready:
+                return ready[i]
+            if i not in memo:
+                memo[i] = 1e9
+                if depth:
+                    memo[i] = max(end[j] + d if j in end else
+                                  max(guess(j, depth - 1, memo), min(free[q] for q in calls[j]["ways"])) + span[j] + d
+                                  for j, d in calls[i]["pred"].items())
+            return memo[i]
+
+        while len(seq) < n:
+            turn_ = []
+            for q in free:
+                ts_ = [when(i) for i in ready if q in calls[i]["ways"]]
+                ts_ = [t for t in ts_ if t is not None]
+                if ts_:
+                    turn_.append((max(free[q], min(ts_)), q))
+            t, q = min(turn_)
+            now = sorted((i for i in ready if q in calls[i]["ways"] and when(i) is not None and when(i) <= t + 1e-9), key=lambda i: -chain[i])
+            soon = [i for i in todo[q][:80] if len(calls[i]["ways"]) == 1 and i not in now]
+            memo, pick, hold = {}, None, None
+            for i in now[:6]:
+                dur = calls[i]["ways"][q]
+                late = None
+                for h in soon:
+                    if chain[h] > chain[i]:
+                        e = max(guess(h, 4, memo), t)
+                        if e < t + dur and max(e + chain[h], e + calls[h]["ways"][q] + chain[i]) < max(t + dur + chain[h], t + chain[i]) - 0.06:
+                            late = e if late is None else min(late, e)
+                if late is None:
+                    pick = i
+                    break
+                hold = late if hold is None else min(hold, late)
+            if pick is None:
+                free[q] = max(hold, t + 0.02)
+                continue
+            i = pick
+            for v in opens(i):
+                place[v] = min(banks, key=lambda b: (banks[b], b))
+                del banks[place[v]]
+                if calls[i]["bulk"]:
+                    bulk.add(v)
+            start[i], way[i] = t, q
+            end[i] = t + calls[i]["ways"][q] + calls[i]["lat"]
+            if calls[i]["busy"]:
+                end[i] = engines = max(end[i] - calls[i]["busy"], engines) + calls[i]["busy"]
+            if q != "A":
+                free[q] = t + calls[i]["ways"][q]
+            del ready[i]
+            for k in calls[i]["ways"]:
+                todo[k].remove(i)
+            seq.append(i)
+            for v in calls[i]["bank"]:
+                left[v] -= 1
+                last[v] = max(last.get(v, 0.0), end[i])
+                if not left[v]:
+                    banks[place[v]] = last[v] + HOP
+                    bulk.discard(v)
+            for k, d in succ[i]:
+                waiting[k] -= 1
+                if not waiting[k]:
+                    ready[k] = max(end[j] + dj for j, dj in calls[k]["pred"].items())
+        if best is None or max(end.values()) < best[0]:
+            best = (max(end.values()), [(i, way[i]) for i in seq], place)
+        behind, prev = {}, {}
+        for i in seq:
+            q = way[i]
+            if q in prev and q != "A" and start[i] < start[prev[q]] + calls[prev[q]]["ways"][q] + 0.05:
+                behind[prev[q]] = i
+            prev[q] = i
+    return best[1], best[2]
+
+
+ARRANGED = []
+
+
 def rank_program(g, core, T, topo):
     rank = T.rank_of(core)
     if rank is None:
         return
     n = len(T.cores)
     Q = {"V": g.vector, "S": g.scalar, "P": g.tensor, "G": g, "Y": g.sync}
+    calls, place = [], {}
     count = {k: 0 for k in SEMAPHORES}
     known = {k: {} for k in Q}
     clock = {}
     log = {}
 
+    def real(r):
+        if r[0] != "ps":
+            return r
+        shift = 512 * (place[r[1] // 512] - r[1] // 512)
+        return (r[0], r[1] + shift, r[2] + shift) + r[3:]
+
     def ap(r):
+        r = real(r)
+        if len(SCRATCH[r[0]][1]) == 3:
+            w = SCRATCH[r[0]][1][2]
+            return T[r[0]][r[4]:r[5], r[1] // w, r[1] % w:(r[2] - 1) % w + 1]
         if r[6] != 1:
             return T[r[0]][r[4]:r[5]:r[6], r[1]:r[2]]
         if r[3] != 1:
@@ -100,7 +259,7 @@ def rank_program(g, core, T, topo):
     def order(q, reads, writes):
         need = {}
         for regs, w in ((reads, False), (writes, True)):
-            for r in regs:
+            for r in map(real, regs):
                 for (o, ow, oq, sem, val) in log.get(r[0], []):
                     if oq == "P" and q == "P":
                         continue
@@ -115,93 +274,146 @@ def rank_program(g, core, T, topo):
     def note(q, reads, writes, sem, val):
         clock[(sem, val)] = dict(known[q])
         for regs, w in ((reads, False), (writes, True)):
-            for r in regs:
+            for r in map(real, regs):
                 old = log.setdefault(r[0], [])
                 if w:
                     old[:] = [e for e in old if e[0] != r]
                 old.append((r, w, q, sem, val))
 
-    def op(q, fn, reads, writes):
-        order(q, reads, writes)
-        fn().then_inc(T.sem[q], 1)
-        count[q] += 1
-        note(q, reads, writes, q, count[q])
+    line = [None]
 
-    def dmas(q, sem, items):
-        for (o, i, rd, wr) in items:
-            order(q, rd, wr)
-            Q[q].dma_start(o, i).then_inc(T.sem[sem], 16)
-            count[sem] += 16
-        for (o, i, rd, wr) in items:
-            note(q, rd, wr, sem, count[sem])
+    def record(ways, issue, reads, writes, lat=0.0, busy=0.0, after=None, bulk=False):
+        calls.append(dict(ways=ways, issue=issue, reads=reads, writes=writes, lat=lat + busy, busy=busy, after=after or {}, bulk=bulk,
+                          line=line[0] and (line[0], list(ways)[0])))
+        return len(calls) - 1
+
+    def op(forms, reads, writes, bulk=False):
+        def issue(q):
+            order(q, reads, writes)
+            forms[q][1]().then_inc(T.sem[q], 1)
+            count[q] += 1
+            note(q, reads, writes, q, count[q])
+        record({q: f[0] for q, f in forms.items()}, issue, reads, writes, bulk=bulk)
+
+    def dmas(q, sem, items, nbytes):
+        def issue(q):
+            for (o, i, rd, wr) in items:
+                order(q, rd, wr)
+                Q[q].dma_start(o, i).then_inc(T.sem[sem], 16)
+                count[sem] += 16
+            for (o, i, rd, wr) in items:
+                note(q, rd, wr, sem, count[sem])
+        record({q: 0.05 * len(items)}, issue, [r for i in items for r in i[2]], [r for i in items for r in i[3]], LOCAL, 0.05 + nbytes / 250e3)
+
+    def regs(a):
+        return [a[0], a[1]] if len(a) == 2 else [a]
 
     def src(a):
-        if len(a) == 2:
-            return ap(a[0]).indirect(ap(a[1])), [a[0], a[1]]
-        return ap(a), [a]
+        return ap(a[0]).indirect(ap(a[1])) if len(a) == 2 else ap(a)
+
+    def plain(o, *ins, twice=False, scalar=False):
+        if len(ins[0]) == 2:
+            return (0.065 if scalar else 0.05) + 1.5 * CYC * size(o)
+        narrow = not scalar and all(SIZE[SCRATCH[r[0]][2]] == 2 for r in (o,) + ins)
+        return CYC * max(64, size(o) * (0.5 if narrow else 1) * (2 if twice else 1))
+
+    def val(s):
+        return ap(s) if isinstance(s, tuple) else s
+
+    def v_copy(o, a):
+        return plain(o, a), lambda: g.vector.tensor_copy(ap(o), src(a))
+
+    def v_ts(o, a, s1, op0, s2=None, op1=None):
+        if op1 is None:
+            return plain(o, a), lambda: g.vector.tensor_scalar(ap(o), src(a), val(s1), None, op0)
+        return plain(o, a), lambda: g.vector.tensor_scalar(ap(o), src(a), val(s1), val(s2), op0, op1)
+
+    def s_act(o, a, func, scale=None, bias=None):
+        kw = {k: s for k, s in (("scale", scale), ("bias", bias)) if s is not None}
+        return plain(o, a, scalar=True), lambda: g.scalar.activation(ap(o), src(a), func, **{k: val(s) for k, s in kw.items()})
+
+    def cols(*s):
+        return [c for c in s if isinstance(c, tuple)]
 
     def copy(o, a):
-        v, rd = src(a)
-        op("V", lambda: g.vector.tensor_copy(ap(o), v), rd, [o])
-
-    def tt(o, a, b, alu):
-        v, rd = src(a)
-        op("V", lambda: g.vector.tensor_tensor(ap(o), v, ap(b), alu), rd + [b], [o])
+        op({"V": v_copy(o, a)}, regs(a), [o])
 
     def ts(o, a, s1, op0, s2=None, op1=None):
-        v, rd = src(a)
-        rd = rd + [s for s in (s1, s2) if isinstance(s, tuple)]
-        a1 = ap(s1) if isinstance(s1, tuple) else s1
-        a2 = ap(s2) if isinstance(s2, tuple) else s2
-        if op1 is None:
-            op("V", lambda: g.vector.tensor_scalar(ap(o), v, a1, None, op0), rd, [o])
-        else:
-            op("V", lambda: g.vector.tensor_scalar(ap(o), v, a1, a2, op0, op1), rd, [o])
-
-    def fill(o, c):
-        op("V", lambda: g.vector.memset(ap(o), c), [], [o])
-
-    def turn(o, a):
-        op("V", lambda: g.vector.transpose(ap(o), ap(a)), [a], [o])
-
-    def scan(o, a, b, op0, op1):
-        op("V", lambda: g.vector.tensor_tensor_scan(ap(o), ap(a), ap(b), 0.0, op0, op1), [a, b], [o])
-
-    def quant(oq, osc, a):
-        op("V", lambda: g.vector.quantize_mx(ap(oq), ap(osc), ap(a)), [a], [oq, osc])
+        op({"V": v_ts(o, a, s1, op0, s2, op1)}, regs(a) + cols(s1, s2), [o])
 
     def act(o, a, func=ACT.Copy, scale=None, bias=None):
-        v, rd = src(a)
-        kw = {}
-        if scale is not None:
-            kw["scale"] = scale
-        if bias is not None:
-            kw["bias"] = ap(bias) if isinstance(bias, tuple) else bias
-            rd = rd + ([bias] if isinstance(bias, tuple) else [])
-        op("S", lambda: g.scalar.activation(ap(o), v, func, **kw), rd, [o])
+        op({"S": s_act(o, a, func, scale, bias)}, regs(a) + cols(scale, bias), [o])
 
     def lin(o, a, scale=None, bias=None):
-        act(o, a, ACT.Identity, scale, bias)
+        op({"S": s_act(o, a, ACT.Identity, scale, bias), "V": v_ts(o, a, scale or 1.0, ALU.mult, bias or 0.0, ALU.add)},
+           [a] + cols(scale, bias), [o])
+
+    def move(o, a, scale=None):
+        op({"S": s_act(o, a, ACT.Copy, scale), "V": v_copy(o, a) if scale is None else v_ts(o, a, scale, ALU.mult)}, regs(a), [o])
+
+    def tt(o, a, b, alu):
+        op({"V": (plain(o, a, b, twice=a[0] != "ps"), lambda: g.vector.tensor_tensor(ap(o), src(a), ap(b), alu))}, regs(a) + [b], [o])
+
+    def fill(o, c):
+        op({"V": (plain(o, o), lambda: g.vector.memset(ap(o), c))}, [], [o])
+
+    def turn(o, a):
+        op({"V": (plain(o, a), lambda: g.vector.transpose(ap(o), ap(a)))}, [a], [o])
+
+    def scan(o, a, b, op0, op1):
+        op({"V": (plain(o, a, b), lambda: g.vector.tensor_tensor_scan(ap(o), ap(a), ap(b), 0.0, op0, op1))}, [a, b], [o])
+
+    def quant(oq, osc, a):
+        op({"V": (0.012 + 0.22e-3 * size(a), lambda: g.vector.quantize_mx(ap(oq), ap(osc), ap(a)))}, [a], [oq, osc])
 
     def pick_codes(o, w, off):
-        op("V", lambda: g.vector.tensor_copy(ap(o).bitcast(dt.uint32), ap(w).bitcast(dt.uint32).indirect(ap(off))), [w, off], [o])
+        op({"V": (plain(o, (w, off)), lambda: g.vector.tensor_copy(ap(o).bitcast(dt.uint32), ap(w).bitcast(dt.uint32).indirect(ap(off))))},
+           [w, off], [o])
 
-    def mm(bank, w, x, start=True, stop=True):
+    results = [0]
+
+    def mm(w, x, into=None, stop=True, bulk=False):
+        if into is None:
+            results[0] += 1
+        v = results[0] if into is None else into
         rs = [R(w[0], w[2], w[2] + w[3]), R(w[1], w[2], w[2] + w[3]), R(x[0], x[2], x[2] + x[3]), R(x[1], x[2], x[2] + x[3])]
-        o = R("ps", 512 * bank, 512 * bank + x[3])
-        op("P", lambda: g.tensor.matmul_mx(ap(o), ap(rs[0]), ap(rs[1]), ap(rs[2]), ap(rs[3]), start, stop), rs, [o])
+        o = ps(v, 0, x[3])
+        op({"P": (PECYC * (x[3] + 16), lambda: g.tensor.matmul_mx(ap(o), ap(rs[0]), ap(rs[1]), ap(rs[2]), ap(rs[3]), into is None, stop))},
+           rs, [o], bulk)
+        return v
 
-    def ps(bank, c0, c1):
-        return R("ps", 512 * bank + c0, 512 * bank + c1)
+    def ps(v, c0, c1):
+        return R("ps", 512 * v + c0, 512 * v + c1)
 
     def iota(o, pattern, base, cm):
-        op("G", lambda: g.iota(ap(o), pattern, base, cm, allow_small_or_imprecise_dtypes=True), [], [o])
+        op({"G": (0.13 + 2 * CYC * size(o), lambda: g.iota(ap(o), pattern, base, cm, allow_small_or_imprecise_dtypes=True))}, [], [o])
 
-    def F(f):
-        return R("ft", 32 * POS[f], 32 * POS[f] + 1)
+    def engines(k):
+        each = [set(topo.engines(T.cores[k], T.cores[(k - d) % n])) for d in STEP]
+        return sorted(each[0] & each[1] & each[2])
 
-    def field(f, pattern, base=0, cm=0, c0=0, c1=32):
-        iota(R("fi", 32 * POS[f] + c0, 32 * POS[f] + c1), pattern, base, cm)
+    def send(d, sem, pieces, token=None):
+        rid, pid, _ = topo.addr(T.cores[(rank - d) % n])
+        sent = []
+        for a, o in pieces:
+            def issue(q, a=a, o=o):
+                order("G", [a], [])
+                cast = [ap(k).bitcast(dt.uint8) if SCRATCH[k[0]][2] == MX else ap(k) for k in (o, a)]
+                g.remote_dma(cast[0], cast[1], T.sem[sem], T.sem.sent, pid, rid, sum(1 << e for e in engines(rank)))
+                count["sent"] += len(engines(rank))
+                if token:
+                    note("G", [], [token], "sent", count["sent"])
+            busy = 0.3 + size(a) * SIZE[SCRATCH[a[0]][2]] / 1e3
+            sent.append(record({"G": 0.3}, issue, [a], [token] if token and (a, o) == pieces[-1] else [], REMOTE, busy,
+                               {k: -c["lat"] for k, c in enumerate(calls) if "G" in c["ways"]}))
+
+        def arrive(q):
+            count[sem] = len(pieces) * len(engines((rank + d) % n))
+            note("G", [], [o for a, o in pieces], sem, count[sem])
+            clock[(sem, count[sem])] = {}
+        record({"A": 0.0}, arrive, [], [o for a, o in pieces], after={k: 0.0 for k in sent})
+
+    M, P112, P7, P120, M3, M2, P14, P31, P1, X = [R("pf", k, k + 1) for k in range(len(BITS))]
 
     def col(k):
         return R("col", k, k + 1)
@@ -210,374 +422,293 @@ def rank_program(g, core, T, topo):
         return R("et", 0, 4 * k, 4)
 
     U2, UF1, UF2 = ("u2q", "u2s", 0, 128), ("uaq", "uas", 0, 128), ("uaq", "uas", 128, 128)
-    WHI, WLO, WLOSS = ("cq", "cs", 0, 128), ("cq", "cs", 128, 128), ("cq", "cs", 256, 128)
-    LU, LKI, LU2, LU1, LNB, LEX, LOE, LA, LX7 = [R("ls", a, b) for a, b in
-                                                 ((0, 25), (26, 27), (28, 29), (30, 31), (32, 33), (34, 38), (38, 40), (40, 56), (56, 60))]
+    WHI, WLO, WLOSS = ("cq", "cs", 0, 128), ("cq", "cs", 128, 128), [("cq", "cs", 256, 128), ("cq", "cs", 384, 128)]
+    LU, LKI, LU2, LU1, LNB, LEX, LOE, LA, LX7, LF = [R("ls", a, b) for a, b in (
+        (0, 25), (26, 27), (28, 29), (30, 31), (32, 33), (34, 38), (38, 40), (40, 56), (56, 60), (60, 64))]
 
-    def scores(r, k, tile):
-        h = ("q%d" % r, "s%d" % r, 128 * k, 128)
-        quant(R(h[0], 128 * k, 128 * k + 128), R(h[1], 128 * k, 128 * k + 128), R(tile, 512 * k, 512 * k + 512))
-        if r == len(STEP):
-            return
-        mm(1 + 2 * k, h, U2)
-        mm(2 * k, U2, h)
-        if k == 0:
-            act(R("sc", 0, 1), ps(1, 0, 1))
-            lin(R("dd", 0, 128), ps(0, 0, 128), -1.0, R("sc", 0, 1))
-
-    def unit(b):
-        quant(R("eq", 256 * b, 256 * b + 240), R("es", 256 * b, 256 * b + 240), R("et", 3 - b, 963 - b))
-
-    dmas("Y", "dx", [(T.xin[:], T.x[:], [], [R("xin")])])
-    dmas("S", "du", [(T.uin[:], T.u[:], [], [R("uin")])])
-    iota(R("jm"), [[0, 2], [1, 128]], 0, -1)
-    field(0, [[0, 2], [1, 16]])
-    field(1, [[16, 2], [0, 16]], 0, 1)
-    field(3, [[0, 4], [1, 8]])
-    field(5, [[8, 4], [0, 8]], 0, 1)
-    iota(R("ch"), [[0, 16], [8, 8]], 0, 0)
-    iota(R("cn"), [[16, 4], [0, 2], [1, 16]], 0, 0)
-    field(2, [[0, 2], [16, 2], [0, 8]], 1)
-    field(4, [[0, 2], [1, 4], [0, 4]])
-    field(6, [[0, 8], [16, 4]], 7, 2)
-    field(7, [[0, 2], [2, 8], [0, 2]])
-    field(8, [[1, 32]])
+    dmas("S", "du", [(T.uin[:], T.u[:], [], [R("uin")])], 1 << 17)
     for k in range(2):
-        field(9, [[1, 2], [2, 2], [8, 4]], 0, 0, 16 * k, 16 * k + 16)
-        field(10, [[1, 2], [4, 4], [8, 2]], 0, 0, 16 * k, 16 * k + 16)
-    iota(R("rows", 0, 8), [[0, 2], [32, 4]], 0, 0)
-    iota(R("rows", 8, 12), [[4, 4]], 0, 0)
-    iota(R("rows", 16, 32), [[32, 8], [0, 2]], 0, 0)
-    iota(R("rows", 32, 48), [[16, 16]], 0, 0)
-    iota(R("rows", 48, 64), [[0, 8], [256, 2]], 0, 0)
+        dmas("Y", "dx%d" % k, [(T.xin[:, 512 * k:512 * k + 512], T.x[:, 512 * k:512 * k + 512], [], [R("xin", 512 * k, 512 * k + 512)])],
+             1 << 17)
+    iota(R("pi", 15, 16), [[0, 1]], 0, 1)
+    iota(R("jm"), [[1, 128]], 0, -1)
+    iota(R("rows", 0, 16), [[16, 16]], 0, 0)
+    iota(R("cn"), [[16, 4], [0, 2], [1, 16]], 0, 0)
+    iota(R("ch"), [[0, 16], [8, 8]], 0, 0)
+    iota(R("fi", 0, 32), [[0, 8], [16, 4]], 7, 2)
+    for k in range(2):
+        iota(R("fi", 32 + 16 * k, 48 + 16 * k), [[1, 2], [2, 2], [8, 4]], 0, 0)
+        iota(R("fi", 64 + 16 * k, 80 + 16 * k), [[1, 2], [4, 4], [8, 2]], 0, 0)
+    turn(R("ft"), R("fi"))
+    for k, (shift, mask) in enumerate(BITS):
+        ts(R("pi", k, k + 1), R("pi", 15, 16), shift, ALU.arith_shift_right, mask, ALU.bitwise_and)
+    copy(R("pf", 0, 5), R("pi", 0, 5))
+    copy(R("pf", 5, 10), R("pi", 5, 10))
+    fill(R("rows", 16, 32, 2), 0.0)
+    fill(R("rows", 17, 32, 2), 256.0)
     fill(R("ni"), 0)
     fill(R("et"), 0.0)
     fill(R("l2"), 2)
     dmas("Y", "dn", [(ap(R("ni", 0, 16, 1, c, 128, 8)), T.nb[c, :], [], [R("ni")]) for c in range(4)]
-         + [(ap(R("ni", 16, 32, 1, c, 128, 8)), T.e[c, :], [], [R("ni")]) for c in range(4)])
-    dmas("Y", "dw", [(T.wq[:].bitcast(dt.uint8), T.wc[:], [], [R("wq")]), (T.wsc[:], T.ws[:], [], [R("wsc")])])
-    dmas("Y", "dv", [(T.vin[:], T.v[:], [], [R("vin")])])
-    for k in range(1, 4):
-        lin(R("ff", k, 1024, 4), zeros(256))
+         + [(ap(R("ni", 16, 32, 1, c, 128, 8)), T.e[c, :], [], [R("ni")]) for c in range(4)], 1 << 14)
+    for k in range(2):
+        fill(R("ff", 512 * k, 512 * k + 512), 0.0)
+        ts(R("et", 3 + 512 * k, 512 + 512 * k, 4), R("jm"), 0.0, ALU.is_equal)
     fill(R("oh"), 0.0)
-    ts(R("et", 3, 1024, 4), R("jm"), 0.0, ALU.is_equal)
-    ts(R("tri"), R("jm", 0, 128), 0.0, ALU.is_lt, 2.0 ** -100, ALU.mult)
-    lin(R("keep"), zeros(256), None, 1.0)
-    unit(0)
-    unit(1)
-    turn(R("ft", 0, 128), R("fi", 0, 128))
-    lin(col(2), F(3), 8.0)
-    lin(col(6), F(1), None, 128.0)
-    lin(R("wt", 0, 512, 2), zeros(256), None, F(1))
+    ts(R("tri"), R("jm"), 0.0, ALU.is_lt, 2.0 ** -100, ALU.mult)
+    fill(R("keep"), 1.0)
+    fill(R("keep", 0, 256, 16), 0.0)
+    for b in range(4):
+        quant(R("eq", 256 * b, 256 * b + 240), R("es", 256 * b, 256 * b + 240), R("et", 3 - b, 963 - b))
+    lin(col(2), P7, 8.0)
+    lin(col(6), P112, None, 128.0)
+    lin(R("wt", 0, 512, 2), zeros(256), None, P112)
     lin(R("wt", 1, 512, 2), zeros(256), None, col(6))
-    lin(R("wt", 512, 1024, 2), zeros(256), None, F(0))
-    lin(R("wt", 513, 1024, 2), zeros(256), None, F(0))
-    unit(2)
-    unit(3)
-    lin(R("keep", 0, 256, 16), zeros(16))
-    fill(R("wt", 1024, 1536), 0.0)
-    fill(R("fb"), 0.0)
+    lin(R("wt", 512, 1024, 2), zeros(256), None, M)
+    lin(R("wt", 513, 1024, 2), zeros(256), None, M)
+    fill(R("wt", 1024, 1540), 0.0)
     fill(R("sj"), 0)
-    lin(R("d0"), zeros(96))
-    lin(R("d1"), zeros(96))
-    tt(col(3), col(2), F(5), ALU.is_gt)
+    fill(R("d0"), 1.0)
+    fill(R("d0", 0, 128, 8), 0.0)
+    fill(R("d1"), 0.0)
+    fill(R("dc"), 0.0)
+    tt(col(3), col(2), P120, ALU.is_gt)
     quant(R("uq"), R("us"), R("uin"))
-    ts(R("wa"), R("ch"), F(5), ALU.is_equal, col(3), ALU.mult)
+    ts(R("wa"), R("ch"), P120, ALU.is_equal, col(3), ALU.mult)
     ts(R("wb"), R("ch"), col(2), ALU.is_equal, col(3), ALU.mult)
     pick_codes(R("u2q"), R("uq"), R("l2"))
-    act(R("u2s"), (R("us"), R("l2")))
-    tt(R("wt", 1024, 1536, 4), R("wa"), R("wb"), ALU.subtract)
-    scores(0, 0, "xin")
-    scores(0, 1, "xin")
-    quant(R("cq"), R("cs"), R("wt"))
-    turn(R("ft", 128, 352), R("fi", 128, 352))
+    move(R("u2s"), (R("us"), R("l2")))
+    tt(R("wt", 1026, 1538, 4), R("wa"), R("wb"), ALU.subtract)
+    quant(R("cq", 0, 256), R("cs", 0, 256), R("wt", 0, 1024))
+    quant(R("cq", 256, 384), R("cs", 256, 384), R("wt", 1026, 1538))
+    quant(R("cq", 384, 512), R("cs", 384, 512), R("wt", 1024, 1536))
+    quant(R("bq", 192, 320), R("bs", 192, 320), R("xin", 0, 512))
+    def listed(lo, hi, a, scale, bias, step=1):
+        ts(R("ls", lo, hi, step), a, scale, ALU.mult, bias, ALU.add)
 
-    def lists():
-        lin(R("lf"), zeros(64))
-        lin(col(0), F(3), 16.0, 1.0)
-        lin(col(1), F(7), 8.0)
-        lin(R("lf", 0, 8), R("rows", 0, 8), None, F(2))
-        lin(R("lf", 8, 16), zeros(8), None, col(0))
-        lin(R("lf", 16, 25), zeros(9), None, col(1))
-        lin(col(7), F(8), 0.0625, F(7))
-        lin(R("lf", 26, 27), F(6))
-        lin(R("lf", 32, 33), F(9))
-        lin(R("lf", 34, 38), R("rows", 8, 12), None, F(4))
-        lin(R("lf", 28, 29), F(0), -0.0625, col(7))
-        lin(R("lf", 38, 39), F(10))
-        lin(R("lf", 39, 40), F(10), None, 2.0)
-        lin(R("lf", 40, 56), R("rows", 16, 32), None, F(8))
-        lin(R("lf", 30, 31), R("lf", 28, 29), 16.0, 7.0)
-        lin(R("lf", 56, 60), R("lf", 34, 38), 16.0, 7.0)
-        lin(col(4), F(3), -1.0)
-        lin(col(5), F(3), 256.0)
-        lin(R("ia"), R("rows", 32, 48), None, F(0))
-
-    def later_constants():
-        copy(R("ls"), R("lf"))
-        copy(R("n0"), R("ni"))
-        pick_codes(R("uaq"), R("uq"), LU)
-        act(R("uas"), (R("us"), LU))
-        for k in range(4):
-            act(R("nf", 16 * k, 16 * k + 16), R("n0", 16 * (k // 2), 16 * (k // 2) + 16))
-
-    def edges():
-        copy(R("n16"), (R("nt", 0, 32), LNB))
-        ts(R("tmp", 0, 16), (R("nt", 32, 64), LNB), 256.0, ALU.mult)
-        ts(R("tmp", 16, 32), R("n16"), float(C), ALU.is_ge, float(FAR - C), ALU.mult)
-        tt(R("tmp", 32, 48), R("tmp", 0, 16), R("n16"), ALU.add)
-        copy(R("lk"), (R("n16"), LU2))
-        tt(R("cand", 0, 64, 4), R("tmp", 32, 48), R("tmp", 16, 32), ALU.add)
-
-    def engines(k):
-        each = [set(topo.engines(T.cores[k], T.cores[(k - d) % n])) for d in STEP]
-        return sorted(each[0] & each[1] & each[2])
-
-    ring = [0]
-
-    def ring_bank():
-        ring[0] += 1
-        return 4 + (ring[0] - 1) % 4
+    fill(R("ls"), 0)
+    lin(col(0), P7, 16.0, 1.0)
+    lin(col(1), P14, 8.0)
+    lin(col(7), M3, 16.0, 1.0)
+    lin(col(11), X, None, P14)
+    lin(col(8), P1, 16.0, M2)
+    lin(col(12), M2, 16.0, 7.0)
+    for k in range(2):
+        listed(4 * k, 4 * k + 4, R("rows", 0, 4), 2.0, col(7))
+        listed(40 + k, 56, R("rows", 0, 8), 2.0, P31, 2)
+        listed(38 + k, 39 + k, R("ft", 64, 65), 1.0, 2.0 * k)
+    listed(8, 16, zeros(8), 1.0, col(0))
+    listed(16, 25, zeros(9), 1.0, col(1))
+    listed(26, 27, R("ft", 0, 1), 1.0, 0.0)
+    listed(28, 29, col(11), 1.0, 0.0)
+    listed(30, 31, col(11), 16.0, 7.0)
+    listed(32, 33, R("ft", 32, 33), 1.0, 0.0)
+    listed(34, 38, R("rows", 0, 4), 0.25, M2)
+    listed(56, 60, R("rows", 0, 4), 4.0, col(12))
+    listed(60, 64, R("rows", 0, 4), 0.25, col(8))
+    lin(col(4), P7, -1.0)
+    lin(col(5), P7, 256.0)
+    lin(col(9), P7, -256.0)
+    ts(col(10), col(4), 1.0, ALU.add, col(5), ALU.mult)
+    lin(R("ia"), R("rows", 0, 16), None, M)
+    copy(R("n0"), R("ni"))
+    for lo, hi in ((0, 16), (16, 25)):
+        pick_codes(R("uaq", 16 * lo, 16 * hi), R("uq"), R("ls", lo, hi))
+        move(R("uas", 16 * lo, 16 * hi), (R("us"), R("ls", lo, hi)))
+    for k in range(4):
+        move(R("nf", 16 * k, 16 * k + 16), R("n0", 16 * (k // 2), 16 * (k // 2) + 16))
+    turn(R("nt"), R("nf"))
+    copy(R("n16"), (R("nt", 0, 32), LNB))
+    ts(R("tmp", 0, 16), (R("nt", 32, 64), LNB), 256.0, ALU.mult)
+    ts(R("tmp", 16, 32), R("n16"), float(C), ALU.is_ge, float(FAR - C), ALU.mult)
+    tt(R("tmp", 32, 48), R("tmp", 0, 16), R("n16"), ALU.add)
+    copy(R("lk"), (R("n16"), LU2))
+    tt(R("cand", 0, 64, 4), R("tmp", 32, 48), R("tmp", 16, 32), ALU.add)
 
     def side(b, h):
         if b == "m":
             return ("uaq", "uas", 256 + 2 * h, 128)
         return ("eq", "es", 256 * b + 16 * h, 128)
 
-    def unpack_half(r, b, h, k):
-        bank = ring_bank()
-        lo = PL * b + C * h + 128 * k
-        mm(bank, side(b, h), ("q%d" % r, "s%d" % r, 128 * k, 128))
-        act(R("win", lo, lo + 128), ps(bank, 0, 128), ACT.Copy, 0.5)
+    def unpack(b, h, x, lo, k):
+        v = mm(side(b, h), x, bulk=True)
+        if b == "m":
+            move(R("mk", lo + C * h, lo + C * h + k), ps(v, 0, k))
+        else:
+            move(R("win", PL * b + lo + C * h, PL * b + lo + C * h + k), ps(v, 0, k), 0.5)
 
-    def exchange(b):
-        dmas("Y", "sw%d" % b, [(ap(o), ap(i), [i], [o]) for (o, i) in
-                               [(R("win", PL * b + C * NPE, PL * b + 2048, 1, 64 * k, 64 * k + 64),
-                                 R("win", PL * b + C * (NPE - 4), PL * b + 1024, 1, 64 - 64 * k, 128 - 64 * k))
-                                for k in range(2)]])
-
-    def place(b, h):
-        return R("mk", C * h, C * h + C) if b == "m" else R("win", PL * b + C * h, PL * b + C * h + C)
-
-    def mean(k, b):
-        tt(R("z", 512 * k + b, 512 * k + 512, 4), (R("win", PL * b, PL * b + PL), R("offb", 8 * k, 8 * k + 8)),
-           R("ah", 256 * b + 128 * k, 256 * b + 128 * k + 128), ALU.add)
-
-    def state(k, b):
-        lo = 256 * b + 128 * k
-        tt(R("xn", 512 * k + b, 512 * k + 512, 4), R("rl", lo, lo + 128), R("af", lo, lo + 128), ALU.add)
+    def frames(x, k, out):
+        many, two = size(out), size(out) // 128 or 1
+        a, b = mm(UF1, x), mm(UF2, x)
+        f2, ff = R("f2", C * k, C * k + many), R("ff", 512 * k, 512 * k + 4 * many // two, 4 // two)
+        move(f2, ps(a, 0, many))
+        tt(ff, ps(b, 0, many), f2, ALU.is_gt)
+        quant(R("ffq", 128 * k, 128 * k + 128), R("ffs", 128 * k, 128 * k + 128), R("ff", 512 * k, 512 * k + 512))
+        for j in range(two):
+            v = ps(mm(WLOSS[j], ("ffq", "ffs", 128 * k, 128)), 0, many // two)
+            o = R(out[0], out[1] + j, out[2], two)
+            op({"V": v_ts(o, v, col(4), ALU.is_equal, col(5), ALU.mult), "S": s_act(o, v, ACT.Relu, col(9), col(10))},
+               [v, col(4), col(5), col(9), col(10)], [o])
 
     first = [(b, h) for b in range(4) for h in (1, 2, 3)] + [(b, 0) for b in range(4)]
     more = [(b, h) for h in range(4, NPE) for b in range(4)]
 
     for r, d in enumerate(STEP):
-        qn, sn, bq, bs, lq, lsc = "q%d" % r, "s%d" % r, "bq%d" % r, "bs%d" % r, "lq%d" % r, "lsc%d" % r
-        own, came = (qn, sn, 0, C), (lq, lsc, 0, 128)
-        todo = first + more[:2] + [("m", h) for h in range(8)] + more[2:]
-        begun = first[:EARLY] if r else []
+        qn, sn, lq, lsc, lb, ll = [k + str(r) for k in ("q", "s", "lq", "lsc", "lb", "ll")]
+        own, gone = (qn, sn, 0, C), ("gone%d" % r, 0, 1, 1, 0, 128, 1)
+        came = ("bq", "bs", 128 - H * r, 128)
+        border = [R(k, 128 - H * r, 128 - H * r + H) for k in ("bq", "bs")]
 
-        def unpack_own(k):
-            for _ in range(k):
-                b, h = todo.pop(0)
-                if (b, h) in begun:
-                    unpack_half(r, b, h, 1)
-                    continue
-                bank = ring_bank()
-                mm(bank, side(b, h), own)
-                act(place(b, h), ps(bank, 0, C), ACT.Copy, None if b == "m" else 0.5)
-
-        if r == 0:
-            lists()
-            unpack_own(4)
-        else:
-            mm(1, UF1, own)
-            act(R("f2"), ps(1, 0, C))
-            unpack_own(6)
-            for b in range(NS):
-                exchange(b)
-        tt(R("fd", 0, 128), R("dd", 0, 128), R("tri"), ALU.is_lt)
-        ts(R("dd", 128, 256), ps(2, 0, 128), ps(3, 0, 1), ALU.subtract, -1.0, ALU.mult)
-        ts(R("fo", 0, 128), ps(2, 0, 128), R("sc", 0, 1), ALU.is_gt)
-        ts(R("fo", 128, 256), ps(0, 0, 128), ps(3, 0, 1), ALU.is_ge)
-        if r:
-            mm(2, UF2, own)
-            unpack_own(3)
-        tt(R("fd", 128, 256), R("dd", 128, 256), R("tri"), ALU.is_lt)
-        scan(R("rk", 0, 128), R("fd", 0, 128), R("fo", 0, 128), ALU.add, ALU.add)
-        scan(R("rk", 128, 256), R("fd", 128, 256), R("fo", 128, 256), ALU.add, ALU.add)
-        ts(R("oh", 0, 512, 4), R("cn"), R("rk", 127, 128), ALU.is_equal)
-        ts(R("oh", 1, 512, 4), R("cn"), R("rk", 255, 256), ALU.is_equal)
+        along, down = [], []
+        for k in range(2):
+            half = (qn, sn, 128 * k, 128)
+            hq, hs = R(qn, 128 * k, 128 * k + 128), R(sn, 128 * k, 128 * k + 128)
+            if r == 0:
+                quant(hq, hs, R("xin", 512 * k, 512 * k + 512))
+            if WHOLE[r]:
+                send(d, "arr%s%d" % ("ab"[k], r), [(hq, R(lq, 128 * k, 128 * k + 128))] + ([(R(sn), R(lsc))] if k else []))
+            down.append(ps(mm(half, U2), 0, 1))
+            along.append(ps(mm(U2, half), 0, 128))
+        act(R("sc", 0, 1), down[0])
+        lin(R("dd", 0, 128), along[0], -1.0, R("sc", 0, 1))
+        ts(R("dd", 128, 256), along[1], down[1], ALU.subtract, -1.0, ALU.mult)
+        ts(R("fo", 0, 128), along[1], R("sc", 0, 1), ALU.is_gt)
+        ts(R("fo", 128, 256), along[0], down[1], ALU.is_ge)
+        for k in range(2):
+            lo, hi = 128 * k, 128 * k + 128
+            tt(R("fd", lo, hi), R("dd", lo, hi), R("tri"), ALU.is_lt)
+            scan(R("rk", lo, hi), R("fd", lo, hi), R("fo", lo, hi), ALU.add, ALU.add)
+            ts(R("oh", k, 512, 4), R("cn"), R("rk", hi - 1, hi), ALU.is_equal)
         quant(R("ohq"), R("ohs"), R("oh"))
-        mm(0, WHI, ("ohq", "ohs", 0, 128), True, False)
-        mm(0, WLO, ("ohq", "ohs", 0, 128), False, True)
-        if r:
-            tt(R("ff", 0, 1024, 4), ps(2, 0, C), R("f2"), ALU.is_gt)
-            quant(R(lq, 64, 192), R(lsc, 64, 192), R("xn", 0, 512))
-            unpack_own(4)
+        v = mm(WHI, ("ohq", "ohs", 0, 128), stop=False)
+        mm(WLO, ("ohq", "ohs", 0, 128), into=v)
+        turn(R("lt"), ps(v, 0, 128))
+        copy(R(lb), R("lt", 0, 128, 32))
+        if WHOLE[r]:
+            send(d, "arrl%d" % r, [(R(lb), R(ll))], gone)
         else:
-            later_constants()
-        turn(R("lt"), ps(0, 0, 128))
-        if r:
-            quant(R("ffq", 0, 128), R("ffs", 0, 128), R("ff", 0, 512))
-        copy(R("lb"), R("lt", 0, 128, 32))
-        if r:
-            quant(R("ffq", 128, 256), R("ffs", 128, 256), R("ff", 512, 1024))
-            mm(3, WLOSS, ("ffq", "ffs", 0, C))
-        pick_codes(R(bq), R(qn), R("lb"))
-        copy(R(bs), (R(sn), R("lb")))
-        rid, pid, _ = topo.addr(T.cores[(rank - d) % n])
-        for (a, o, rg) in ((T[bq][:].bitcast(dt.uint8), T[lq][:, 0:H].bitcast(dt.uint8), R(bq)), (T[bs][:], T[lsc][:, 0:H], R(bs))):
-            order("G", [rg], [])
-            g.remote_dma(o, a, T.sem["arr%d" % r], T.sem.sent, pid, rid, sum(1 << e for e in engines(rank)))
-            count["sent"] += len(engines(rank))
-        count["arr%d" % r] = 2 * len(engines((rank + d) % n))
-        note("G", [], [R(lq, 0, H), R(lsc, 0, H)], "arr%d" % r, count["arr%d" % r])
-        clock[("arr%d" % r, count["arr%d" % r])] = {}
+            pick_codes(R(lq, 0, H), R(qn), R(lb))
+            move(R(lsc, 0, H), (R(sn), R(lb)))
+            send(d, "arrl%d" % r, [(R(lq, 0, H), border[0]), (R(lsc, 0, H), border[1])], gone)
+
+        todo = first + more + [("m", h) for h in range(8)]
+        for j, (b, h) in enumerate(todo):
+            if r and j < EARLY:
+                for k in range(2):
+                    unpack(b, h, (qn, sn, 128 * k, 128), 128 * k, 128)
+            else:
+                unpack(b, h, own, 0, C)
+        for b in range(4):
+            pairs = [(R("win", PL * b + C * NPE, PL * b + 2048, 1, 64 * k, 64 * k + 64),
+                      R("win", PL * b + C * (NPE - 4), PL * b + 1024, 1, 64 - 64 * k, 128 - 64 * k)) for k in range(2)]
+            dmas("Y", "sw%d%d" % (r, b), [(ap(o), ap(i), [i] + ([gone] if b >= NS else []), [o]) for (o, i) in pairs],
+                 (8 - NPE) << 16)
         if r == 0:
-            unpack_own(4)
-            mm(1, UF1, own)
-            mm(2, UF2, own)
-            unpack_own(6)
-            copy(R("f2"), ps(1, 0, C))
-            quant(R(lq, 64, 192), R(lsc, 64, 192), R("xin", 0, 512))
-            tt(R("ff", 0, 1024, 4), ps(2, 0, C), R("f2"), ALU.is_gt)
-            turn(R("nt"), R("nf"))
-            quant(R("ffq"), R("ffs"), R("ff"))
-            mm(3, WLOSS, ("ffq", "ffs", 0, C))
-            edges()
-        unpack_own(3)
-        ts(R("kl", 0, C), ps(3, 0, C), col(4), ALU.is_equal, col(5), ALU.mult)
-        mine = [todo.pop() for _ in range(NV[r])]
-        for k, (b, h) in enumerate(mine):
-            mm(k, side(b, h), own)
-        unpack_own(min(4, len(todo)))
-        wait("Y", "sent", count["sent"])
-        for b in range(NS if r else 0, 4):
-            exchange(b)
-
-        def take(k):
-            if k < len(mine):
-                b, h = mine[k]
-                if b == "m":
-                    copy(place(b, h), ps(k, 0, C))
-                else:
-                    ts(place(b, h), ps(k, 0, C), 0.5, ALU.mult)
-
-        copy(R("ga"), (R("kl", 0, C), LA))
-        take(0)
+            dmas("Y", "dw", [(T.wq[:].bitcast(dt.uint8), T.wc[:], [gone, R("win", 3 * PL + 2047, 3 * PL + 2048)], [R("wq")]),
+                             (T.wsc[:], T.ws[:], [], [R("wsc")])], 5 << 16)
+        if r == 1:
+            dmas("Y", "dv", [(T.vin[:], T.v[:], [R("win", 3 * PL + 2047, 3 * PL + 2048)], [R("vin")])], 1 << 17)
+            quant(R("vq"), R("vs"), R("vin"))
+        frames(own, 0, R("kl", 0, C))
+        move(R("ga"), (R("kl", 0, C), LA))
         turn(R("ta"), R("ga"))
-        take(1)
         scan(R("sa"), R("keep"), R("ta"), ALU.mult, ALU.add)
-        take(2)
         ts(R("pre"), (R("sa"), LKI), -1.0, ALU.mult, 2048.0, ALU.add)
         tt(R("oa"), R("sa", 7, 256, 16), R("ia"), ALU.add)
         tt(R("wi"), R("pre"), R("cand", 0, 64, 4), ALU.add)
         copy(R("offa"), R("oa"))
         ts(R("wr"), R("wi"), MASK, ALU.bitwise_and)
-        tt(R("preu"), (R("wr"), LU2), R("rows", 48, 64), ALU.add)
+        tt(R("preu"), (R("wr"), LU2), R("rows", 16, 32), ALU.add)
         copy(R("wx"), (R("wr"), LEX))
-        if r:
-            copy(R("ah", 0, 256), (R("win", 0, 2048), R("offa")))
-        unpack_own(len(todo))
-        if r == 1:
-            quant(R("vq"), R("vs"), R("vin"))
+        for b in range(4):
+            for k in range(2):
+                lo = 256 * b + 128 * k
+                move(R("ah", lo, lo + 128), (R("win", PL * b, PL * b + 2048), R("offa", 8 * k, 8 * k + 8)))
+            move(R("af", 256 * b, 256 * b + 256), R("ah", 256 * b, 256 * b + 256), 2.0)
 
-        mm(1, UF1, came)
-        mm(2, UF2, came)
-        late = [("m", h) for h in range(8)] + [(b, h) for b in range(4) for h in range(8)]
-        wide = [0, 4, 5, 6, 7]
+        if WHOLE[r]:
+            frames((lq, lsc, 0, C), 1, R("kr"))
+            copy(R("kl", C, C + H), (R("kr"), R(ll)))
+            pick_codes(border[0], R(lq), R(ll))
+            move(border[1], (R(lsc), R(ll)))
+        else:
+            frames(came, 1, R("kl", C, C + H))
+        for b in ("m", 0, 1, 2, 3):
+            for h in range(8):
+                unpack(b, h, came, FAR, H)
 
-        def unpack_came(k):
-            for _ in range(k):
-                b, h = late.pop(0)
-                bank = wide.pop(0)
-                wide.append(bank)
-                mm(bank, side(b, h), came)
-                if b == "m":
-                    act(R("mk", FAR + C * h, FAR + C * h + H), ps(bank, 0, H))
-                else:
-                    act(R("win", PL * b + FAR + C * h, PL * b + FAR + C * h + H), ps(bank, 0, H), ACT.Copy, 0.5)
-
-        unpack_came(6)
-        copy(R("f2", 0, H), ps(1, 0, H))
-        tt(R("fb", 0, 4 * H, 4), ps(2, 0, H), R("f2", 0, H), ALU.is_gt)
-        quant(R("fbq"), R("fbs"), R("fb"))
-        mm(3, WLOSS, ("fbq", "fbs", 0, 128))
-        wide[:0] = [1, 2]
-        unpack_came(2)
-        ts(R("kl", C, C + H), ps(3, 0, H), col(4), ALU.is_equal, col(5), ALU.mult)
-        copy(R("gk", 0, 128), (R("kl"), R("lk", 0, 8)))
-        act(R("gk", 128, 256), (R("kl"), R("lk", 8, 16)))
-        unpack_came(len(late))
         for k in range(2):
-            turn(R("tk", 128 * k, 128 * k + 128), R("gk", 128 * k, 128 * k + 128))
-        for k in range(2):
-            scan(R("sk", 128 * k, 128 * k + 128), R("keep", 0, 128), R("tk", 128 * k, 128 * k + 128), ALU.mult, ALU.add)
+            lo, hi = 128 * k, 128 * k + 128
+            move(R("gk", lo, hi), (R("kl"), R("lk", 8 * k, 8 * k + 8)))
+            turn(R("tk", lo, hi), R("gk", lo, hi))
+            scan(R("sk", lo, hi), R("keep", 0, 128), R("tk", lo, hi), ALU.mult, ALU.add)
         tt(R("ui"), (R("sk"), LU1), R("preu"), ALU.add)
         tt(R("ci"), (R("sk"), LX7), R("wx"), ALU.add)
         ts(R("uj"), R("ui"), MASK, ALU.bitwise_and)
         ts(R("cand"), R("ci"), MASK, ALU.bitwise_and)
         copy(R("offm"), R("uj"))
-        tt(R("d1", 0, 96, 3), R("cand", 32, 64), R("cand", 0, 32), ALU.subtract)
+        c0, c2, c1, c3 = [R("cand", 16 * k, 16 * k + 16) for k in range(4)]
+        tt(R("dc", 0, 64, 4), c0, c1, ALU.subtract)
+        tt(R("dc", 1, 64, 4), c3, c2, ALU.subtract)
+        tt(R("dc", 2, 64, 4), c1, c0, ALU.subtract)
+        tt(R("d1", 0, 128, 8), c2, c0, ALU.subtract)
+        copy(R("d1", 4, 128, 8), c0)
         for k in range(2):
-            copy(R("gm", 128 * k, 128 * k + 128), (R("mk"), R("offm", 8 * k, 8 * k + 8)))
-        copy(R("d1", 1, 96, 3), R("cand", 0, 32))
-        for k in range(2):
-            turn(R("tm", 128 * k, 128 * k + 128), R("gm", 128 * k, 128 * k + 128))
+            lo, hi = 128 * k, 128 * k + 128
+            move(R("gm", lo, hi), (R("mk"), R("offm", 8 * k, 8 * k + 8)))
+            turn(R("tm", lo, hi), R("gm", lo, hi))
         even, odd = R("tm", 0, 128, 4), R("tm", 128, 256, 4)
         tt(R("e2"), odd, even, ALU.max)
-        tt(R("d0", 1, 96, 3), odd, even, ALU.is_gt)
-        tt(R("d0", 2, 48, 3), R("e2", 16, 32), R("e2", 0, 16), ALU.is_le)
-        tt(R("d0", 50, 96, 3), R("e2", 16, 32), R("e2", 0, 16), ALU.is_gt)
+        tt(R("fl"), odd, even, ALU.is_gt)
+        tt(R("d0", 4, 128, 8), R("e2", 16, 32), R("e2", 0, 16), ALU.is_gt)
+        tt(R("d1", 1, 128, 2), (R("fl"), LF), R("dc"), ALU.mult)
         scan(R("e5"), R("d0"), R("d1"), ALU.mult, ALU.add)
-        tt(R("e8"), R("e5", 2, 48, 3), R("e5", 50, 96, 3), ALU.add)
-        for b in range(1 if r else 0, 4):
-            act(R("ah", 256 * b, 256 * b + 256), (R("win", PL * b, PL * b + 2048), R("offa")))
         for a in range(4):
             for k in range(4):
-                i = R("e8", k, 16, 4, 32 * a, 32 * a + 32)
-                if a == 3:
-                    act(R("ob", 4, 8, 1, 32 * k, 32 * k + 32), i)
+                i = R("e5", 8 * k + 5, 128, 32, 32 * a, 32 * a + 32)
+                if a >= 2:
+                    move(R("ob", 4 * a, 4 * a + 4, 1, 32 * k, 32 * k + 32), i)
                 else:
                     copy(R("offb", 4 * a, 4 * a + 4, 1, 32 * k, 32 * k + 32), i)
+        copy(R("offb", 8, 16), R("ob", 8, 16))
+        line[0] = "tail"
         for k in range(2):
-            for b in range(k, 4):
-                if k == 0 and b == 3:
-                    copy(R("offb", 12, 16), R("ob", 4, 8))
-                mean(k, b)
-            if k == 0:
-                mean(1, 0)
+            for b in range(4):
+                lo = 256 * b + 128 * k
+                tt(R("z", 512 * k + b, 512 * k + 512, 4), (R("win", PL * b, PL * b + PL), R("offb", 8 * k, 8 * k + 8)),
+                   R("ah", lo, lo + 128), ALU.add)
             quant(R("zq", 128 * k, 128 * k + 128), R("zs", 128 * k, 128 * k + 128), R("z", 512 * k, 512 * k + 512))
             for b in range(4):
-                mm(4 * k + b, ("wq", "wsc", 128 * b, 128), ("zq", "zs", 128 * k, 128))
-            if k == 0:
-                act(R("af"), R("ah"), ACT.Copy, 2.0)
-            for b in range(4):
-                act(R("rl", 256 * b + 128 * k, 256 * b + 128 * k + 128), ps(4 * k + b, 0, 128), ACT.Relu, 0.03125)
-        if r == 2:
-            ts(R("sj", 0, 16), R("cand", 0, 64, 4), 8, ALU.arith_shift_right, 7, ALU.bitwise_and)
-            copy(R("og"), (R("sj"), LOE))
-            turn(R("ot"), R("og"))
-            dmas("Y", "oute", [(T.oe[c, :], ap(R("ot", 0, 16, 1, c, 128, 8)), [R("ot")], []) for c in range(4)])
+                lo = 256 * b + 128 * k
+                v = mm(("wq", "wsc", 128 * b, 128), ("zq", "zs", 128 * k, 128))
+                act(R("rl", lo, lo + 128), ps(v, 0, 128), ACT.Relu, 0.03125)
         for k in range(2):
-            for b in range(k, 4):
-                state(k, b)
-            if k == 0:
-                state(1, 0)
-            scores(r + 1, k, "xn")
-            if k == 0 and r < 2:
-                for (b, h) in first[:EARLY]:
-                    unpack_half(r + 1, b, h, 0)
-            if r == 2:
-                mm(k, ("vq", "vs", 0, 128), ("q3", "s3", 128 * k, 128))
-                act(R("yb", 128 * k, 128 * k + 128), ps(k, 0, 128))
-                if k == 0:
-                    dmas("Y", "outa", [(T.oc[:, 0:512], T.q3[:, 0:128].bitcast(dt.uint8), [R("q3", 0, 128)], []),
-                                       (T.y[:, 0:128], T.yb[:, 0:128], [R("yb", 0, 128)], [])])
+            for b in range(4):
+                lo = 256 * b + 128 * k
+                tt(R("xn", 512 * k + b, 512 * k + 512, 4), R("rl", lo, lo + 128), R("af", lo, lo + 128), ALU.add)
+            quant(R("q%d" % (r + 1), 128 * k, 128 * k + 128), R("s%d" % (r + 1), 128 * k, 128 * k + 128), R("xn", 512 * k, 512 * k + 512))
+        line[0] = None
 
-    dmas("S", "out", [(T.y[:, 128:256], T.yb[:, 128:256], [R("yb", 128, 256)], [])])
-    dmas("Y", "out", [(T.oc[:, 512:1024], T.q3[:, 128:256].bitcast(dt.uint8), [R("q3")], [])]
-         + [(T.osc[4 * k:4 * k + 4, :], T.s3[32 * k:32 * k + 4, :], [R("s3")], []) for k in range(4)])
+    ts(R("sj", 0, 16), R("cand", 0, 64, 4), 8, ALU.arith_shift_right, 7, ALU.bitwise_and)
+    copy(R("og"), (R("sj"), LOE))
+    turn(R("ot"), R("og"))
+    dmas("Y", "oute", [(T.oe[c, :], ap(R("ot", 0, 16, 1, c, 128, 8)), [R("ot")], []) for c in range(4)], 0)
+    for k in range(2):
+        lo, hi = 128 * k, 128 * k + 128
+        v = mm(("vq", "vs", 0, 128), ("q3", "s3", lo, 128))
+        act(R("yb", lo, hi), ps(v, 0, 128))
+        codes = [(T.oc[:, 4 * lo:4 * hi], T.q3[:, lo:hi].bitcast(dt.uint8), [R("q3", lo, hi)], [])]
+        if k == 0:
+            dmas("Y", "outa", codes + [(T.y[:, lo:hi], T.yb[:, lo:hi], [R("yb", lo, hi)], [])], 1 << 17)
+        else:
+            dmas("S", "outy", [(T.y[:, lo:hi], T.yb[:, lo:hi], [R("yb", lo, hi)], [])], 1 << 16)
+            dmas("Y", "out", codes + [(T.osc[4 * j:4 * j + 4, :], T.s3[32 * j:32 * j + 4, :], [R("s3")], []) for j in range(4)], 1 << 16)
+
+    if not ARRANGED:
+        ARRANGED.extend(arrange(calls))
+    place.update(ARRANGED[1])
+    for i, q in ARRANGED[0]:
+        calls[i]["issue"](q)
     for sem in SEMAPHORES:
         if count[sem]:
             known["G"].pop(sem, None)

@@ -4,13 +4,22 @@ F32, BF, I32, U16, MX, U8 = "float32", "bfloat16", "int32", "uint16", "float8_e4
 STEP = [1, 2, 4]
 C, H = 256, 64
 FAR, MASK, PL = 4096, 4096 + 2047, 6144
-NPE = 5
+NPE = 4
 EARLY = 6
 NS = 0
 WHOLE = [True, True, False]
 BULK = 4
-BITS = [(0, 15), (0, 112), (0, 7), (0, 120), (3, 1), (2, 3), (0, 14), (0, 31), (0, 1), (4, 1)]
-CYC, HOP, PECYC, LOCAL, REMOTE, PASSES = 0.83e-3, 0.2, 0.6e-3, 1.2, 1.2, 4
+BITS = [(0, 15), (0, 112), (0, 7), (0, 120), (3, 1), (2, 3), (0, 14), (0, 31), (0, 1), (4, 1), (0, 96)]
+CYC, HOP, PECYC, LOCAL, REMOTE, PASSES = 0.83e-3, 0.21, 0.6e-3, 1.1, 0.9, 12
+SLACK, FIRST, MIX = 0.04, 1.5, 0.5
+MARGIN, ROWS, WIDE = 0.05, 0.3, 256
+SHAKE = 0.1
+MACHINES = [(0.21, 1.0, 1.0, 1.0), (0.23, 1.0, 0.7, 0.8), (0.18, 1.1, 1.35, 1.0), (0.2, 1.35, 1.2, 1.4), (0.24, 1.05, 1.0, 1.5)]
+FUSED, TWICE = 4, 1.5
+FOUR = True
+HALVES = True
+NSR = [0, 0, 0]
+LATE = True
 
 
 def _s(n, d):
@@ -27,21 +36,22 @@ SCRATCH = {
     "jm": _s(128, BF), "tri": _s(128, BF), "cn": _s(128, BF), "ch": _s(128, BF), "keep": _s(256, BF),
     "pi": _s(16, I32), "pf": _s(16, F32),
     "fi": _s(96, F32), "ft": _s(96, F32), "rows": _s(32, F32), "col": _s(16, F32), "wa": _s(128, BF), "wb": _s(128, BF),
-    "l2": _s(8, U16), "ls": _s(64, U16), "lk": _s(16, U16),
+    "l2": _s(8, U16), "ls": _s(64, U16), "lf": _s(64, F32), "lk": _s(16, U16),
     "ia": _s(16, F32), "ni": _s(32, I32), "n0": _s(32, F32), "nf": _s(64, F32), "nt": _s(64, F32), "n16": _s(16, F32), "tmp": _s(48, F32),
     "sc": _s(8, F32),
     "dd": _s(256, BF), "fo": _s(256, BF), "fd": _s(256, BF), "rk": _s(256, BF), "oh": _s(512, BF), "ohq": _s(128, MX), "ohs": _s(128, U8),
     "lt": _s(128, F32),
     "f2": _s(512, F32), "ff": _s(1024, BF), "ffq": _s(256, MX), "ffs": _s(256, U8),
-    "kl": _s(320, BF), "kr": _s(256, BF), "ga": _s(256, BF), "ta": _s(256, BF), "sa": _s(256, BF), "gk": _s(256, BF), "tk": _s(256, BF), "sk": _s(256, BF),
-    "oa": _s(16, F32), "offa": _s(16, U16), "pre": _s(16, F32), "preu": _s(16, F32), "wi": _s(16, I32), "wr": _s(16, I32), "wx": _s(64, F32),
-    "ui": _s(16, I32), "uj": _s(16, I32), "offm": _s(16, U16), "sj": _s(32, I32), "ci": _s(64, I32),
+    "kl": _s(320, BF), "kr": _s(256, BF), "ga": _s(256, BF), "ta": _s(256, BF), "sa": _s(128, F32), "gk": _s(256, BF), "tk": _s(256, BF), "sk": _s(128, F32),
+    "offa": _s(16, U16), "pre": _s(16, F32), "wi": _s(16, I32), "wr": _s(16, I32), "wy": _s(16, I32), "ib": _s(16, F32),
+    "da": _s(128, F32), "ad": _s(128, F32), "pat": _s(128, F32), "wf": _s(128, F32), "dk": _s(128, F32),
+    "offm": _s(32, U16), "sj": _s(32, I32),
     "cand": _s(64, I32), "gm": _s(256, F32), "tm": _s(256, F32),
     "e2": _s(32, F32), "fl": _s(32, F32), "dc": _s(64, F32), "e5": _s(128, F32), "d0": _s(128, F32), "d1": _s(128, F32),
     "offb": _s(16, U16), "ob": _s(16, F32),
-    "win": ("sbuf", [128, 4, PL], BF), "mk": _s(PL, F32),
+    "win": ("sbuf", [128, 4, PL], BF), "mk": _s(PL + C, F32),
     "bq": _s(320, MX), "bs": _s(320, U8),
-    "ah": _s(1024, BF), "af": _s(1024, BF), "z": _s(1024, BF), "zq": _s(256, MX), "zs": _s(256, U8), "rl": _s(1024, F32), "xn": _s(1024, BF),
+    "ah": _s(1024, BF), "bh": _s(1024, BF), "af": _s(1024, BF), "z": _s(1024, BF), "zq": _s(256, MX), "zs": _s(256, U8), "rl": _s(1024, F32), "xn": _s(1024, BF),
     "og": _s(32, F32), "ot": _s(32, F32), "yb": _s(256, F32),
 }
 for _r in range(4):
@@ -54,7 +64,7 @@ for _r in range(3):
     SCRATCH["ll%d" % _r] = _s(4, U16)
 SIZE = {F32: 4, BF: 2, I32: 4, U16: 2, MX: 4, U8: 1}
 
-SEMAPHORES = (["V", "S", "P", "G", "dx0", "dx1", "du", "dw", "dv", "dn", "sent", "out", "outa", "outy", "oute"]
+SEMAPHORES = (["V", "S", "P", "G", "dx0", "dx1", "du", "dw", "dv", "dn", "db", "sent", "go", "out", "outa", "outy", "oute"]
               + ["sw%d%d" % (r, b) for r in range(3) for b in range(4)]
               + ["%s%d" % (a, r) for r in range(3) for a in ("arra", "arrb", "arrl")])
 
@@ -91,7 +101,7 @@ def link(calls):
                 for (o, ow, j) in log.get(r[0] if r[0] != "ps" else r[1] // 512, []):
                     other = list(calls[j]["ways"])
                     if j != i and (((w or ow) and meets(r, o)) or (r[0] == "ps" and (other != list(c["ways"]) or len(other) > 1))):
-                        c["pred"][j] = 0.0 if other == ["P"] == list(c["ways"]) else HOP
+                        c["pred"][j] = 0.0 if other == ["P"] == list(c["ways"]) else HOP - calls[j]["lat"] * (r[0] not in SCRATCH)
         for regs, w in ((c["reads"], False), (c["writes"], True)):
             for r in regs:
                 old = log.setdefault(r[0] if r[0] != "ps" else r[1] // 512, [])
@@ -215,6 +225,133 @@ def arrange(calls):
     return best[1], best[2]
 
 
+def lay(calls, pred, succ, chain, forward):
+    n = len(calls)
+    ways, lat = [c["ways"] for c in calls], [c["lat"] for c in calls]
+    free = {q: 0.0 for q in "VSPGYA"}
+    lack = [set(p) for p in pred]
+    at = [0.0 if forward else lat[i] for i in range(n)]
+    ready = {q: {i for i in range(n) if q in ways[i] and not lack[i]} for q in free}
+    todo = {q: sorted((i for i in range(n) if [q] == list(ways[i])), key=lambda i: -chain[i]) for q in free}
+    left = {}
+    for c in calls:
+        for v in c["bank"]:
+            left[v] = left.get(v, 0) + 1
+    banks, last, bulk, place = {b: 0.0 for b in range(8)}, {}, set(), {}
+    seq, end, engines = [], [0.0] * n, 0.0
+
+    def when(i):
+        if forward and "P" in ways[i] and calls[i]["bank"][0] not in place:
+            if not banks or (calls[i]["bulk"] and len(bulk) >= BULK):
+                return 1e9
+            return max(at[i], min(banks.values()))
+        return at[i]
+
+    def guess(i, depth):
+        if len(lack[i]) > 3 or (lack[i] and not depth):
+            return 1e9
+        return max([at[i]] + [max(guess(j, depth - 1), min(free[q] for q in ways[j])) + max(ways[j].values()) + lat[j] + pred[i][j]
+                              for j in lack[i]])
+
+    while len(seq) < n:
+        t, q = min((max(free[q], min(map(when, ready[q]))), q) for q in free if ready[q])
+        now = sorted((i for i in ready[q] if when(i) <= t + 1e-9), key=lambda i: -chain[i])
+        if q == "V" and forward:
+            now = [i for i in now if len(ways[i]) == 1 or at[i] + MARGIN <= t or not calls[i]["bank"]]
+            if not now:
+                free[q] = t + 0.03
+                continue
+        soon = [(max(guess(h, 3), t), h) for h in todo[q][:30] if h not in now and chain[h] > chain[now[-1]]]
+        hold = 1e9
+        for i in now[:8]:
+            dur = ways[i][q]
+            late = [e for e, h in soon if chain[h] > chain[i] and e < t + dur
+                    and max(e + chain[h], e + ways[h][q] + chain[i]) < max(t + dur + chain[h], t + chain[i]) - SLACK]
+            if not late:
+                break
+            hold = min(hold, min(late))
+        else:
+            free[q] = max(hold, t + 0.02)
+            continue
+        if forward and q == "P" and calls[i]["bank"][0] not in place:
+            v = calls[i]["bank"][0]
+            place[v] = min(banks, key=lambda b: (banks[b], b))
+            del banks[place[v]]
+            if calls[i]["bulk"]:
+                bulk.add(v)
+        end[i] = t + ways[i][q] + (lat[i] if forward else 0.0)
+        if calls[i]["busy"] and forward:
+            end[i] = engines = max(end[i] - calls[i]["busy"], engines) + calls[i]["busy"]
+        if q != "A":
+            free[q] = t + ways[i][q]
+        for k in ways[i]:
+            ready[k].discard(i)
+        if len(ways[i]) == 1:
+            todo[q].remove(i)
+        seq.append((i, q))
+        for v in calls[i]["bank"] if forward else []:
+            left[v] -= 1
+            last[v] = max(last.get(v, 0.0), end[i])
+            if not left[v]:
+                banks[place[v]] = last[v] + HOP
+                bulk.discard(v)
+        for k, d in succ[i].items():
+            lack[k].discard(i)
+            at[k] = max(at[k], end[i] + d + (0.0 if forward else lat[k]))
+            if not lack[k]:
+                for w in ways[k]:
+                    ready[w].add(k)
+    return end, seq, place
+
+
+def arrange(calls):
+    link(calls)
+    pred, succ = [c["pred"] for c in calls], [{} for c in calls]
+    for i, c in enumerate(calls):
+        c["bank"] = sorted({r[1] // 512 for r in c["reads"] + c["writes"] if r[0] == "ps"})
+        for j, d in c["pred"].items():
+            succ[j][i] = d
+    chain, line, best = [0.0] * len(calls), {}, None
+    for i in reversed(range(len(calls))):
+        c = calls[i]
+        span = max(c["ways"].values()) + c["lat"]
+        chain[i] = span + max([0.0] + [d + chain[k] for k, d in succ[i].items()])
+        if c["line"]:
+            chain[i] = line[c["line"]] = max(chain[i], span + line.get(c["line"], 0.0))
+    seed = 1
+    for k in range(PASSES):
+        shaken = []
+        for a in chain:
+            seed = seed * 48271 % 2147483647
+            shaken.append(a + SHAKE * seed / 2147483647)
+        end, seq, place = lay(calls, pred, succ, shaken, True)
+        took = sum(replay(calls, seq, place, *m) for m in MACHINES)
+        if best is None or took < best[0]:
+            best = (took, seq, place)
+        chain = [MIX * a + (1 - MIX) * b for a, b in zip(lay(calls, succ, pred, end, False)[0], chain)]
+    return best[1], best[2]
+
+
+def replay(calls, seq, place, hop, compute, tensor, dma):
+    free, issued, end, bank, engines = {}, {}, {}, {}, 0.0
+    for i, q in seq:
+        c = calls[i]
+        t = free.get(q, 0.0)
+        for j, d in c["pred"].items():
+            t = max(t, end[j] + hop * (d > 0) if d in (0.0, HOP) else issued[j] + hop * (d + calls[j]["lat"] > 0))
+        if q == "P":
+            t = max(t, bank.get(place[c["bank"][0]], 0.0))
+        issued[i] = t + c["ways"][q] * (tensor if q == "P" else compute if not c["lat"] else 1.0)
+        end[i] = issued[i] + c["lat"] - c["busy"]
+        if c["busy"]:
+            end[i] = engines = max(end[i], engines) + c["busy"] * dma
+        if q != "A":
+            free[q] = issued[i]
+        for v in c["bank"] if q != "P" else []:
+            bank[place[v]] = max(bank.get(place[v], 0.0), end[i] + hop)
+    return max(end.values())
+
+
 ARRANGED = []
 
 
@@ -315,7 +452,7 @@ def rank_program(g, core, T, topo):
         if len(ins[0]) == 2:
             return (0.065 if scalar else 0.05) + 1.5 * CYC * size(o)
         narrow = not scalar and all(SIZE[SCRATCH[r[0]][2]] == 2 for r in (o,) + ins)
-        return CYC * max(64, size(o) * (0.5 if narrow else 1) * (2 if twice else 1))
+        return CYC * max(64, size(o) * ((TWICE if narrow else 2) if twice else 0.5 if narrow else 1))
 
     def val(s):
         return ap(s) if isinstance(s, tuple) else s
@@ -355,7 +492,13 @@ def rank_program(g, core, T, topo):
         op({"V": (plain(o, a, b, twice=a[0] != "ps"), lambda: g.vector.tensor_tensor(ap(o), src(a), ap(b), alu))}, regs(a) + [b], [o])
 
     def fill(o, c):
-        op({"V": (plain(o, o), lambda: g.vector.memset(ap(o), c))}, [], [o])
+        if SCRATCH[o[0]][2] in (F32, BF) and o[0] != "et":
+            for lo in range(0, size(o), 256):
+                part = R(o[0], o[1] + lo * o[3], min(o[2], o[1] + (lo + 256) * o[3]), o[3])
+                op({"S": s_act(part, zeros(size(part)), ACT.Identity, None, c), "V": (plain(part, part), lambda k=part: g.vector.memset(ap(k), c))},
+                   [zeros(size(part))], [part])
+        else:
+            op({"V": (plain(o, o), lambda: g.vector.memset(ap(o), c))}, [], [o])
 
     def turn(o, a):
         op({"V": (plain(o, a), lambda: g.vector.transpose(ap(o), ap(a)))}, [a], [o])
@@ -401,11 +544,14 @@ def rank_program(g, core, T, topo):
                 cast = [ap(k).bitcast(dt.uint8) if SCRATCH[k[0]][2] == MX else ap(k) for k in (o, a)]
                 g.remote_dma(cast[0], cast[1], T.sem[sem], T.sem.sent, pid, rid, sum(1 << e for e in engines(rank)))
                 count["sent"] += len(engines(rank))
-                if token:
-                    note("G", [], [token], "sent", count["sent"])
-            busy = 0.3 + size(a) * SIZE[SCRATCH[a[0]][2]] / 1e3
-            sent.append(record({"G": 0.3}, issue, [a], [token] if token and (a, o) == pieces[-1] else [], REMOTE, busy,
-                               {k: -c["lat"] for k, c in enumerate(calls) if "G" in c["ways"]}))
+                if token and (a, o) == pieces[-1]:
+                    g.sem_inc(T.sem.go, 1)
+                    count["go"] += 1
+                    note("G", [], [token], "go", count["go"])
+            busy = ROWS + size(a) * SIZE[SCRATCH[a[0]][2]] / 1.25e3
+            sent.append(record({"G": 0.3 if any(c["busy"] for c in calls if "G" in c["ways"]) else FIRST}, issue, [a], [token] if token and (a, o) == pieces[-1] else [], REMOTE, busy,
+                               {k: -c["lat"] for k, c in enumerate(calls) if "G" in c["ways"]
+                                and (c["lat"] or token or not LATE or c["writes"][0][0] not in ("pat", "fi"))}))
 
         def arrive(q):
             count[sem] = len(pieces) * len(engines((rank + d) % n))
@@ -413,7 +559,7 @@ def rank_program(g, core, T, topo):
             clock[(sem, count[sem])] = {}
         record({"A": 0.0}, arrive, [], [o for a, o in pieces], after={k: 0.0 for k in sent})
 
-    M, P112, P7, P120, M3, M2, P14, P31, P1, X = [R("pf", k, k + 1) for k in range(len(BITS))]
+    M, P112, P7, P120, M3, M2, P14, P31, P1, X, P96 = [R("pf", k, k + 1) for k in range(len(BITS))]
 
     def col(k):
         return R("col", k, k + 1)
@@ -421,10 +567,10 @@ def rank_program(g, core, T, topo):
     def zeros(k):
         return R("et", 0, 4 * k, 4)
 
-    U2, UF1, UF2 = ("u2q", "u2s", 0, 128), ("uaq", "uas", 0, 128), ("uaq", "uas", 128, 128)
+    U2, UF = ("u2q", "u2s", 0, 128), ("uaq", "uas", 128, 128)
     WHI, WLO, WLOSS = ("cq", "cs", 0, 128), ("cq", "cs", 128, 128), [("cq", "cs", 256, 128), ("cq", "cs", 384, 128)]
-    LU, LKI, LU2, LU1, LNB, LEX, LOE, LA, LX7, LF = [R("ls", a, b) for a, b in (
-        (0, 25), (26, 27), (28, 29), (30, 31), (32, 33), (34, 38), (38, 40), (40, 56), (56, 60), (60, 64))]
+    LX8, LKI, LU2, LU1, LNB, LOE, LA, LX7, LF = [R("ls", a, b) for a, b in (
+        (0, 8), (26, 27), (28, 29), (30, 31), (32, 33), (38, 40), (40, 56), (56, 60), (60, 64))]
 
     dmas("S", "du", [(T.uin[:], T.u[:], [], [R("uin")])], 1 << 17)
     for k in range(2):
@@ -434,8 +580,10 @@ def rank_program(g, core, T, topo):
     iota(R("jm"), [[1, 128]], 0, -1)
     iota(R("rows", 0, 16), [[16, 16]], 0, 0)
     iota(R("cn"), [[16, 4], [0, 2], [1, 16]], 0, 0)
-    iota(R("ch"), [[0, 16], [8, 8]], 0, 0)
-    iota(R("fi", 0, 32), [[0, 8], [16, 4]], 7, 2)
+    iota(R("ch"), [[0, 8], [8, 8], [0, 2]], 0, 0)
+    iota(R("rows", 16, 32), [[0, 4], [16, 4]], 1792, 0)
+    iota(R("pat"), [[0, 16], [-256, 8]], 1536, 0)
+    iota(R("fi", 0, 32), [[0, 8], [8, 4]], 7, 1)
     for k in range(2):
         iota(R("fi", 32 + 16 * k, 48 + 16 * k), [[1, 2], [2, 2], [8, 4]], 0, 0)
         iota(R("fi", 64 + 16 * k, 80 + 16 * k), [[1, 2], [4, 4], [8, 2]], 0, 0)
@@ -443,11 +591,9 @@ def rank_program(g, core, T, topo):
     for k, (shift, mask) in enumerate(BITS):
         ts(R("pi", k, k + 1), R("pi", 15, 16), shift, ALU.arith_shift_right, mask, ALU.bitwise_and)
     copy(R("pf", 0, 5), R("pi", 0, 5))
-    copy(R("pf", 5, 10), R("pi", 5, 10))
-    fill(R("rows", 16, 32, 2), 0.0)
-    fill(R("rows", 17, 32, 2), 256.0)
-    fill(R("ni"), 0)
+    copy(R("pf", 5, 11), R("pi", 5, 11))
     fill(R("et"), 0.0)
+    fill(R("ni"), 0)
     fill(R("l2"), 2)
     dmas("Y", "dn", [(ap(R("ni", 0, 16, 1, c, 128, 8)), T.nb[c, :], [], [R("ni")]) for c in range(4)]
          + [(ap(R("ni", 16, 32, 1, c, 128, 8)), T.e[c, :], [], [R("ni")]) for c in range(4)], 1 << 14)
@@ -456,8 +602,6 @@ def rank_program(g, core, T, topo):
         ts(R("et", 3 + 512 * k, 512 + 512 * k, 4), R("jm"), 0.0, ALU.is_equal)
     fill(R("oh"), 0.0)
     ts(R("tri"), R("jm"), 0.0, ALU.is_lt, 2.0 ** -100, ALU.mult)
-    fill(R("keep"), 1.0)
-    fill(R("keep", 0, 256, 16), 0.0)
     for b in range(4):
         quant(R("eq", 256 * b, 256 * b + 240), R("es", 256 * b, 256 * b + 240), R("et", 3 - b, 963 - b))
     lin(col(2), P7, 8.0)
@@ -466,7 +610,8 @@ def rank_program(g, core, T, topo):
     lin(R("wt", 1, 512, 2), zeros(256), None, col(6))
     lin(R("wt", 512, 1024, 2), zeros(256), None, M)
     lin(R("wt", 513, 1024, 2), zeros(256), None, M)
-    fill(R("wt", 1024, 1540), 0.0)
+    fill(R("wt", 1024, 1536), 0.0)
+    fill(R("wt", 1536, 1540), 0.0)
     fill(R("sj"), 0)
     fill(R("d0"), 1.0)
     fill(R("d0", 0, 128, 8), 0.0)
@@ -481,38 +626,44 @@ def rank_program(g, core, T, topo):
     tt(R("wt", 1026, 1538, 4), R("wa"), R("wb"), ALU.subtract)
     quant(R("cq", 0, 256), R("cs", 0, 256), R("wt", 0, 1024))
     quant(R("cq", 256, 384), R("cs", 256, 384), R("wt", 1026, 1538))
-    quant(R("cq", 384, 512), R("cs", 384, 512), R("wt", 1024, 1536))
-    quant(R("bq", 192, 320), R("bs", 192, 320), R("xin", 0, 512))
+    if not HALVES:
+        quant(R("cq", 384, 512), R("cs", 384, 512), R("wt", 1024, 1536))
     def listed(lo, hi, a, scale, bias, step=1):
-        ts(R("ls", lo, hi, step), a, scale, ALU.mult, bias, ALU.add)
+        lin(R("lf", lo, hi, step), a, scale, bias)
 
-    fill(R("ls"), 0)
+    fill(R("lf"), 0.0)
     lin(col(0), P7, 16.0, 1.0)
     lin(col(1), P14, 8.0)
     lin(col(7), M3, 16.0, 1.0)
     lin(col(11), X, None, P14)
     lin(col(8), P1, 16.0, M2)
-    lin(col(12), M2, 16.0, 7.0)
+    lin(col(12), M2, 8.0, 7.0)
+    lin(col(13), X, 8.0, 7.0)
     for k in range(2):
-        listed(4 * k, 4 * k + 4, R("rows", 0, 4), 2.0, col(7))
         listed(40 + k, 56, R("rows", 0, 8), 2.0, P31, 2)
         listed(38 + k, 39 + k, R("ft", 64, 65), 1.0, 2.0 * k)
-    listed(8, 16, zeros(8), 1.0, col(0))
+    listed(8, 12, R("rows", 0, 4), 2.0, col(7))
+    listed(12, 16, zeros(4), 1.0, col(0))
     listed(16, 25, zeros(9), 1.0, col(1))
     listed(26, 27, R("ft", 0, 1), 1.0, 0.0)
     listed(28, 29, col(11), 1.0, 0.0)
-    listed(30, 31, col(11), 16.0, 7.0)
+    listed(30, 31, P7, 16.0, col(13))
     listed(32, 33, R("ft", 32, 33), 1.0, 0.0)
-    listed(34, 38, R("rows", 0, 4), 0.25, M2)
-    listed(56, 60, R("rows", 0, 4), 4.0, col(12))
+    listed(0, 8, R("rows", 0, 8), 0.125, M3)
+    listed(56, 60, R("rows", 0, 4), 2.0, col(12))
     listed(60, 64, R("rows", 0, 4), 0.25, col(8))
-    lin(col(4), P7, -1.0)
-    lin(col(5), P7, 256.0)
-    lin(col(9), P7, -256.0)
-    ts(col(10), col(4), 1.0, ALU.add, col(5), ALU.mult)
-    lin(R("ia"), R("rows", 0, 16), None, M)
+    for lo, hi in ((8, 16), (16, 26), (26, 64), (0, 8)):
+        copy(R("ls", lo, hi), R("lf", lo, hi))
+    lin(col(4), P14, -0.5)
+    lin(col(5), P14, 0.5)
+    lin(col(9), M, -1.0, -1792.0)
+    lin(col(10), P96, 2.0, M)
+    fill(R("da"), 256.0)
+    lin(R("da", 7, 128, 8), R("rows", 0, 16), -1.0, col(9))
+    fill(R("ad"), -0.125)
+    lin(R("ib"), R("rows", 16, 32), None, col(10))
     copy(R("n0"), R("ni"))
-    for lo, hi in ((0, 16), (16, 25)):
+    for lo, hi in ((8, 16), (16, 25)):
         pick_codes(R("uaq", 16 * lo, 16 * hi), R("uq"), R("ls", lo, hi))
         move(R("uas", 16 * lo, 16 * hi), (R("us"), R("ls", lo, hi)))
     for k in range(4):
@@ -531,7 +682,9 @@ def rank_program(g, core, T, topo):
         return ("eq", "es", 256 * b + 16 * h, 128)
 
     def unpack(b, h, x, lo, k):
+        line[0] = "unpack"
         v = mm(side(b, h), x, bulk=True)
+        line[0] = None
         if b == "m":
             move(R("mk", lo + C * h, lo + C * h + k), ps(v, 0, k))
         else:
@@ -539,16 +692,15 @@ def rank_program(g, core, T, topo):
 
     def frames(x, k, out):
         many, two = size(out), size(out) // 128 or 1
-        a, b = mm(UF1, x), mm(UF2, x)
-        f2, ff = R("f2", C * k, C * k + many), R("ff", 512 * k, 512 * k + 4 * many // two, 4 // two)
-        move(f2, ps(a, 0, many))
-        tt(ff, ps(b, 0, many), f2, ALU.is_gt)
+        a = mm(UF, x)
+        f2, ff = R("f2", C * k, C * k + many, 1, 0, 64), R("ff", 512 * k, 512 * k + 4 * many // two, 4 // two, 0, 64)
+        move(f2, R("ps", 512 * a, 512 * a + many, 1, 0, 64))
+        tt(ff, R("ps", 512 * a, 512 * a + many, 1, 64, 128), f2, ALU.is_gt)
         quant(R("ffq", 128 * k, 128 * k + 128), R("ffs", 128 * k, 128 * k + 128), R("ff", 512 * k, 512 * k + 512))
         for j in range(two):
             v = ps(mm(WLOSS[j], ("ffq", "ffs", 128 * k, 128)), 0, many // two)
             o = R(out[0], out[1] + j, out[2], two)
-            op({"V": v_ts(o, v, col(4), ALU.is_equal, col(5), ALU.mult), "S": s_act(o, v, ACT.Relu, col(9), col(10))},
-               [v, col(4), col(5), col(9), col(10)], [o])
+            op({"V": v_ts(o, v, col(4), ALU.not_equal), "S": s_act(o, v, ACT.Sign, None, col(5))}, [v, col(4), col(5)], [o])
 
     first = [(b, h) for b in range(4) for h in (1, 2, 3)] + [(b, 0) for b in range(4)]
     more = [(b, h) for h in range(4, NPE) for b in range(4)]
@@ -566,11 +718,12 @@ def rank_program(g, core, T, topo):
             if r == 0:
                 quant(hq, hs, R("xin", 512 * k, 512 * k + 512))
             if WHOLE[r]:
-                send(d, "arr%s%d" % ("ab"[k], r), [(hq, R(lq, 128 * k, 128 * k + 128))] + ([(R(sn), R(lsc))] if k else []))
+                send(d, "arr%s%d" % ("ab"[k], r), [(hq, R(lq, 128 * k, 128 * k + 128))]
+                     + ([(hs, R(lsc, 128 * k, 128 * k + 128))] if FOUR else [(R(sn), R(lsc))] if k else []))
             down.append(ps(mm(half, U2), 0, 1))
             along.append(ps(mm(U2, half), 0, 128))
         act(R("sc", 0, 1), down[0])
-        lin(R("dd", 0, 128), along[0], -1.0, R("sc", 0, 1))
+        act(R("dd", 0, 128), along[0], ACT.Identity, -1.0, R("sc", 0, 1))
         ts(R("dd", 128, 256), along[1], down[1], ALU.subtract, -1.0, ALU.mult)
         ts(R("fo", 0, 128), along[1], R("sc", 0, 1), ALU.is_gt)
         ts(R("fo", 128, 256), along[0], down[1], ALU.is_ge)
@@ -591,7 +744,7 @@ def rank_program(g, core, T, topo):
             move(R(lsc, 0, H), (R(sn), R(lb)))
             send(d, "arrl%d" % r, [(R(lq, 0, H), border[0]), (R(lsc, 0, H), border[1])], gone)
 
-        todo = first + more + [("m", h) for h in range(8)]
+        todo = first + more + [("m", h) for h in range(9)]
         for j, (b, h) in enumerate(todo):
             if r and j < EARLY:
                 for k in range(2):
@@ -601,52 +754,60 @@ def rank_program(g, core, T, topo):
         for b in range(4):
             pairs = [(R("win", PL * b + C * NPE, PL * b + 2048, 1, 64 * k, 64 * k + 64),
                       R("win", PL * b + C * (NPE - 4), PL * b + 1024, 1, 64 - 64 * k, 128 - 64 * k)) for k in range(2)]
-            dmas("Y", "sw%d%d" % (r, b), [(ap(o), ap(i), [i] + ([gone] if b >= NS else []), [o]) for (o, i) in pairs],
+            dmas("Y", "sw%d%d" % (r, b), [(ap(o), ap(i), [i] + ([gone] if b >= NSR[r] else []), [o]) for (o, i) in pairs],
                  (8 - NPE) << 16)
         if r == 0:
+            dmas("Y", "db", [(T.bq[:, 192:256].bitcast(dt.uint8), T.q0[:, 0:H].bitcast(dt.uint8), [R("q0", 0, H)], [R("bq", 192, 256)]),
+                             (T.bs[:, 192:256], T.s0[:, 0:H], [R("s0", 0, H)], [R("bs", 192, 256)])], 5 << 13)
             dmas("Y", "dw", [(T.wq[:].bitcast(dt.uint8), T.wc[:], [gone, R("win", 3 * PL + 2047, 3 * PL + 2048)], [R("wq")]),
                              (T.wsc[:], T.ws[:], [], [R("wsc")])], 5 << 16)
         if r == 1:
             dmas("Y", "dv", [(T.vin[:], T.v[:], [R("win", 3 * PL + 2047, 3 * PL + 2048)], [R("vin")])], 1 << 17)
             quant(R("vq"), R("vs"), R("vin"))
-        frames(own, 0, R("kl", 0, C))
+        if HALVES:
+            for k in range(2):
+                frames((qn, sn, 128 * k, 128), k, R("kl", 128 * k, 128 * k + 128))
+        else:
+            frames(own, 0, R("kl", 0, C))
         move(R("ga"), (R("kl", 0, C), LA))
         turn(R("ta"), R("ga"))
-        scan(R("sa"), R("keep"), R("ta"), ALU.mult, ALU.add)
-        ts(R("pre"), (R("sa"), LKI), -1.0, ALU.mult, 2048.0, ALU.add)
-        tt(R("oa"), R("sa", 7, 256, 16), R("ia"), ALU.add)
-        tt(R("wi"), R("pre"), R("cand", 0, 64, 4), ALU.add)
-        copy(R("offa"), R("oa"))
+        scan(R("sa"), R("ta", 0, 256, 2), R("da"), ALU.mult, ALU.add)
+        ts(R("offa"), R("sa", 7, 128, 8), -1.0, ALU.mult)
+        tt(R("pre"), R("cand", 0, 64, 4), R("ib"), ALU.add)
+        tt(R("wi"), (R("sa"), LKI), R("pre"), ALU.add)
         ts(R("wr"), R("wi"), MASK, ALU.bitwise_and)
-        tt(R("preu"), (R("wr"), LU2), R("rows", 16, 32), ALU.add)
-        copy(R("wx"), (R("wr"), LEX))
+        ts(R("wy"), R("wi"), 1792, ALU.bitwise_and)
+        ts(R("ad", 7, 128, 8), R("wr"), 1 / 2048, ALU.mult)
+        tt(R("wf"), (R("wy"), LX8), R("pat"), ALU.is_equal)
+        tt(R("dk"), R("wf"), R("ad"), ALU.add)
         for b in range(4):
-            for k in range(2):
-                lo = 256 * b + 128 * k
-                move(R("ah", lo, lo + 128), (R("win", PL * b, PL * b + 2048), R("offa", 8 * k, 8 * k + 8)))
+            for lo in range(0, C, WIDE):
+                move(R("ah", C * b + lo, C * b + lo + WIDE), (R("win", PL * b, PL * b + 2048), R("offa", lo // 16, (lo + WIDE) // 16)))
             move(R("af", 256 * b, 256 * b + 256), R("ah", 256 * b, 256 * b + 256), 2.0)
 
         if WHOLE[r]:
-            frames((lq, lsc, 0, C), 1, R("kr"))
+            if HALVES:
+                for k in range(2):
+                    frames((lq, lsc, 128 * k, 128), k, R("kr", 128 * k, 128 * k + 128))
+            else:
+                frames((lq, lsc, 0, C), 1, R("kr"))
             copy(R("kl", C, C + H), (R("kr"), R(ll)))
             pick_codes(border[0], R(lq), R(ll))
             move(border[1], (R(lsc), R(ll)))
         else:
             frames(came, 1, R("kl", C, C + H))
         for b in ("m", 0, 1, 2, 3):
-            for h in range(8):
+            for h in range(9 if b == "m" else 8):
                 unpack(b, h, came, FAR, H)
 
         for k in range(2):
             lo, hi = 128 * k, 128 * k + 128
             move(R("gk", lo, hi), (R("kl"), R("lk", 8 * k, 8 * k + 8)))
             turn(R("tk", lo, hi), R("gk", lo, hi))
-            scan(R("sk", lo, hi), R("keep", 0, 128), R("tk", lo, hi), ALU.mult, ALU.add)
-        tt(R("ui"), (R("sk"), LU1), R("preu"), ALU.add)
-        tt(R("ci"), (R("sk"), LX7), R("wx"), ALU.add)
-        ts(R("uj"), R("ui"), MASK, ALU.bitwise_and)
-        ts(R("cand"), R("ci"), MASK, ALU.bitwise_and)
-        copy(R("offm"), R("uj"))
+            scan(R("sk", lo // 2, hi // 2), R("tk", lo, hi, 2), R("dk", lo // 2, hi // 2), ALU.mult, ALU.add)
+        for k in range(2):
+            ts(R("offm", k, 32, 2), (R("sk"), LU1), 2048.0, ALU.mult, 256.0 * k, ALU.add)
+        ts(R("cand"), (R("sk"), LX7), 2048.0, ALU.mult)
         c0, c2, c1, c3 = [R("cand", 16 * k, 16 * k + 16) for k in range(4)]
         tt(R("dc", 0, 64, 4), c0, c1, ALU.subtract)
         tt(R("dc", 1, 64, 4), c3, c2, ALU.subtract)
@@ -667,16 +828,20 @@ def rank_program(g, core, T, topo):
             for k in range(4):
                 i = R("e5", 8 * k + 5, 128, 32, 32 * a, 32 * a + 32)
                 if a >= 2:
-                    move(R("ob", 4 * a, 4 * a + 4, 1, 32 * k, 32 * k + 32), i)
+                    act(R("ob", 4 * a, 4 * a + 4, 1, 32 * k, 32 * k + 32), i)
                 else:
                     copy(R("offb", 4 * a, 4 * a + 4, 1, 32 * k, 32 * k + 32), i)
-        copy(R("offb", 8, 16), R("ob", 8, 16))
         line[0] = "tail"
         for k in range(2):
             for b in range(4):
                 lo = 256 * b + 128 * k
-                tt(R("z", 512 * k + b, 512 * k + 512, 4), (R("win", PL * b, PL * b + PL), R("offb", 8 * k, 8 * k + 8)),
-                   R("ah", lo, lo + 128), ALU.add)
+                parts = (R("win", PL * b, PL * b + PL), R("offb", 8 * k, 8 * k + 8))
+                if 4 * k + b >= FUSED:
+                    act(R("bh", lo, lo + 128), parts)
+                    parts = R("bh", lo, lo + 128)
+                tt(R("z", 512 * k + b, 512 * k + 512, 4), parts, R("ah", lo, lo + 128), ALU.add)
+                if (k, b) == (0, 0):
+                    copy(R("offb", 8, 16), R("ob", 8, 16))
             quant(R("zq", 128 * k, 128 * k + 128), R("zs", 128 * k, 128 * k + 128), R("z", 512 * k, 512 * k + 512))
             for b in range(4):
                 lo = 256 * b + 128 * k

@@ -4,22 +4,33 @@ F32, BF, I32, U16, MX, U8 = "float32", "bfloat16", "int32", "uint16", "float8_e4
 STEP = [1, 2, 4]
 C, H = 256, 64
 FAR, MASK, PL = 4096, 4096 + 2047, 6144
-NPE = 4
-EARLY = 6
-NS = 0
 WHOLE = [True, True, False]
+FOUR = [False, True, True]
+BOTH = False
+ALL = True
+TWO = [0, 2, 2]
+BIG = 1e29
+POLISH, WARM = 7000, 0.03
+URGENT = 0.2
+SPINE = ("dd", "fo", "fd", "rk", "oh", "ohq", "lt", "lb0", "lb1", "lb2", "lq2", "lsc2", "ge", "te", "me", "ke", "sk", "offm", "gm", "tm", "e2", "fl", "d0", "d1", "e5",
+         "offb", "ob", "bh", "z", "zq", "rl", "xn", "q1", "q2", "q3", "bq", "bs")
+SOON = [0, 0, 0]
+EARLY = 6
+FUSED = 4
 BULK = 4
-BITS = [(0, 15), (0, 112), (0, 7), (0, 120), (3, 1), (2, 3), (0, 14), (0, 31), (0, 1), (4, 1), (0, 96)]
-CYC, HOP, PECYC, LOCAL, REMOTE, PASSES = 0.83e-3, 0.21, 0.6e-3, 1.1, 0.9, 12
-SLACK, FIRST, MIX = 0.04, 1.5, 0.5
-MARGIN, ROWS, WIDE = 0.05, 0.3, 256
-SHAKE = 0.1
+CYC, PECYC, HOP, LOCAL, REMOTE, ROWS, FIRST = 0.83e-3, 0.6e-3, 0.21, 1.1, 0.9, 0.3, 1.5
+PASSES, SLACK, MARGIN, SHAKE = 30, 0.04, 0.05, 0.15
 MACHINES = [(0.21, 1.0, 1.0, 1.0), (0.23, 1.0, 0.7, 0.8), (0.18, 1.1, 1.35, 1.0), (0.2, 1.35, 1.2, 1.4), (0.24, 1.05, 1.0, 1.5)]
-FUSED, TWICE = 4, 1.5
-FOUR = True
-HALVES = True
-NSR = [0, 0, 0]
-LATE = True
+FIELDS = [
+    ("lnb", [([[1, 2], [2, 2], [8, 4]], 0)] * 2, 0),
+    ("lki", [([[8, 2], [0, 4], [16, 2]], 7), ([[-8, 2], [0, 4], [16, 2]], 15)], 1),
+    ("lp", [([[4, 2], [8, 8]], 0), ([[-4, 2], [8, 8]], 4)], 0),
+    ("ib0", [([[16, 2], [1, 16]], 0)], 2), ("ib1", [([[-16, 2], [1, 16]], 16)], 2),
+    ("lu2", [([[4, 4], [1, 2]], 0), ([[4, 4], [-1, 2]], 1), ([[4, 4], [1, 2]], 2), ([[4, 4], [-1, 2]], 3)], 0),
+    ("lx7", [([[8, 2], [64, 2], [0, 4]], 7), ([[8, 2], [-64, 2], [0, 4]], 71)], 0),
+    ("lfl", [([[1, 4], [0, 2], [16, 2]], 0)] * 2, 0), ("loe", [([[1, 2], [4, 4], [8, 2]], 0)] * 2, 0)]
+GROUPS = [(0, 3), (3, 6), (6, 9)]
+BITS = [("m", 0, 15), ("p112", 0, 112), ("h", 1, 7), ("p1", 0, 1), ("p31", 0, 31), ("m3", 3, 1)]
 
 
 def _s(n, d):
@@ -30,28 +41,30 @@ SCRATCH = {
     "ps": ("psum", [128, 4096], F32),
     "xin": _s(1024, BF), "uin": _s(512, BF), "vin": _s(512, BF),
     "wq": _s(512, MX), "wsc": _s(512, U8), "uq": _s(128, MX), "us": _s(128, U8), "vq": _s(128, MX), "vs": _s(128, U8),
-    "u2q": _s(128, MX), "u2s": _s(128, U8), "uaq": _s(400, MX), "uas": _s(400, U8),
+    "u2q": _s(128, MX), "u2s": _s(128, U8), "uaq": _s(144, MX), "uas": _s(144, U8),
     "et": _s(1040, BF), "eq": _s(1024, MX), "es": _s(1024, U8),
-    "wt": _s(1540, BF), "cq": _s(512, MX), "cs": _s(512, U8),
-    "jm": _s(128, BF), "tri": _s(128, BF), "cn": _s(128, BF), "ch": _s(128, BF), "keep": _s(256, BF),
-    "pi": _s(16, I32), "pf": _s(16, F32),
-    "fi": _s(96, F32), "ft": _s(96, F32), "rows": _s(32, F32), "col": _s(16, F32), "wa": _s(128, BF), "wb": _s(128, BF),
-    "l2": _s(8, U16), "ls": _s(64, U16), "lf": _s(64, F32), "lk": _s(16, U16),
-    "ia": _s(16, F32), "ni": _s(32, I32), "n0": _s(32, F32), "nf": _s(64, F32), "nt": _s(64, F32), "n16": _s(16, F32), "tmp": _s(48, F32),
-    "sc": _s(8, F32),
+    "wt": _s(1024, BF), "cq": _s(256, MX), "cs": _s(256, U8),
+    "jm": _s(128, BF), "tri": _s(128, BF), "cn": _s(128, BF),
+    "fi": _s(32 * len(FIELDS), F32), "ft": _s(32 * len(FIELDS), F32), "rows": _s(32, F32), "up": _s(8, F32),
+    "pi": _s(8, I32), "pf": _s(8, F32), "six": _s(16, F32),
+    "l2": _s(16, U16), "ls": _s(64, U16), "lk": _s(16, U16),
+    "ni": _s(32, I32), "n0": _s(32, F32), "nf": _s(64, F32), "nt": _s(64, F32), "n16": _s(16, F32), "tmp": _s(80, F32),
     "dd": _s(256, BF), "fo": _s(256, BF), "fd": _s(256, BF), "rk": _s(256, BF), "oh": _s(512, BF), "ohq": _s(128, MX), "ohs": _s(128, U8),
     "lt": _s(128, F32),
-    "f2": _s(512, F32), "ff": _s(1024, BF), "ffq": _s(256, MX), "ffs": _s(256, U8),
-    "kl": _s(320, BF), "kr": _s(256, BF), "ga": _s(256, BF), "ta": _s(256, BF), "sa": _s(128, F32), "gk": _s(256, BF), "tk": _s(256, BF), "sk": _s(128, F32),
+    "sa": _s(128, F32), "pr": _s(256, F32), "cap": _s(64, F32),
+    "ga": _s(256, F32), "ta": _s(256, F32), "ma": _s(144, F32), "ka": _s(128, F32),
+    "ge": _s(256, F32), "te": _s(256, F32), "me": _s(144, F32), "ke": _s(128, F32),
+    "sk": _s(128, F32),
     "offa": _s(16, U16), "pre": _s(16, F32), "wi": _s(16, I32), "wr": _s(16, I32), "wy": _s(16, I32), "ib": _s(16, F32),
     "da": _s(128, F32), "ad": _s(128, F32), "pat": _s(128, F32), "wf": _s(128, F32), "dk": _s(128, F32),
     "offm": _s(32, U16), "sj": _s(32, I32),
     "cand": _s(64, I32), "gm": _s(256, F32), "tm": _s(256, F32),
     "e2": _s(32, F32), "fl": _s(32, F32), "dc": _s(64, F32), "e5": _s(128, F32), "d0": _s(128, F32), "d1": _s(128, F32),
     "offb": _s(16, U16), "ob": _s(16, F32),
-    "win": ("sbuf", [128, 4, PL], BF), "mk": _s(PL + C, F32),
-    "bq": _s(320, MX), "bs": _s(320, U8),
-    "ah": _s(1024, BF), "bh": _s(1024, BF), "af": _s(1024, BF), "z": _s(1024, BF), "zq": _s(256, MX), "zs": _s(256, U8), "rl": _s(1024, F32), "xn": _s(1024, BF),
+    "win": _s(4 * PL, BF), "mk": _s(H + PL + C, F32),
+    "bq": _s(256, MX), "bs": _s(256, U8),
+    "ah": _s(1024, BF), "bh": _s(1024, BF), "af": _s(1024, BF), "z": _s(1024, BF), "zq": _s(256, MX), "zs": _s(256, U8),
+    "rl": _s(1024, F32), "xn": _s(1024, BF),
     "og": _s(32, F32), "ot": _s(32, F32), "yb": _s(256, F32),
 }
 for _r in range(4):
@@ -61,21 +74,17 @@ for _r in range(3):
     SCRATCH["lq%d" % _r] = _s(256, MX)
     SCRATCH["lsc%d" % _r] = _s(256, U8)
     SCRATCH["lb%d" % _r] = _s(4, U16)
-    SCRATCH["ll%d" % _r] = _s(4, U16)
+    if WHOLE[_r]:
+        SCRATCH["ll%d" % _r] = _s(4, U16)
 SIZE = {F32: 4, BF: 2, I32: 4, U16: 2, MX: 4, U8: 1}
 
-SEMAPHORES = (["V", "S", "P", "G", "dx0", "dx1", "du", "dw", "dv", "dn", "db", "sent", "go", "out", "outa", "outy", "oute"]
-              + ["sw%d%d" % (r, b) for r in range(3) for b in range(4)]
+SEMAPHORES = (["V", "S", "P", "G", "dx0", "dx1", "du", "dw", "dv", "dn", "db", "dz0", "dz1", "dz2", "sent", "go", "out", "outa", "outy", "oute"]
+              + ["%s%d%d" % (a, r, b) for r in range(3) for b in range(4) for a in ("sv", "sw")]
               + ["%s%d" % (a, r) for r in range(3) for a in ("arra", "arrb", "arrl")])
 
 
-def width(name):
-    shape = SCRATCH[name][1]
-    return shape[1] * (shape[2] if len(shape) == 3 else 1)
-
-
 def R(name, c0=0, c1=None, step=1, p0=0, p1=128, pstep=1):
-    return (name, c0, width(name) if c1 is None else c1, step, p0, p1, pstep)
+    return (name, c0, SCRATCH[name][1][1] if c1 is None else c1, step, p0, p1, pstep)
 
 
 def size(r):
@@ -110,125 +119,10 @@ def link(calls):
                 old.append((r, w, i))
 
 
-def arrange(calls):
-    link(calls)
-    n = len(calls)
-    span = [max(c["ways"].values()) + c["lat"] for c in calls]
-    users = {}
-    for i, c in enumerate(calls):
-        c["bank"] = sorted({r[1] // 512 for r in c["reads"] + c["writes"] if r[0] == "ps"})
-        for v in c["bank"]:
-            users.setdefault(v, []).append(i)
-    succ = [[] for _ in calls]
-    for i, c in enumerate(calls):
-        for j, d in c["pred"].items():
-            succ[j].append((i, d))
-    best, behind, chain = None, {}, None
-    for _ in range(PASSES):
-        new, line = [0.0] * n, {}
-        for i in reversed(range(n)):
-            new[i] = span[i] + max([0.0] + [d + new[k] for k, d in succ[i]])
-            if i in behind:
-                new[i] = max(new[i], calls[i]["ways"][way[i]] + chain[behind[i]])
-            if calls[i]["line"]:
-                new[i] = line[calls[i]["line"]] = max(new[i], span[i] + line.get(calls[i]["line"], 0.0))
-        chain = new if chain is None else [(a + b) / 2 for a, b in zip(chain, new)]
-        start, way, end = {}, {}, {}
-        free = {q: 0.0 for q in "VSPGYA"}
-        waiting = [len(c["pred"]) for c in calls]
-        ready = {i: 0.0 for i in range(n) if not waiting[i]}
-        todo = {q: [i for i in range(n) if q in calls[i]["ways"]] for q in free}
-        banks, held, left, last = {b: 0.0 for b in range(8)}, {}, {v: len(u) for v, u in users.items()}, {}
-        bulk, place, seq, engines = set(), {}, [], 0.0
-
-        def opens(i):
-            return [v for v in calls[i]["bank"] if v not in place]
-
-        def when(i):
-            if opens(i):
-                if not banks or (calls[i]["bulk"] and len(bulk) >= BULK):
-                    return None
-                return max(ready[i], min(banks.values()))
-            return ready[i]
-
-        def guess(i, depth, memo):
-            if i in ready:
-                return ready[i]
-            if i not in memo:
-                memo[i] = 1e9
-                if depth:
-                    memo[i] = max(end[j] + d if j in end else
-                                  max(guess(j, depth - 1, memo), min(free[q] for q in calls[j]["ways"])) + span[j] + d
-                                  for j, d in calls[i]["pred"].items())
-            return memo[i]
-
-        while len(seq) < n:
-            turn_ = []
-            for q in free:
-                ts_ = [when(i) for i in ready if q in calls[i]["ways"]]
-                ts_ = [t for t in ts_ if t is not None]
-                if ts_:
-                    turn_.append((max(free[q], min(ts_)), q))
-            t, q = min(turn_)
-            now = sorted((i for i in ready if q in calls[i]["ways"] and when(i) is not None and when(i) <= t + 1e-9), key=lambda i: -chain[i])
-            soon = [i for i in todo[q][:80] if len(calls[i]["ways"]) == 1 and i not in now]
-            memo, pick, hold = {}, None, None
-            for i in now[:6]:
-                dur = calls[i]["ways"][q]
-                late = None
-                for h in soon:
-                    if chain[h] > chain[i]:
-                        e = max(guess(h, 4, memo), t)
-                        if e < t + dur and max(e + chain[h], e + calls[h]["ways"][q] + chain[i]) < max(t + dur + chain[h], t + chain[i]) - 0.06:
-                            late = e if late is None else min(late, e)
-                if late is None:
-                    pick = i
-                    break
-                hold = late if hold is None else min(hold, late)
-            if pick is None:
-                free[q] = max(hold, t + 0.02)
-                continue
-            i = pick
-            for v in opens(i):
-                place[v] = min(banks, key=lambda b: (banks[b], b))
-                del banks[place[v]]
-                if calls[i]["bulk"]:
-                    bulk.add(v)
-            start[i], way[i] = t, q
-            end[i] = t + calls[i]["ways"][q] + calls[i]["lat"]
-            if calls[i]["busy"]:
-                end[i] = engines = max(end[i] - calls[i]["busy"], engines) + calls[i]["busy"]
-            if q != "A":
-                free[q] = t + calls[i]["ways"][q]
-            del ready[i]
-            for k in calls[i]["ways"]:
-                todo[k].remove(i)
-            seq.append(i)
-            for v in calls[i]["bank"]:
-                left[v] -= 1
-                last[v] = max(last.get(v, 0.0), end[i])
-                if not left[v]:
-                    banks[place[v]] = last[v] + HOP
-                    bulk.discard(v)
-            for k, d in succ[i]:
-                waiting[k] -= 1
-                if not waiting[k]:
-                    ready[k] = max(end[j] + dj for j, dj in calls[k]["pred"].items())
-        if best is None or max(end.values()) < best[0]:
-            best = (max(end.values()), [(i, way[i]) for i in seq], place)
-        behind, prev = {}, {}
-        for i in seq:
-            q = way[i]
-            if q in prev and q != "A" and start[i] < start[prev[q]] + calls[prev[q]]["ways"][q] + 0.05:
-                behind[prev[q]] = i
-            prev[q] = i
-    return best[1], best[2]
-
-
 def lay(calls, pred, succ, chain, forward):
     n = len(calls)
     ways, lat = [c["ways"] for c in calls], [c["lat"] for c in calls]
-    free = {q: 0.0 for q in "VSPGYA"}
+    free, idle = {q: 0.0 for q in "VSPGYA"}, {q: 0 for q in "VSPGYA"}
     lack = [set(p) for p in pred]
     at = [0.0 if forward else lat[i] for i in range(n)]
     ready = {q: {i for i in range(n) if q in ways[i] and not lack[i]} for q in free}
@@ -265,14 +159,18 @@ def lay(calls, pred, succ, chain, forward):
         hold = 1e9
         for i in now[:8]:
             dur = ways[i][q]
-            late = [e for e, h in soon if chain[h] > chain[i] and e < t + dur
+            late = [e for e, h in soon if chain[h] > chain[i] and e < t + dur - 1e-6
                     and max(e + chain[h], e + ways[h][q] + chain[i]) < max(t + dur + chain[h], t + chain[i]) - SLACK]
             if not late:
                 break
             hold = min(hold, min(late))
         else:
-            free[q] = max(hold, t + 0.02)
-            continue
+            idle[q] += 1
+            if idle[q] < 12:
+                free[q] = max(hold, t + 0.02)
+                continue
+            i = now[0]
+        idle[q] = 0
         if forward and q == "P" and calls[i]["bank"][0] not in place:
             v = calls[i]["bank"][0]
             place[v] = min(banks, key=lambda b: (banks[b], b))
@@ -304,11 +202,78 @@ def lay(calls, pred, succ, chain, forward):
     return end, seq, place
 
 
+def replay(calls, seq, place, hop, compute, tensor, dma):
+    n = len(calls)
+    free, issued, end, why = {q: (0.0, None) for q in "VSPGYA"}, [0.0] * n, [0.0] * n, [None] * n
+    bank, engines = [(0.0, None)] * 8, 0.0
+    for i, q in seq:
+        c = calls[i]
+        t, why[i] = free[q]
+        for j, landed, waits in c["needs"]:
+            e = (end[j] if landed else issued[j]) + hop * waits
+            if e > t:
+                t, why[i] = e, j
+        if q == "P" and bank[place[c["bank"][0]]][0] > t:
+            t, why[i] = bank[place[c["bank"][0]]]
+        issued[i] = t + c["ways"][q] * (tensor if q == "P" else dma if c["lat"] else compute)
+        end[i] = issued[i] + c["lat"] - c["busy"]
+        if c["busy"]:
+            end[i] = engines = max(end[i], engines) + c["busy"] * dma
+        if q != "A":
+            free[q] = (issued[i], i)
+        if q != "P":
+            for v in c["bank"]:
+                bank[place[v]] = max(bank[place[v]], (end[i] + hop, i))
+    return max(end), end.index(max(end)), why
+
+
+def polish(calls, seq, place):
+    hard, users = [set(c["pred"]) for c in calls], {}
+    for i, q in seq:
+        for v in calls[i]["bank"]:
+            before = users.setdefault(place[v], [])
+            hard[i].update(j for j, w in before if w != v)
+            before[:] = [e for e in before if e[1] == v] + [(i, v)] if q == "P" else before + [(i, v)]
+    now, seed = [replay(calls, seq, place, *m) for m in MACHINES], 7
+    for k in range(POLISH):
+        took, i, why = now[k % len(MACHINES)]
+        at, pairs = {j: p for p, (j, q) in enumerate(seq)}, []
+        while why[i] is not None:
+            if why[i] not in hard[i]:
+                pairs.append((why[i], i))
+            i = why[i]
+        seed = seed * 48271 % 2147483647
+        j, i = pairs[seed % len(pairs)]
+        new, kind = list(seq), seed // 4096 % 4
+        if kind >= 2:
+            who = (j, i)[kind - 2]
+            other = [q for q in calls[who]["ways"] if q != seq[at[who]][1]]
+            if not other:
+                kind -= 2
+            else:
+                new[at[who]] = (who, other[0])
+        if kind == 0:
+            if any(at[h] > at[j] for h in hard[i]):
+                continue
+            new.insert(at[j], new.pop(at[i]))
+        if kind == 1:
+            if any(j in hard[h] for h, q in seq[at[j] + 1:at[i]]):
+                continue
+            new.insert(at[i], new.pop(at[j]))
+        if replay(calls, new, place, *MACHINES[k % len(MACHINES)])[0] <= took + WARM:
+            then = [replay(calls, new, place, *m) for m in MACHINES]
+            if sum(a[0] for a in then) <= sum(a[0] for a in now) + WARM * (1 - k / POLISH):
+                now, seq = then, new
+    return seq
+
+
 def arrange(calls):
     link(calls)
     pred, succ = [c["pred"] for c in calls], [{} for c in calls]
     for i, c in enumerate(calls):
         c["bank"] = sorted({r[1] // 512 for r in c["reads"] + c["writes"] if r[0] == "ps"})
+        c["needs"] = [(j, d in (0.0, HOP), d > 0 if d in (0.0, HOP) else d + calls[j]["lat"] > 0) for j, d in c["pred"].items()
+                      if not any(calls[k]["pred"].get(j) == HOP and e == HOP for k, e in c["pred"].items())]
         for j, d in c["pred"].items():
             succ[j][i] = d
     chain, line, best = [0.0] * len(calls), {}, None
@@ -321,35 +286,15 @@ def arrange(calls):
     seed = 1
     for k in range(PASSES):
         shaken = []
-        for a in chain:
+        for a, c in zip(chain, calls):
             seed = seed * 48271 % 2147483647
-            shaken.append(a + SHAKE * seed / 2147483647)
+            shaken.append(a + SHAKE * seed / 2147483647 + URGENT * (k % 3) * (c["writes"][:1] != [] and c["writes"][0][0] in SPINE))
         end, seq, place = lay(calls, pred, succ, shaken, True)
-        took = sum(replay(calls, seq, place, *m) for m in MACHINES)
+        took = sum(replay(calls, seq, place, *m)[0] for m in MACHINES)
         if best is None or took < best[0]:
             best = (took, seq, place)
-        chain = [MIX * a + (1 - MIX) * b for a, b in zip(lay(calls, succ, pred, end, False)[0], chain)]
-    return best[1], best[2]
-
-
-def replay(calls, seq, place, hop, compute, tensor, dma):
-    free, issued, end, bank, engines = {}, {}, {}, {}, 0.0
-    for i, q in seq:
-        c = calls[i]
-        t = free.get(q, 0.0)
-        for j, d in c["pred"].items():
-            t = max(t, end[j] + hop * (d > 0) if d in (0.0, HOP) else issued[j] + hop * (d + calls[j]["lat"] > 0))
-        if q == "P":
-            t = max(t, bank.get(place[c["bank"][0]], 0.0))
-        issued[i] = t + c["ways"][q] * (tensor if q == "P" else compute if not c["lat"] else 1.0)
-        end[i] = issued[i] + c["lat"] - c["busy"]
-        if c["busy"]:
-            end[i] = engines = max(end[i], engines) + c["busy"] * dma
-        if q != "A":
-            free[q] = issued[i]
-        for v in c["bank"] if q != "P" else []:
-            bank[place[v]] = max(bank.get(place[v], 0.0), end[i] + hop)
-    return max(end.values())
+        chain = [(a + b) / 2 for a, b in zip(lay(calls, succ, pred, end, False)[0], chain)]
+    return polish(calls, best[1], best[2]), best[2]
 
 
 ARRANGED = []
@@ -375,9 +320,6 @@ def rank_program(g, core, T, topo):
 
     def ap(r):
         r = real(r)
-        if len(SCRATCH[r[0]][1]) == 3:
-            w = SCRATCH[r[0]][1][2]
-            return T[r[0]][r[4]:r[5], r[1] // w, r[1] % w:(r[2] - 1) % w + 1]
         if r[6] != 1:
             return T[r[0]][r[4]:r[5]:r[6], r[1]:r[2]]
         if r[3] != 1:
@@ -430,9 +372,9 @@ def rank_program(g, core, T, topo):
             forms[q][1]().then_inc(T.sem[q], 1)
             count[q] += 1
             note(q, reads, writes, q, count[q])
-        record({q: f[0] for q, f in forms.items()}, issue, reads, writes, bulk=bulk)
+        return record({q: f[0] for q, f in forms.items()}, issue, reads, writes, bulk=bulk)
 
-    def dmas(q, sem, items, nbytes):
+    def dmas(q, sem, items, nbytes, after=None):
         def issue(q):
             for (o, i, rd, wr) in items:
                 order(q, rd, wr)
@@ -440,7 +382,14 @@ def rank_program(g, core, T, topo):
                 count[sem] += 16
             for (o, i, rd, wr) in items:
                 note(q, rd, wr, sem, count[sem])
-        record({q: 0.05 * len(items)}, issue, [r for i in items for r in i[2]], [r for i in items for r in i[3]], LOCAL, 0.05 + nbytes / 250e3)
+        return record({q: 0.05 * len(items)}, issue, [r for i in items for r in i[2]], [r for i in items for r in i[3]],
+                      LOCAL, 0.05 + nbytes / 250e3, {} if after is None else {after: -calls[after]["lat"]})
+
+    def inside(q, sem, pairs):
+        def view(r):
+            return ap(r).bitcast(dt.uint8) if SCRATCH[r[0]][2] == MX else ap(r)
+        dmas(q, sem, [(view(o), view(i), [i] + more, [o]) for o, i, more in pairs],
+             sum((o[5] - o[4]) * size(o) * SIZE[SCRATCH[o[0]][2]] for o, i, more in pairs))
 
     def regs(a):
         return [a[0], a[1]] if len(a) == 2 else [a]
@@ -452,7 +401,7 @@ def rank_program(g, core, T, topo):
         if len(ins[0]) == 2:
             return (0.065 if scalar else 0.05) + 1.5 * CYC * size(o)
         narrow = not scalar and all(SIZE[SCRATCH[r[0]][2]] == 2 for r in (o,) + ins)
-        return CYC * max(64, size(o) * ((TWICE if narrow else 2) if twice else 0.5 if narrow else 1))
+        return CYC * max(64, size(o) * ((1.5 if narrow else 2) if twice else 0.5 if narrow else 1))
 
     def val(s):
         return ap(s) if isinstance(s, tuple) else s
@@ -491,27 +440,28 @@ def rank_program(g, core, T, topo):
     def tt(o, a, b, alu):
         op({"V": (plain(o, a, b, twice=a[0] != "ps"), lambda: g.vector.tensor_tensor(ap(o), src(a), ap(b), alu))}, regs(a) + [b], [o])
 
+    def memset(o, c):
+        op({"V": (plain(o, o), lambda: g.vector.memset(ap(o), c))}, [], [o])
+
+    def zeros(k):
+        return R("et", 0, 4 * k, 4)
+
     def fill(o, c):
-        if SCRATCH[o[0]][2] in (F32, BF) and o[0] != "et":
-            for lo in range(0, size(o), 256):
-                part = R(o[0], o[1] + lo * o[3], min(o[2], o[1] + (lo + 256) * o[3]), o[3])
-                op({"S": s_act(part, zeros(size(part)), ACT.Identity, None, c), "V": (plain(part, part), lambda k=part: g.vector.memset(ap(k), c))},
-                   [zeros(size(part))], [part])
-        else:
-            op({"V": (plain(o, o), lambda: g.vector.memset(ap(o), c))}, [], [o])
+        op({"S": s_act(o, zeros(size(o)), ACT.Identity, None, c), "V": (plain(o, o), lambda: g.vector.memset(ap(o), c))}, [zeros(size(o))], [o])
 
     def turn(o, a):
         op({"V": (plain(o, a), lambda: g.vector.transpose(ap(o), ap(a)))}, [a], [o])
 
-    def scan(o, a, b, op0, op1):
-        op({"V": (plain(o, a, b), lambda: g.vector.tensor_tensor_scan(ap(o), ap(a), ap(b), 0.0, op0, op1))}, [a, b], [o])
+    def scan(o, a, b, op0, op1, first=0.0):
+        op({"V": (plain(o, a, b), lambda: g.vector.tensor_tensor_scan(ap(o), ap(a), ap(b), first, op0, op1))}, [a, b], [o])
 
     def quant(oq, osc, a):
         op({"V": (0.012 + 0.22e-3 * size(a), lambda: g.vector.quantize_mx(ap(oq), ap(osc), ap(a)))}, [a], [oq, osc])
 
-    def pick_codes(o, w, off):
-        op({"V": (plain(o, (w, off)), lambda: g.vector.tensor_copy(ap(o).bitcast(dt.uint32), ap(w).bitcast(dt.uint32).indirect(ap(off))))},
-           [w, off], [o])
+    def pick(oq, osc, wq, ws, off):
+        op({"V": (plain(oq, (wq, off)), lambda: g.vector.tensor_copy(ap(oq).bitcast(dt.uint32), ap(wq).bitcast(dt.uint32).indirect(ap(off))))},
+           [wq, off], [oq])
+        move(osc, (ws, off))
 
     results = [0]
 
@@ -525,189 +475,168 @@ def rank_program(g, core, T, topo):
            rs, [o], bulk)
         return v
 
-    def ps(v, c0, c1):
-        return R("ps", 512 * v + c0, 512 * v + c1)
+    def ps(v, c0, c1, p0=0, p1=128):
+        return R("ps", 512 * v + c0, 512 * v + c1, 1, p0, p1)
+
+    ahead = []
 
     def iota(o, pattern, base, cm):
-        op({"G": (0.13 + 2 * CYC * size(o), lambda: g.iota(ap(o), pattern, base, cm, allow_small_or_imprecise_dtypes=True))}, [], [o])
+        k = op({"G": (0.13 + 2 * CYC * size(o), lambda: g.iota(ap(o), pattern, base, cm, allow_small_or_imprecise_dtypes=True))}, [], [o])
+        calls[k]["after"] = {j: -calls[j]["lat"] for j in ahead[-1:]}
+        ahead.append(k)
 
-    def engines(k):
+    def engines(k, d):
         each = [set(topo.engines(T.cores[k], T.cores[(k - d) % n])) for d in STEP]
-        return sorted(each[0] & each[1] & each[2])
+        return sorted(each[STEP.index(d)] if ALL else each[0] & each[1] & each[2])
 
     def send(d, sem, pieces, token=None):
         rid, pid, _ = topo.addr(T.cores[(rank - d) % n])
         sent = []
         for a, o in pieces:
-            def issue(q, a=a, o=o):
+            last = token and (a, o) == pieces[-1]
+
+            def issue(q, a=a, o=o, last=last):
                 order("G", [a], [])
                 cast = [ap(k).bitcast(dt.uint8) if SCRATCH[k[0]][2] == MX else ap(k) for k in (o, a)]
-                g.remote_dma(cast[0], cast[1], T.sem[sem], T.sem.sent, pid, rid, sum(1 << e for e in engines(rank)))
-                count["sent"] += len(engines(rank))
-                if token and (a, o) == pieces[-1]:
+                g.remote_dma(cast[0], cast[1], T.sem[sem], T.sem.sent, pid, rid, sum(1 << e for e in engines(rank, d)))
+                count["sent"] += len(engines(rank, d))
+                if last:
                     g.sem_inc(T.sem.go, 1)
                     count["go"] += 1
                     note("G", [], [token], "go", count["go"])
-            busy = ROWS + size(a) * SIZE[SCRATCH[a[0]][2]] / 1.25e3
-            sent.append(record({"G": 0.3 if any(c["busy"] for c in calls if "G" in c["ways"]) else FIRST}, issue, [a], [token] if token and (a, o) == pieces[-1] else [], REMOTE, busy,
-                               {k: -c["lat"] for k, c in enumerate(calls) if "G" in c["ways"]
-                                and (c["lat"] or token or not LATE or c["writes"][0][0] not in ("pat", "fi"))}))
+            sent.append(record({"G": 0.3 if any(calls[k]["busy"] for k in ahead) else FIRST}, issue, [a], [token] if last else [], REMOTE,
+                               ROWS + size(a) * SIZE[SCRATCH[a[0]][2]] / 1.25e3, {k: -calls[k]["lat"] for k in ahead[-1:]}))
+            ahead.append(sent[-1])
 
         def arrive(q):
-            count[sem] = len(pieces) * len(engines((rank + d) % n))
+            count[sem] = len(pieces) * len(engines((rank + d) % n, d))
             note("G", [], [o for a, o in pieces], sem, count[sem])
             clock[(sem, count[sem])] = {}
         record({"A": 0.0}, arrive, [], [o for a, o in pieces], after={k: 0.0 for k in sent})
 
-    M, P112, P7, P120, M3, M2, P14, P31, P1, X, P96 = [R("pf", k, k + 1) for k in range(len(BITS))]
+    U2, WHI, WLO = ("u2q", "u2s", 0, 128), ("cq", "cs", 0, 128), ("cq", "cs", 128, 128)
+    LX8, LUM, LNB, LKI, LP, LU2, LOE, LA, LX7, LF = [R("ls", a, b) for a, b in (
+        (0, 8), (16, 25), (26, 27), (28, 29), (30, 31), (32, 33), (38, 40), (40, 56), (56, 60), (60, 64))]
+    F = {f[0]: R("ft", 32 * k, 32 * k + 1) for k, f in enumerate(FIELDS)}
+    F.update({f[0]: R("pf", k, k + 1) for k, f in enumerate(BITS)})
 
-    def col(k):
-        return R("col", k, k + 1)
+    def fields(lo, hi):
+        for k in range(lo, hi):
+            name, pieces, cm = FIELDS[k]
+            many = 32 // len(pieces)
+            for j, (pattern, base) in enumerate(pieces):
+                iota(R("fi", 32 * k + many * j, 32 * k + many * j + many), pattern, base, cm)
+        turn(R("ft", 32 * lo, 32 * hi), R("fi", 32 * lo, 32 * hi))
 
-    def zeros(k):
-        return R("et", 0, 4 * k, 4)
-
-    U2, UF = ("u2q", "u2s", 0, 128), ("uaq", "uas", 128, 128)
-    WHI, WLO, WLOSS = ("cq", "cs", 0, 128), ("cq", "cs", 128, 128), [("cq", "cs", 256, 128), ("cq", "cs", 384, 128)]
-    LX8, LKI, LU2, LU1, LNB, LOE, LA, LX7, LF = [R("ls", a, b) for a, b in (
-        (0, 8), (26, 27), (28, 29), (30, 31), (32, 33), (38, 40), (40, 56), (56, 60), (60, 64))]
-
-    dmas("S", "du", [(T.uin[:], T.u[:], [], [R("uin")])], 1 << 17)
-    for k in range(2):
-        dmas("Y", "dx%d" % k, [(T.xin[:, 512 * k:512 * k + 512], T.x[:, 512 * k:512 * k + 512], [], [R("xin", 512 * k, 512 * k + 512)])],
-             1 << 17)
-    iota(R("pi", 15, 16), [[0, 1]], 0, 1)
+    load = None
+    for sem, to, piece in (("dx0", R("xin", 0, 512), T.x[:, 0:512]), ("du", R("uin"), T.u[:]), ("dx1", R("xin", 512, 1024), T.x[:, 512:1024])):
+        load = dmas("Y", sem, [(ap(to), piece, [], [to])], 1 << 17, load)
+    memset(R("ni"), 0)
+    memset(R("et"), 0.0)
+    memset(R("l2", 0, 8), 2)
+    memset(R("sj"), 0)
+    load = dmas("Y", "dn", [(ap(R("ni", 0, 16, 1, c, 128, 8)), T.nb[c, :], [], [R("ni")]) for c in range(4)]
+                + [(ap(R("ni", 16, 32, 1, c, 128, 8)), T.e[c, :], [], [R("ni")]) for c in range(4)], 1 << 14, load)
     iota(R("jm"), [[1, 128]], 0, -1)
+    iota(R("pi", 7, 8), [[0, 1]], 0, 1)
     iota(R("rows", 0, 16), [[16, 16]], 0, 0)
     iota(R("cn"), [[16, 4], [0, 2], [1, 16]], 0, 0)
-    iota(R("ch"), [[0, 8], [8, 8], [0, 2]], 0, 0)
-    iota(R("rows", 16, 32), [[0, 4], [16, 4]], 1792, 0)
-    iota(R("pat"), [[0, 16], [-256, 8]], 1536, 0)
-    iota(R("fi", 0, 32), [[0, 8], [8, 4]], 7, 1)
+    fields(*GROUPS[0])
+    for k, (name, shift, mask) in enumerate(BITS):
+        ts(R("pi", k, k + 1), R("pi", 7, 8), shift, ALU.arith_shift_right, mask, ALU.bitwise_and)
+    copy(R("pf", 0, 4), R("pi", 0, 4))
+    copy(R("pf", 4, 6), R("pi", 4, 6))
+    fill(R("six"), 16.0)
     for k in range(2):
-        iota(R("fi", 32 + 16 * k, 48 + 16 * k), [[1, 2], [2, 2], [8, 4]], 0, 0)
-        iota(R("fi", 64 + 16 * k, 80 + 16 * k), [[1, 2], [4, 4], [8, 2]], 0, 0)
-    turn(R("ft"), R("fi"))
-    for k, (shift, mask) in enumerate(BITS):
-        ts(R("pi", k, k + 1), R("pi", 15, 16), shift, ALU.arith_shift_right, mask, ALU.bitwise_and)
-    copy(R("pf", 0, 5), R("pi", 0, 5))
-    copy(R("pf", 5, 11), R("pi", 5, 11))
-    fill(R("et"), 0.0)
-    fill(R("ni"), 0)
-    fill(R("l2"), 2)
-    dmas("Y", "dn", [(ap(R("ni", 0, 16, 1, c, 128, 8)), T.nb[c, :], [], [R("ni")]) for c in range(4)]
-         + [(ap(R("ni", 16, 32, 1, c, 128, 8)), T.e[c, :], [], [R("ni")]) for c in range(4)], 1 << 14)
-    for k in range(2):
-        fill(R("ff", 512 * k, 512 * k + 512), 0.0)
+        fill(R("oh", 256 * k, 256 * k + 256), 0.0)
         ts(R("et", 3 + 512 * k, 512 + 512 * k, 4), R("jm"), 0.0, ALU.is_equal)
-    fill(R("oh"), 0.0)
     ts(R("tri"), R("jm"), 0.0, ALU.is_lt, 2.0 ** -100, ALU.mult)
     for b in range(4):
         quant(R("eq", 256 * b, 256 * b + 240), R("es", 256 * b, 256 * b + 240), R("et", 3 - b, 963 - b))
-    lin(col(2), P7, 8.0)
-    lin(col(6), P112, None, 128.0)
-    lin(R("wt", 0, 512, 2), zeros(256), None, P112)
-    lin(R("wt", 1, 512, 2), zeros(256), None, col(6))
-    lin(R("wt", 512, 1024, 2), zeros(256), None, M)
-    lin(R("wt", 513, 1024, 2), zeros(256), None, M)
-    fill(R("wt", 1024, 1536), 0.0)
-    fill(R("wt", 1536, 1540), 0.0)
-    fill(R("sj"), 0)
-    fill(R("d0"), 1.0)
-    fill(R("d0", 0, 128, 8), 0.0)
-    fill(R("d1"), 0.0)
-    fill(R("dc"), 0.0)
-    tt(col(3), col(2), P120, ALU.is_gt)
-    quant(R("uq"), R("us"), R("uin"))
-    ts(R("wa"), R("ch"), P120, ALU.is_equal, col(3), ALU.mult)
-    ts(R("wb"), R("ch"), col(2), ALU.is_equal, col(3), ALU.mult)
-    pick_codes(R("u2q"), R("uq"), R("l2"))
-    move(R("u2s"), (R("us"), R("l2")))
-    tt(R("wt", 1026, 1538, 4), R("wa"), R("wb"), ALU.subtract)
+    lin(R("wt", 0, 512, 2), zeros(256), None, F["p112"])
+    lin(R("up", 0, 1), F["p112"], None, 128.0)
+    lin(R("wt", 1, 512, 2), zeros(256), None, R("up", 0, 1))
+    lin(R("wt", 512, 1024, 2), zeros(256), None, F["m"])
+    lin(R("wt", 513, 1024, 2), zeros(256), None, F["m"])
     quant(R("cq", 0, 256), R("cs", 0, 256), R("wt", 0, 1024))
-    quant(R("cq", 256, 384), R("cs", 256, 384), R("wt", 1026, 1538))
-    if not HALVES:
-        quant(R("cq", 384, 512), R("cs", 384, 512), R("wt", 1024, 1536))
-    def listed(lo, hi, a, scale, bias, step=1):
-        lin(R("lf", lo, hi, step), a, scale, bias)
-
-    fill(R("lf"), 0.0)
-    lin(col(0), P7, 16.0, 1.0)
-    lin(col(1), P14, 8.0)
-    lin(col(7), M3, 16.0, 1.0)
-    lin(col(11), X, None, P14)
-    lin(col(8), P1, 16.0, M2)
-    lin(col(12), M2, 8.0, 7.0)
-    lin(col(13), X, 8.0, 7.0)
-    for k in range(2):
-        listed(40 + k, 56, R("rows", 0, 8), 2.0, P31, 2)
-        listed(38 + k, 39 + k, R("ft", 64, 65), 1.0, 2.0 * k)
-    listed(8, 12, R("rows", 0, 4), 2.0, col(7))
-    listed(12, 16, zeros(4), 1.0, col(0))
-    listed(16, 25, zeros(9), 1.0, col(1))
-    listed(26, 27, R("ft", 0, 1), 1.0, 0.0)
-    listed(28, 29, col(11), 1.0, 0.0)
-    listed(30, 31, P7, 16.0, col(13))
-    listed(32, 33, R("ft", 32, 33), 1.0, 0.0)
-    listed(0, 8, R("rows", 0, 8), 0.125, M3)
-    listed(56, 60, R("rows", 0, 4), 2.0, col(12))
-    listed(60, 64, R("rows", 0, 4), 0.25, col(8))
-    for lo, hi in ((8, 16), (16, 26), (26, 64), (0, 8)):
-        copy(R("ls", lo, hi), R("lf", lo, hi))
-    lin(col(4), P14, -0.5)
-    lin(col(5), P14, 0.5)
-    lin(col(9), M, -1.0, -1792.0)
-    lin(col(10), P96, 2.0, M)
-    fill(R("da"), 256.0)
-    lin(R("da", 7, 128, 8), R("rows", 0, 16), -1.0, col(9))
     fill(R("ad"), -0.125)
-    lin(R("ib"), R("rows", 16, 32), None, col(10))
+    fill(R("da"), 256.0)
+    lin(R("up", 2, 3), F["m"], -1.0, -1792.0)
+    lin(R("da", 7, 128, 8), R("rows", 0, 16), -1.0, R("up", 2, 3))
+
+    def listed(to, a, scale, field):
+        ts(to, a, scale, ALU.mult, F[field], ALU.add)
+
+    ts(LUM, R("six", 0, 9), F["h"], ALU.mult, F["p1"], ALU.add)
+    quant(R("uq"), R("us"), R("uin"))
+    pick(R("u2q"), R("u2s"), R("uq"), R("us"), R("l2", 0, 8))
+    fill(R("cap"), BIG)
+    fill(R("cap", 7, 64, 8), -BIG)
+    fill(R("ma", 0, 144, 72), -BIG)
+    fill(R("me", 0, 144, 72), -BIG)
+    memset(R("cand"), 0)
     copy(R("n0"), R("ni"))
-    for lo, hi in ((8, 16), (16, 25)):
-        pick_codes(R("uaq", 16 * lo, 16 * hi), R("uq"), R("ls", lo, hi))
-        move(R("uas", 16 * lo, 16 * hi), (R("us"), R("ls", lo, hi)))
     for k in range(4):
         move(R("nf", 16 * k, 16 * k + 16), R("n0", 16 * (k // 2), 16 * (k // 2) + 16))
     turn(R("nt"), R("nf"))
+
+    pick(R("uaq"), R("uas"), R("uq"), R("us"), LUM)
+    for k in range(2):
+        listed(R("ls", 40 + k, 56, 2), R("rows", 0, 8), 2.0, "p31")
+    listed(LX8, R("rows", 0, 8), 0.125, "m3")
+    copy(R("ls", 26, 32, 2), R("ft", 0, 96, 32))
     copy(R("n16"), (R("nt", 0, 32), LNB))
     ts(R("tmp", 0, 16), (R("nt", 32, 64), LNB), 256.0, ALU.mult)
     ts(R("tmp", 16, 32), R("n16"), float(C), ALU.is_ge, float(FAR - C), ALU.mult)
     tt(R("tmp", 32, 48), R("tmp", 0, 16), R("n16"), ALU.add)
-    copy(R("lk"), (R("n16"), LU2))
     tt(R("cand", 0, 64, 4), R("tmp", 32, 48), R("tmp", 16, 32), ALU.add)
+    ts(R("tmp", 48, 64), R("n16"), float(C), ALU.is_ge, -float(C + H), ALU.mult)
+    tt(R("tmp", 64, 80), R("tmp", 48, 64), R("n16"), ALU.add)
 
-    def side(b, h):
-        if b == "m":
-            return ("uaq", "uas", 256 + 2 * h, 128)
-        return ("eq", "es", 256 * b + 16 * h, 128)
+    def while_the_columns_leave():
+        iota(R("rows", 16, 24), [[0, 4], [32, 2]], 1792, 0)
+        fields(*GROUPS[1])
+        iota(R("pat"), [[0, 16], [-256, 8]], 1536, 0)
+        for k in range(2):
+            lin(R("ib", 8 * k, 8 * k + 8), R("rows", 16, 24), None, F["ib%d" % k])
+        copy(LU2, F["lu2"])
+        ts(R("lk"), (R("tmp", 64, 80), LU2), float(H), ALU.add)
+
+    def while_the_list_leaves():
+        fields(*GROUPS[2])
+        for name, c in (("dc", 0), ("d1", 0), ("d0", 1)):
+            iota(R(name), [[0, size(R(name))]], c, 0)
+        iota(R("d0", 0, 128, 8), [[0, 16]], 0, 0)
+        listed(LX7, R("rows", 0, 4), 1.0, "lx7")
+        listed(LF, R("rows", 0, 4), 0.25, "lfl")
+        listed(LOE, R("rows", 0, 2), 0.125, "loe")
 
     def unpack(b, h, x, lo, k):
         line[0] = "unpack"
-        v = mm(side(b, h), x, bulk=True)
+        v = mm(("uaq", "uas", 2 * h, 128) if b == "m" else ("eq", "es", 256 * b + 16 * h, 128), x, bulk=True)
         line[0] = None
         if b == "m":
-            move(R("mk", lo + C * h, lo + C * h + k), ps(v, 0, k))
+            move(R("mk", H + lo + C * h, H + lo + C * h + k), ps(v, 0, k))
         else:
             move(R("win", PL * b + lo + C * h, PL * b + lo + C * h + k), ps(v, 0, k), 0.5)
 
-    def frames(x, k, out):
-        many, two = size(out), size(out) // 128 or 1
-        a = mm(UF, x)
-        f2, ff = R("f2", C * k, C * k + many, 1, 0, 64), R("ff", 512 * k, 512 * k + 4 * many // two, 4 // two, 0, 64)
-        move(f2, R("ps", 512 * a, 512 * a + many, 1, 0, 64))
-        tt(ff, R("ps", 512 * a, 512 * a + many, 1, 64, 128), f2, ALU.is_gt)
-        quant(R("ffq", 128 * k, 128 * k + 128), R("ffs", 128 * k, 128 * k + 128), R("ff", 512 * k, 512 * k + 512))
-        for j in range(two):
-            v = ps(mm(WLOSS[j], ("ffq", "ffs", 128 * k, 128)), 0, many // two)
-            o = R(out[0], out[1] + j, out[2], two)
-            op({"V": v_ts(o, v, col(4), ALU.not_equal), "S": s_act(o, v, ACT.Sign, None, col(5))}, [v, col(4), col(5)], [o])
+    def products(x, out):
+        move(out, ps(mm(("uaq", "uas", 0, 128), x), 0, size(out)))
 
-    first = [(b, h) for b in range(4) for h in (1, 2, 3)] + [(b, 0) for b in range(4)]
-    more = [(b, h) for h in range(4, NPE) for b in range(4)]
+    def framed(table, off, name, steps, out):
+        for k in range(2):
+            lo, hi, half = 128 * k, 128 * k + 128, (64 * k, 64 * k + 64)
+            for j in ((0, 4) if (name, k) == ("e", 0) else (0,)):
+                many = 4 if (name, k) == ("e", 0) else 8
+                move(R("g" + name, lo + 16 * j, lo + 16 * (j + many)), (table, R(off[0], off[1] + 8 * k + j, off[1] + 8 * k + j + many)))
+            turn(R("t" + name, lo, hi), R("g" + name, lo, hi))
+            scan(R("m" + name, 72 * k + 1, 72 * k + 65), R("t" + name, lo + 1, hi, 2), R("cap"), ALU.max, ALU.min, -BIG)
+            tt(R("k" + name, *half), R("t" + name, lo + 1, hi, 2), R("m" + name, 72 * k, 72 * k + 64), ALU.is_le)
+            scan(R(out, *half), R("k" + name, *half), R(steps, *half), ALU.mult, ALU.add)
 
     for r, d in enumerate(STEP):
         qn, sn, lq, lsc, lb, ll = [k + str(r) for k in ("q", "s", "lq", "lsc", "lb", "ll")]
-        own, gone = (qn, sn, 0, C), ("gone%d" % r, 0, 1, 1, 0, 128, 1)
+        own, left, gone = (qn, sn, 0, C), ("left%d" % r, 0, 1, 1, 0, 128, 1), ("gone%d" % r, 0, 1, 1, 0, 128, 1)
         came = ("bq", "bs", 128 - H * r, 128)
         border = [R(k, 128 - H * r, 128 - H * r + H) for k in ("bq", "bs")]
 
@@ -719,13 +648,17 @@ def rank_program(g, core, T, topo):
                 quant(hq, hs, R("xin", 512 * k, 512 * k + 512))
             if WHOLE[r]:
                 send(d, "arr%s%d" % ("ab"[k], r), [(hq, R(lq, 128 * k, 128 * k + 128))]
-                     + ([(hs, R(lsc, 128 * k, 128 * k + 128))] if FOUR else [(R(sn), R(lsc))] if k else []))
+                     + ([(hs, R(lsc, 128 * k, 128 * k + 128))] if FOUR[r] else [(R(sn), R(lsc))] if k else []), left if k and SOON[r] + TWO[r] else None)
             down.append(ps(mm(half, U2), 0, 1))
             along.append(ps(mm(U2, half), 0, 128))
-        act(R("sc", 0, 1), down[0])
-        act(R("dd", 0, 128), along[0], ACT.Identity, -1.0, R("sc", 0, 1))
+        if r or not BOTH:
+            act(R("up", 4, 5), down[0])
+            down[0] = R("up", 4, 5)
+            act(R("dd", 0, 128), along[0], ACT.Identity, -1.0, down[0])
+        else:
+            ts(R("dd", 0, 128), along[0], down[0], ALU.subtract, -1.0, ALU.mult)
         ts(R("dd", 128, 256), along[1], down[1], ALU.subtract, -1.0, ALU.mult)
-        ts(R("fo", 0, 128), along[1], R("sc", 0, 1), ALU.is_gt)
+        ts(R("fo", 0, 128), along[1], down[0], ALU.is_gt)
         ts(R("fo", 128, 256), along[0], down[1], ALU.is_ge)
         for k in range(2):
             lo, hi = 128 * k, 128 * k + 128
@@ -737,43 +670,42 @@ def rank_program(g, core, T, topo):
         mm(WLO, ("ohq", "ohs", 0, 128), into=v)
         turn(R("lt"), ps(v, 0, 128))
         copy(R(lb), R("lt", 0, 128, 32))
+        if r == 0:
+            while_the_columns_leave()
         if WHOLE[r]:
             send(d, "arrl%d" % r, [(R(lb), R(ll))], gone)
         else:
-            pick_codes(R(lq, 0, H), R(qn), R(lb))
-            move(R(lsc, 0, H), (R(sn), R(lb)))
+            pick(R(lq, 0, H), R(lsc, 0, H), R(qn), R(sn), R(lb))
             send(d, "arrl%d" % r, [(R(lq, 0, H), border[0]), (R(lsc, 0, H), border[1])], gone)
+        if r == 0:
+            while_the_list_leaves()
 
-        todo = first + more + [("m", h) for h in range(9)]
-        for j, (b, h) in enumerate(todo):
+        for j, (b, h) in enumerate([(b, h) for b in range(4) for h in range(2 if b < TWO[r] else 4)] + [("m", h) for h in range(1, 9)]):
             if r and j < EARLY:
                 for k in range(2):
                     unpack(b, h, (qn, sn, 128 * k, 128), 128 * k, 128)
             else:
                 unpack(b, h, own, 0, C)
+        for b in range(TWO[r]):
+            inside("Y", "sv%d%d" % (r, b), [(R("win", PL * b + 512, PL * b + 1024, 1, p0, p1),
+                                            R("win", PL * b, PL * b + 512, 1, (p0 + 32) % 128, (p1 + 31) % 128 + 1), [left])
+                                           for p0, p1 in ((0, 96), (96, 128))])
         for b in range(4):
-            pairs = [(R("win", PL * b + C * NPE, PL * b + 2048, 1, 64 * k, 64 * k + 64),
-                      R("win", PL * b + C * (NPE - 4), PL * b + 1024, 1, 64 - 64 * k, 128 - 64 * k)) for k in range(2)]
-            dmas("Y", "sw%d%d" % (r, b), [(ap(o), ap(i), [i] + ([gone] if b >= NSR[r] else []), [o]) for (o, i) in pairs],
-                 (8 - NPE) << 16)
+            inside("Y", "sw%d%d" % (r, b), [(R("win", PL * b + 1024, PL * b + 2048, 1, 64 * k, 64 * k + 64),
+                                            R("win", PL * b, PL * b + 1024, 1, 64 - 64 * k, 128 - 64 * k), [left if b < SOON[r] else gone])
+                                           for k in range(2)])
         if r == 0:
-            dmas("Y", "db", [(T.bq[:, 192:256].bitcast(dt.uint8), T.q0[:, 0:H].bitcast(dt.uint8), [R("q0", 0, H)], [R("bq", 192, 256)]),
-                             (T.bs[:, 192:256], T.s0[:, 0:H], [R("s0", 0, H)], [R("bs", 192, 256)])], 5 << 13)
-            dmas("Y", "dw", [(T.wq[:].bitcast(dt.uint8), T.wc[:], [gone, R("win", 3 * PL + 2047, 3 * PL + 2048)], [R("wq")]),
+            inside("Y", "db", [(R("bq", 192, 256), R("q0", 0, H), []), (R("bs", 192, 256), R("s0", 0, H), [])])
+            dmas("Y", "dw", [(T.wq[:].bitcast(dt.uint8), T.wc[:], [R("win", 3 * PL + 2047, 3 * PL + 2048)], [R("wq")]),
                              (T.wsc[:], T.ws[:], [], [R("wsc")])], 5 << 16)
         if r == 1:
             dmas("Y", "dv", [(T.vin[:], T.v[:], [R("win", 3 * PL + 2047, 3 * PL + 2048)], [R("vin")])], 1 << 17)
             quant(R("vq"), R("vs"), R("vin"))
-        if HALVES:
-            for k in range(2):
-                frames((qn, sn, 128 * k, 128), k, R("kl", 128 * k, 128 * k + 128))
-        else:
-            frames(own, 0, R("kl", 0, C))
-        move(R("ga"), (R("kl", 0, C), LA))
-        turn(R("ta"), R("ga"))
-        scan(R("sa"), R("ta", 0, 256, 2), R("da"), ALU.mult, ALU.add)
+        for k in range(2):
+            products((qn, sn, 128 * k, 128), R("mk", H + 128 * k, H + 128 * k + 128))
+        framed(R("mk", H, H + C), LA, "a", "da", "sa")
         ts(R("offa"), R("sa", 7, 128, 8), -1.0, ALU.mult)
-        tt(R("pre"), R("cand", 0, 64, 4), R("ib"), ALU.add)
+        tt(R("pre"), (R("cand"), LP), R("ib"), ALU.add)
         tt(R("wi"), (R("sa"), LKI), R("pre"), ALU.add)
         ts(R("wr"), R("wi"), MASK, ALU.bitwise_and)
         ts(R("wy"), R("wi"), 1792, ALU.bitwise_and)
@@ -781,32 +713,23 @@ def rank_program(g, core, T, topo):
         tt(R("wf"), (R("wy"), LX8), R("pat"), ALU.is_equal)
         tt(R("dk"), R("wf"), R("ad"), ALU.add)
         for b in range(4):
-            for lo in range(0, C, WIDE):
-                move(R("ah", C * b + lo, C * b + lo + WIDE), (R("win", PL * b, PL * b + 2048), R("offa", lo // 16, (lo + WIDE) // 16)))
-            move(R("af", 256 * b, 256 * b + 256), R("ah", 256 * b, 256 * b + 256), 2.0)
+            move(R("ah", C * b, C * b + C), (R("win", PL * b, PL * b + 2048), R("offa")))
+            move(R("af", C * b, C * b + C), R("ah", C * b, C * b + C), 2.0)
 
         if WHOLE[r]:
-            if HALVES:
-                for k in range(2):
-                    frames((lq, lsc, 128 * k, 128), k, R("kr", 128 * k, 128 * k + 128))
-            else:
-                frames((lq, lsc, 0, C), 1, R("kr"))
-            copy(R("kl", C, C + H), (R("kr"), R(ll)))
-            pick_codes(border[0], R(lq), R(ll))
-            move(border[1], (R(lsc), R(ll)))
+            for k in range(2):
+                products((lq, lsc, 128 * k, 128), R("pr", 128 * k, 128 * k + 128))
+            move(R("mk", 0, H), (R("pr"), R(ll)))
+            pick(border[0], border[1], R(lq), R(lsc), R(ll))
         else:
-            frames(came, 1, R("kl", C, C + H))
+            products(came, R("mk", 0, H))
         for b in ("m", 0, 1, 2, 3):
             for h in range(9 if b == "m" else 8):
                 unpack(b, h, came, FAR, H)
 
+        framed(R("mk", 0, H + C), R("lk"), "e", "dk", "sk")
         for k in range(2):
-            lo, hi = 128 * k, 128 * k + 128
-            move(R("gk", lo, hi), (R("kl"), R("lk", 8 * k, 8 * k + 8)))
-            turn(R("tk", lo, hi), R("gk", lo, hi))
-            scan(R("sk", lo // 2, hi // 2), R("tk", lo, hi, 2), R("dk", lo // 2, hi // 2), ALU.mult, ALU.add)
-        for k in range(2):
-            ts(R("offm", k, 32, 2), (R("sk"), LU1), 2048.0, ALU.mult, 256.0 * k, ALU.add)
+            ts(R("offm", k, 16, 2), R("sk", 7, 64, 8), 2048.0, ALU.mult, 256.0 * k, ALU.add)
         ts(R("cand"), (R("sk"), LX7), 2048.0, ALU.mult)
         c0, c2, c1, c3 = [R("cand", 16 * k, 16 * k + 16) for k in range(4)]
         tt(R("dc", 0, 64, 4), c0, c1, ALU.subtract)
@@ -816,7 +739,7 @@ def rank_program(g, core, T, topo):
         copy(R("d1", 4, 128, 8), c0)
         for k in range(2):
             lo, hi = 128 * k, 128 * k + 128
-            move(R("gm", lo, hi), (R("mk"), R("offm", 8 * k, 8 * k + 8)))
+            move(R("gm", lo, hi), (R("mk", H), R("offm", 8 * k, 8 * k + 8)))
             turn(R("tm", lo, hi), R("gm", lo, hi))
         even, odd = R("tm", 0, 128, 4), R("tm", 128, 256, 4)
         tt(R("e2"), odd, even, ALU.max)
@@ -824,6 +747,7 @@ def rank_program(g, core, T, topo):
         tt(R("d0", 4, 128, 8), R("e2", 16, 32), R("e2", 0, 16), ALU.is_gt)
         tt(R("d1", 1, 128, 2), (R("fl"), LF), R("dc"), ALU.mult)
         scan(R("e5"), R("d0"), R("d1"), ALU.mult, ALU.add)
+        line[0] = "tail"
         for a in range(4):
             for k in range(4):
                 i = R("e5", 8 * k + 5, 128, 32, 32 * a, 32 * a + 32)
@@ -839,9 +763,12 @@ def rank_program(g, core, T, topo):
                 if 4 * k + b >= FUSED:
                     act(R("bh", lo, lo + 128), parts)
                     parts = R("bh", lo, lo + 128)
-                tt(R("z", 512 * k + b, 512 * k + 512, 4), parts, R("ah", lo, lo + 128), ALU.add)
                 if (k, b) == (0, 0):
+                    for j in range(2):
+                        tt(R("z", 256 * j, 256 * j + 256, 4), (parts[0], R("offb", 4 * j, 4 * j + 4)), R("ah", 64 * j, 64 * j + 64), ALU.add)
                     copy(R("offb", 8, 16), R("ob", 8, 16))
+                else:
+                    tt(R("z", 512 * k + b, 512 * k + 512, 4), parts, R("ah", lo, lo + 128), ALU.add)
             quant(R("zq", 128 * k, 128 * k + 128), R("zs", 128 * k, 128 * k + 128), R("z", 512 * k, 512 * k + 512))
             for b in range(4):
                 lo = 256 * b + 128 * k

@@ -3,28 +3,37 @@ from concourse.mybir import dt, AluOpType as ALU, ActivationFunctionType as ACT
 F32, BF, I32, U16, MX, U8 = "float32", "bfloat16", "int32", "uint16", "float8_e4m3fn_x4", "uint8"
 STEP = [1, 2, 4]
 C, H = 256, 64
-FAR, MASK, PL = 4096, 4096 + 2047, 6144
+FAR, MASK = 4096, 4096 + 2047
+NEAR, PL = 2048, 2560
 WHOLE = [True, True, False]
 FOUR = [False, True, True]
 BOTH = False
 ALL = True
-TWO = [0, 2, 2]
+MADE = [[2, 2, 4, 4], [4, 4, 4, 4], [4, 4, 4, 4]]
+TELL = 0
+FLAGS = [True, True, True]
+LATE = False
+MOVED = [[0, 0, 0, 4], [0, 0, 0, 4], [0, 0, 0, 4]]
+BORDER = ["YYYP", "YYGP", "YYYP"]
+MARKS, FIRSTLY = [8, 2, 8], "lll"
 BIG = 1e29
-POLISH, WARM = 7000, 0.03
-URGENT = 0.2
-SPINE = ("dd", "fo", "fd", "rk", "oh", "ohq", "lt", "lb0", "lb1", "lb2", "lq2", "lsc2", "ge", "te", "me", "ke", "sk", "offm", "gm", "tm", "e2", "fl", "d0", "d1", "e5",
+POLISH, WARM = 24000, 0.03
+URGENT = 0.3
+SPINE = ("dd", "fo", "fd", "rk", "oh", "ohq", "lt", "lb0", "lb1", "lb2", "lq2", "lsc2", "gb", "tb", "kt", "ge", "te", "me", "ke", "sk", "offm", "gm", "tm", "e2", "fl", "d0", "d1", "e5",
          "offb", "ob", "bh", "z", "zq", "rl", "xn", "q1", "q2", "q3", "bq", "bs")
-SOON = [0, 0, 0]
+SOON = [0, 0, 1]
 EARLY = 6
 FUSED = 4
 BULK = 4
 CYC, PECYC, HOP, LOCAL, REMOTE, ROWS, FIRST = 0.83e-3, 0.6e-3, 0.21, 1.1, 0.9, 0.3, 1.5
-PASSES, SLACK, MARGIN, SHAKE = 30, 0.04, 0.05, 0.15
-MACHINES = [(0.21, 1.0, 1.0, 1.0), (0.23, 1.0, 0.7, 0.8), (0.18, 1.1, 1.35, 1.0), (0.2, 1.35, 1.2, 1.4), (0.24, 1.05, 1.0, 1.5)]
+WRITE, PORT = 160e3, [300e3, 300e3, 110e3]
+AGAIN = 0
+PASSES, SLACK, MARGIN, SHAKE = 12, 0.04, 0.05, 0.15
+MACHINES = [(0.21, 1.0, 1.0, 1.0), (0.23, 1.12, 0.7, 0.8), (0.18, 1.25, 1.35, 1.0), (0.2, 1.45, 1.2, 1.2), (0.24, 1.3, 1.0, 1.4)]
 FIELDS = [
     ("lnb", [([[1, 2], [2, 2], [8, 4]], 0)] * 2, 0),
     ("lki", [([[8, 2], [0, 4], [16, 2]], 7), ([[-8, 2], [0, 4], [16, 2]], 15)], 1),
-    ("lp", [([[4, 2], [8, 8]], 0), ([[-4, 2], [8, 8]], 4)], 0),
+    ("lp", [([[8, 2], [16, 8]], 0), ([[-8, 2], [16, 8]], 8)], 0),
     ("ib0", [([[16, 2], [1, 16]], 0)], 2), ("ib1", [([[-16, 2], [1, 16]], 16)], 2),
     ("lu2", [([[4, 4], [1, 2]], 0), ([[4, 4], [-1, 2]], 1), ([[4, 4], [1, 2]], 2), ([[4, 4], [-1, 2]], 3)], 0),
     ("lx7", [([[8, 2], [64, 2], [0, 4]], 7), ([[8, 2], [-64, 2], [0, 4]], 71)], 0),
@@ -48,20 +57,21 @@ SCRATCH = {
     "fi": _s(32 * len(FIELDS), F32), "ft": _s(32 * len(FIELDS), F32), "rows": _s(32, F32), "up": _s(8, F32),
     "pi": _s(8, I32), "pf": _s(8, F32), "six": _s(16, F32),
     "l2": _s(16, U16), "ls": _s(64, U16), "lk": _s(16, U16),
-    "ni": _s(32, I32), "n0": _s(32, F32), "nf": _s(64, F32), "nt": _s(64, F32), "n16": _s(16, F32), "tmp": _s(80, F32),
+    "ni": _s(32, I32), "n0": _s(32, F32), "nf": _s(64, F32), "nt": _s(64, F32), "n16": _s(16, F32), "tmp": _s(128, F32),
     "dd": _s(256, BF), "fo": _s(256, BF), "fd": _s(256, BF), "rk": _s(256, BF), "oh": _s(512, BF), "ohq": _s(128, MX), "ohs": _s(128, U8),
     "lt": _s(128, F32),
     "sa": _s(128, F32), "pr": _s(256, F32), "cap": _s(64, F32),
-    "ga": _s(256, F32), "ta": _s(256, F32), "ma": _s(144, F32), "ka": _s(128, F32),
+    "ta": _s(256, F32), "ma": _s(144, F32),
     "ge": _s(256, F32), "te": _s(256, F32), "me": _s(144, F32), "ke": _s(128, F32),
-    "sk": _s(128, F32),
+    "sk": _s(128, F32), "kp": _s(512, BF), "kt": _s(3 * H + 2 * C, BF),
+    "fuq": _s(16, MX), "fus": _s(32, U8), "fq": _s(128, MX), "fs": _s(128, U8), "db": _s(128, F32), "gb": _s(512, BF), "tb": _s(512, BF),
     "offa": _s(16, U16), "pre": _s(16, F32), "wi": _s(16, I32), "wr": _s(16, I32), "wy": _s(16, I32), "ib": _s(16, F32),
-    "da": _s(128, F32), "ad": _s(128, F32), "pat": _s(128, F32), "wf": _s(128, F32), "dk": _s(128, F32),
+    "da": _s(128, F32), "pat": _s(128, F32), "wf": _s(128, F32), "dk": _s(128, F32),
     "offm": _s(32, U16), "sj": _s(32, I32),
-    "cand": _s(64, I32), "gm": _s(256, F32), "tm": _s(256, F32),
+    "cand": _s(16, I32), "cv": _s(128, F32), "gm": _s(256, F32), "tm": _s(256, F32),
     "e2": _s(32, F32), "fl": _s(32, F32), "dc": _s(64, F32), "e5": _s(128, F32), "d0": _s(128, F32), "d1": _s(128, F32),
     "offb": _s(16, U16), "ob": _s(16, F32),
-    "win": _s(4 * PL, BF), "mk": _s(H + PL + C, F32),
+    "win": _s(4 * PL, BF), "mk": _s(H + FAR + 9 * C, F32), "sg": _s(128, F32), "cw": _s(128, F32),
     "bq": _s(256, MX), "bs": _s(256, U8),
     "ah": _s(1024, BF), "bh": _s(1024, BF), "af": _s(1024, BF), "z": _s(1024, BF), "zq": _s(256, MX), "zs": _s(256, U8),
     "rl": _s(1024, F32), "xn": _s(1024, BF),
@@ -73,14 +83,12 @@ for _r in range(4):
 for _r in range(3):
     SCRATCH["lq%d" % _r] = _s(256, MX)
     SCRATCH["lsc%d" % _r] = _s(256, U8)
-    SCRATCH["lb%d" % _r] = _s(4, U16)
-    if WHOLE[_r]:
-        SCRATCH["ll%d" % _r] = _s(4, U16)
+    SCRATCH["lb%d" % _r] = SCRATCH["ll%d" % _r] = _s(4 if WHOLE[_r] else 12, U16)
 SIZE = {F32: 4, BF: 2, I32: 4, U16: 2, MX: 4, U8: 1}
 
-SEMAPHORES = (["V", "S", "P", "G", "dx0", "dx1", "du", "dw", "dv", "dn", "db", "dz0", "dz1", "dz2", "sent", "go", "out", "outa", "outy", "oute"]
-              + ["%s%d%d" % (a, r, b) for r in range(3) for b in range(4) for a in ("sv", "sw")]
-              + ["%s%d" % (a, r) for r in range(3) for a in ("arra", "arrb", "arrl")])
+SEMAPHORES = (["V", "S", "P", "G", "dx0", "dx1", "du", "dw", "dv", "dn", "db", "dz0", "dz1", "dz2", "sent", "go", "arru", "out", "outa", "outy", "oute"]
+              + ["%s%d%d" % (a, r, b) for r in range(3) for b in range(4) for a in ("sv", "sw", "sb")]
+              + ["%s%d" % (a, r) for r in range(3) for a in ("arra", "arrb", "arrl", "sm")])
 
 
 def R(name, c0=0, c1=None, step=1, p0=0, p1=128, pstep=1):
@@ -202,29 +210,42 @@ def lay(calls, pred, succ, chain, forward):
     return end, seq, place
 
 
-def replay(calls, seq, place, hop, compute, tensor, dma):
+def replay(calls, seq, place, hop, compute, tensor, dma, same=0, earlier=None):
     n = len(calls)
-    free, issued, end, why = {q: (0.0, None) for q in "VSPGYA"}, [0.0] * n, [0.0] * n, [None] * n
-    bank, engines = [(0.0, None)] * 8, 0.0
-    for i, q in seq:
-        c = calls[i]
-        t, why[i] = free[q]
-        for j, landed, waits in c["needs"]:
+    if same < 64:
+        free, issued, end, why = {q: (0.0, None) for q in "VSPGYA"}, [0.0] * n, [0.0] * n, [None] * n
+        bank, engines, kept, at = [(0.0, None)] * 8, 0.0, [], 0
+    else:
+        why, issued, end, kept, at = list(earlier[2]), list(earlier[3]), list(earlier[4]), earlier[5][:same // 64], same // 64 * 64
+        free, bank, engines = dict(earlier[5][same // 64][0]), list(earlier[5][same // 64][1]), earlier[5][same // 64][2]
+    for p in range(at, n):
+        if not p % 64:
+            kept.append((dict(free), list(bank), engines))
+        i, q = seq[p]
+        needs, banks, ways, lat, busy = calls[i]["short"]
+        t, w = free[q]
+        for j, landed, waits in needs:
             e = (end[j] if landed else issued[j]) + hop * waits
             if e > t:
-                t, why[i] = e, j
-        if q == "P" and bank[place[c["bank"][0]]][0] > t:
-            t, why[i] = bank[place[c["bank"][0]]]
-        issued[i] = t + c["ways"][q] * (tensor if q == "P" else dma if c["lat"] else compute)
-        end[i] = issued[i] + c["lat"] - c["busy"]
-        if c["busy"]:
-            end[i] = engines = max(end[i], engines) + c["busy"] * dma
-        if q != "A":
-            free[q] = (issued[i], i)
-        if q != "P":
-            for v in c["bank"]:
-                bank[place[v]] = max(bank[place[v]], (end[i] + hop, i))
-    return max(end), end.index(max(end)), why
+                t, w = e, j
+        if q == "P":
+            if bank[place[banks[0]]][0] > t:
+                t, w = bank[place[banks[0]]]
+            issued[i] = end[i] = t = t + ways[q] * tensor
+            free[q] = (t, i)
+        elif lat:
+            issued[i] = t = t + ways[q] * dma
+            end[i] = engines = max(t + lat - busy, engines) + busy * dma
+            free[q] = (t, i)
+        else:
+            issued[i] = end[i] = t = t + ways[q] * compute
+            if q != "A":
+                free[q] = (t, i)
+            for v in banks:
+                if bank[place[v]][0] < t + hop:
+                    bank[place[v]] = (t + hop, i)
+        why[i] = w
+    return max(end), end.index(max(end)), why, issued, end, kept
 
 
 def polish(calls, seq, place):
@@ -234,10 +255,10 @@ def polish(calls, seq, place):
             before = users.setdefault(place[v], [])
             hard[i].update(j for j, w in before if w != v)
             before[:] = [e for e in before if e[1] == v] + [(i, v)] if q == "P" else before + [(i, v)]
-    now, seed = [replay(calls, seq, place, *m) for m in MACHINES], 7
+    now, seed, at = [replay(calls, seq, place, *m) for m in MACHINES], 7, {j: p for p, (j, q) in enumerate(seq)}
     for k in range(POLISH):
-        took, i, why = now[k % len(MACHINES)]
-        at, pairs = {j: p for p, (j, q) in enumerate(seq)}, []
+        took, i, why = now[k % len(MACHINES)][:3]
+        pairs = []
         while why[i] is not None:
             if why[i] not in hard[i]:
                 pairs.append((why[i], i))
@@ -260,10 +281,12 @@ def polish(calls, seq, place):
             if any(j in hard[h] for h, q in seq[at[j] + 1:at[i]]):
                 continue
             new.insert(at[i], new.pop(at[j]))
-        if replay(calls, new, place, *MACHINES[k % len(MACHINES)])[0] <= took + WARM:
-            then = [replay(calls, new, place, *m) for m in MACHINES]
+        same, one = min(at[i], at[j]), k % len(MACHINES)
+        first = replay(calls, new, place, *MACHINES[one], same, now[one])
+        if first[0] <= took + WARM:
+            then = [first if h == one else replay(calls, new, place, *m, same, now[h]) for h, m in enumerate(MACHINES)]
             if sum(a[0] for a in then) <= sum(a[0] for a in now) + WARM * (1 - k / POLISH):
-                now, seq = then, new
+                now, seq, at = then, new, {j: p for p, (j, q) in enumerate(new)}
     return seq
 
 
@@ -274,6 +297,7 @@ def arrange(calls):
         c["bank"] = sorted({r[1] // 512 for r in c["reads"] + c["writes"] if r[0] == "ps"})
         c["needs"] = [(j, d in (0.0, HOP), d > 0 if d in (0.0, HOP) else d + calls[j]["lat"] > 0) for j, d in c["pred"].items()
                       if not any(calls[k]["pred"].get(j) == HOP and e == HOP for k, e in c["pred"].items())]
+        c["short"] = (c["needs"], c["bank"], c["ways"], c["lat"], c["busy"])
         for j, d in c["pred"].items():
             succ[j][i] = d
     chain, line, best = [0.0] * len(calls), {}, None
@@ -283,7 +307,7 @@ def arrange(calls):
         chain[i] = span + max([0.0] + [d + chain[k] for k, d in succ[i].items()])
         if c["line"]:
             chain[i] = line[c["line"]] = max(chain[i], span + line.get(c["line"], 0.0))
-    seed = 1
+    seed, tried = 1, []
     for k in range(PASSES):
         shaken = []
         for a, c in zip(chain, calls):
@@ -292,8 +316,21 @@ def arrange(calls):
         end, seq, place = lay(calls, pred, succ, shaken, True)
         took = sum(replay(calls, seq, place, *m)[0] for m in MACHINES)
         if best is None or took < best[0]:
-            best = (took, seq, place)
+            best = (took, seq, place, shaken)
+        tried.append(shaken)
         chain = [(a + b) / 2 for a, b in zip(lay(calls, succ, pred, end, False)[0], chain)]
+    for k in range(AGAIN):
+        seed = seed * 48271 % 2147483647
+        other, mine = tried[seed % len(tried)], [i for i, c in enumerate(calls) if c["round"] == k % len(STEP)]
+        shift = sum(best[3][i] - other[i] for i in mine) / len(mine)
+        shaken = list(best[3])
+        for i in mine:
+            seed = seed * 48271 % 2147483647
+            shaken[i] = other[i] + shift if k // len(STEP) % 2 == 0 else shaken[i] + SHAKE * (seed / 2147483647 - 0.5)
+        end, seq, place = lay(calls, pred, succ, shaken, True)
+        took = sum(replay(calls, seq, place, *m)[0] for m in MACHINES)
+        if took < best[0]:
+            best = (took, seq, place, shaken)
     return polish(calls, best[1], best[2]), best[2]
 
 
@@ -359,11 +396,12 @@ def rank_program(g, core, T, topo):
                     old[:] = [e for e in old if e[0] != r]
                 old.append((r, w, q, sem, val))
 
+    now = [0]
     line = [None]
 
     def record(ways, issue, reads, writes, lat=0.0, busy=0.0, after=None, bulk=False):
         calls.append(dict(ways=ways, issue=issue, reads=reads, writes=writes, lat=lat + busy, busy=busy, after=after or {}, bulk=bulk,
-                          line=line[0] and (line[0], list(ways)[0])))
+                          line=line[0] and (line[0], list(ways)[0]), round=now[0]))
         return len(calls) - 1
 
     def op(forms, reads, writes, bulk=False):
@@ -389,7 +427,7 @@ def rank_program(g, core, T, topo):
         def view(r):
             return ap(r).bitcast(dt.uint8) if SCRATCH[r[0]][2] == MX else ap(r)
         dmas(q, sem, [(view(o), view(i), [i] + more, [o]) for o, i, more in pairs],
-             sum((o[5] - o[4]) * size(o) * SIZE[SCRATCH[o[0]][2]] for o, i, more in pairs))
+             sum(len(range(*o[4:])) * size(o) * SIZE[SCRATCH[o[0]][2]] for o, i, more in pairs))
 
     def regs(a):
         return [a[0], a[1]] if len(a) == 2 else [a]
@@ -485,9 +523,23 @@ def rank_program(g, core, T, topo):
         calls[k]["after"] = {j: -calls[j]["lat"] for j in ahead[-1:]}
         ahead.append(k)
 
+    def carry(o, a):
+        def call():
+            if count["G"]:
+                wait("G", "G", count["G"])
+            return g.affine_select(ap(o), ap(a), [[0, size(o)]], ALU.is_gt, 0.0, 1, 0)
+        k = op({"G": (0.17 + 2 * CYC * size(o), call)}, [a], [o])
+        calls[k]["after"] = {j: -calls[j]["lat"] for j in ahead[-1:]}
+        calls[k]["after"].update({j: HOP for j in [j for j in ahead if not calls[j]["lat"]][-1:]})
+        ahead.append(k)
+
     def engines(k, d):
         each = [set(topo.engines(T.cores[k], T.cores[(k - d) % n])) for d in STEP]
         return sorted(each[STEP.index(d)] if ALL else each[0] & each[1] & each[2])
+
+    def moving(d, nbytes):
+        ports = [(topo.chip(c), topo.die(c)) for j, c in enumerate(T.cores) if topo.chip(c) != topo.chip(T.cores[(j - d) % n])]
+        return max(ROWS + nbytes / WRITE, 0.1 + nbytes * max(map(ports.count, ports)) / PORT[STEP.index(d)])
 
     def send(d, sem, pieces, token=None):
         rid, pid, _ = topo.addr(T.cores[(rank - d) % n])
@@ -505,7 +557,7 @@ def rank_program(g, core, T, topo):
                     count["go"] += 1
                     note("G", [], [token], "go", count["go"])
             sent.append(record({"G": 0.3 if any(calls[k]["busy"] for k in ahead) else FIRST}, issue, [a], [token] if last else [], REMOTE,
-                               ROWS + size(a) * SIZE[SCRATCH[a[0]][2]] / 1.25e3, {k: -calls[k]["lat"] for k in ahead[-1:]}))
+                               moving(d, 128 * size(a) * SIZE[SCRATCH[a[0]][2]]), {k: -calls[k]["lat"] for k in ahead[-1:]}))
             ahead.append(sent[-1])
 
         def arrive(q):
@@ -537,6 +589,8 @@ def rank_program(g, core, T, topo):
     memset(R("sj"), 0)
     load = dmas("Y", "dn", [(ap(R("ni", 0, 16, 1, c, 128, 8)), T.nb[c, :], [], [R("ni")]) for c in range(4)]
                 + [(ap(R("ni", 16, 32, 1, c, 128, 8)), T.e[c, :], [], [R("ni")]) for c in range(4)], 1 << 14, load)
+    if not LATE:
+        dmas("Y", "dw", [(T.wq[:].bitcast(dt.uint8), T.wc[:], [], [R("wq")]), (T.wsc[:], T.ws[:], [], [R("wsc")])], 5 << 16, load)
     iota(R("jm"), [[1, 128]], 0, -1)
     iota(R("pi", 7, 8), [[0, 1]], 0, 1)
     iota(R("rows", 0, 16), [[16, 16]], 0, 0)
@@ -552,14 +606,14 @@ def rank_program(g, core, T, topo):
         ts(R("et", 3 + 512 * k, 512 + 512 * k, 4), R("jm"), 0.0, ALU.is_equal)
     ts(R("tri"), R("jm"), 0.0, ALU.is_lt, 2.0 ** -100, ALU.mult)
     for b in range(4):
-        quant(R("eq", 256 * b, 256 * b + 240), R("es", 256 * b, 256 * b + 240), R("et", 3 - b, 963 - b))
+        k = 112 + 16 * max([m[b] for m in MADE] + [8 if w[b] == "P" else 4 for w in BORDER])
+        quant(R("eq", 256 * b, 256 * b + k), R("es", 256 * b, 256 * b + k), R("et", 3 - b, 3 - b + 4 * k))
     lin(R("wt", 0, 512, 2), zeros(256), None, F["p112"])
     lin(R("up", 0, 1), F["p112"], None, 128.0)
     lin(R("wt", 1, 512, 2), zeros(256), None, R("up", 0, 1))
     lin(R("wt", 512, 1024, 2), zeros(256), None, F["m"])
     lin(R("wt", 513, 1024, 2), zeros(256), None, F["m"])
     quant(R("cq", 0, 256), R("cs", 0, 256), R("wt", 0, 1024))
-    fill(R("ad"), -0.125)
     fill(R("da"), 256.0)
     lin(R("up", 2, 3), F["m"], -1.0, -1792.0)
     lin(R("da", 7, 128, 8), R("rows", 0, 16), -1.0, R("up", 2, 3))
@@ -574,7 +628,11 @@ def rank_program(g, core, T, topo):
     fill(R("cap", 7, 64, 8), -BIG)
     fill(R("ma", 0, 144, 72), -BIG)
     fill(R("me", 0, 144, 72), -BIG)
-    memset(R("cand"), 0)
+    fill(R("cw", 0, 128, 2), 0.0)
+    fill(R("sg", 0, 128, 2), 0.0)
+    fill(R("kp", 0, 512, 2), 0.0)
+    for h in range(MARKS[0], 9 if MARKS[0] < 8 else 0):
+        fill(R("mk", H + C * h, H + C * h + C), 0.0)
     copy(R("n0"), R("ni"))
     for k in range(4):
         move(R("nf", 16 * k, 16 * k + 16), R("n0", 16 * (k // 2), 16 * (k // 2) + 16))
@@ -589,7 +647,7 @@ def rank_program(g, core, T, topo):
     ts(R("tmp", 0, 16), (R("nt", 32, 64), LNB), 256.0, ALU.mult)
     ts(R("tmp", 16, 32), R("n16"), float(C), ALU.is_ge, float(FAR - C), ALU.mult)
     tt(R("tmp", 32, 48), R("tmp", 0, 16), R("n16"), ALU.add)
-    tt(R("cand", 0, 64, 4), R("tmp", 32, 48), R("tmp", 16, 32), ALU.add)
+    tt(R("cw", 0, 128, 8), R("tmp", 32, 48), R("tmp", 16, 32), ALU.add)
     ts(R("tmp", 48, 64), R("n16"), float(C), ALU.is_ge, -float(C + H), ALU.mult)
     tt(R("tmp", 64, 80), R("tmp", 48, 64), R("n16"), ALU.add)
 
@@ -601,42 +659,67 @@ def rank_program(g, core, T, topo):
             lin(R("ib", 8 * k, 8 * k + 8), R("rows", 16, 24), None, F["ib%d" % k])
         copy(LU2, F["lu2"])
         ts(R("lk"), (R("tmp", 64, 80), LU2), float(H), ALU.add)
+        ts(R("tmp", 96, 112), R("n16"), float(C), ALU.is_ge)
+        lin(R("tmp", 112, 128), R("n16"), 0.75, NEAR - FAR / 4 - 0.75 * C)
+        tt(R("tmp", 80, 96), R("tmp", 96, 112), R("tmp", 112, 128), ALU.mult)
+        for k in range(4):
+            move(R("cw", 2 * k + 1, 128, 8), R("tmp", 80, 96))
+            lin(R("sg", 2 * k + 1, 128, 8), R("tmp", 96, 112), -0.75, 1.0)
 
     def while_the_list_leaves():
         fields(*GROUPS[2])
-        for name, c in (("dc", 0), ("d1", 0), ("d0", 1)):
-            iota(R(name), [[0, size(R(name))]], c, 0)
-        iota(R("d0", 0, 128, 8), [[0, 16]], 0, 0)
+        for name, c in (("dc", 0.0), ("d1", 0.0), ("d0", 1.0)):
+            fill(R(name), c)
+        fill(R("d0", 0, 128, 8), 0.0)
         listed(LX7, R("rows", 0, 4), 1.0, "lx7")
         listed(LF, R("rows", 0, 4), 0.25, "lfl")
         listed(LOE, R("rows", 0, 2), 0.125, "loe")
 
-    def unpack(b, h, x, lo, k):
+    def unpack(b, h, x, lo, k, ninth=True):
         line[0] = "unpack"
         v = mm(("uaq", "uas", 2 * h, 128) if b == "m" else ("eq", "es", 256 * b + 16 * h, 128), x, bulk=True)
         line[0] = None
         if b == "m":
-            move(R("mk", H + lo + C * h, H + lo + C * h + k), ps(v, 0, k))
+            for at in ((0, 8) if h == 0 and ninth else (h,)):
+                move(R("mk", H + lo + C * at, H + lo + C * at + k), ps(v, 0, k))
         else:
-            move(R("win", PL * b + lo + C * h, PL * b + lo + C * h + k), ps(v, 0, k), 0.5)
+            at = PL * b + (NEAR + H * h if lo == FAR else lo + C * h)
+            move(R("win", at, at + k), ps(v, 0, k), 0.5)
 
     def products(x, out):
         move(out, ps(mm(("uaq", "uas", 0, 128), x), 0, size(out)))
 
-    def framed(table, off, name, steps, out):
+    def framed(table, off, name, steps, out, urgent=True):
         for k in range(2):
             lo, hi, half = 128 * k, 128 * k + 128, (64 * k, 64 * k + 64)
-            for j in ((0, 4) if (name, k) == ("e", 0) else (0,)):
-                many = 4 if (name, k) == ("e", 0) else 8
+            for j in ((0, 4) if (name, k, urgent) == ("e", 0, True) else (0,)):
+                many = 4 if (name, k, urgent) == ("e", 0, True) else 8
                 move(R("g" + name, lo + 16 * j, lo + 16 * (j + many)), (table, R(off[0], off[1] + 8 * k + j, off[1] + 8 * k + j + many)))
             turn(R("t" + name, lo, hi), R("g" + name, lo, hi))
             scan(R("m" + name, 72 * k + 1, 72 * k + 65), R("t" + name, lo + 1, hi, 2), R("cap"), ALU.max, ALU.min, -BIG)
             tt(R("k" + name, *half), R("t" + name, lo + 1, hi, 2), R("m" + name, 72 * k, 72 * k + 64), ALU.is_le)
             scan(R(out, *half), R("k" + name, *half), R(steps, *half), ALU.mult, ALU.add)
 
+    def flagged(x, name, k, out):
+        lo, at = 128 * k, 128 * k + (C if name == "e" else 0)
+        turn(R("t" + name, lo, lo + 128), ps(mm(("uaq", "uas", 0, 128), x), 0, 128))
+        scan(R("m" + name, 72 * k + 1, 72 * k + 65), R("t" + name, lo + 1, lo + 128, 2), R("cap"), ALU.max, ALU.min, -BIG)
+        tt(R("kp", at + 1, at + 128, 2), R("t" + name, lo + 1, lo + 128, 2), R("m" + name, 72 * k, 72 * k + 64), ALU.is_le)
+        turn(out, R("kp", at, at + 128))
+
+    def looked(table, off, name, steps, out):
+        for k in range(2):
+            lo = 128 * k + (C if name == "e" else 0)
+            for j in ((0, 4) if (name, k) == ("e", 0) else (0,)):
+                many = 4 if (name, k) == ("e", 0) else 8
+                move(R("gb", lo + 16 * j, lo + 16 * (j + many)), (table, R(off[0], off[1] + 8 * k + j, off[1] + 8 * k + j + many)))
+            turn(R("tb", lo, lo + 128), R("gb", lo, lo + 128))
+            scan(R(out, 64 * k, 64 * k + 64), R("tb", lo + 1, lo + 128, 2), R(steps, 64 * k, 64 * k + 64), ALU.mult, ALU.add)
+
     for r, d in enumerate(STEP):
         qn, sn, lq, lsc, lb, ll = [k + str(r) for k in ("q", "s", "lq", "lsc", "lb", "ll")]
         own, left, gone = (qn, sn, 0, C), ("left%d" % r, 0, 1, 1, 0, 128, 1), ("gone%d" % r, 0, 1, 1, 0, 128, 1)
+        now[0] = r
         came = ("bq", "bs", 128 - H * r, 128)
         border = [R(k, 128 - H * r, 128 - H * r + H) for k in ("bq", "bs")]
 
@@ -648,7 +731,7 @@ def rank_program(g, core, T, topo):
                 quant(hq, hs, R("xin", 512 * k, 512 * k + 512))
             if WHOLE[r]:
                 send(d, "arr%s%d" % ("ab"[k], r), [(hq, R(lq, 128 * k, 128 * k + 128))]
-                     + ([(hs, R(lsc, 128 * k, 128 * k + 128))] if FOUR[r] else [(R(sn), R(lsc))] if k else []), left if k and SOON[r] + TWO[r] else None)
+                     + ([(hs, R(lsc, 128 * k, 128 * k + 128))] if FOUR[r] else [(R(sn), R(lsc))] if k else []), left if k else None)
             down.append(ps(mm(half, U2), 0, 1))
             along.append(ps(mm(U2, half), 0, 128))
         if r or not BOTH:
@@ -669,74 +752,134 @@ def rank_program(g, core, T, topo):
         v = mm(WHI, ("ohq", "ohs", 0, 128), stop=False)
         mm(WLO, ("ohq", "ohs", 0, 128), into=v)
         turn(R("lt"), ps(v, 0, 128))
-        copy(R(lb), R("lt", 0, 128, 32))
+        copy(R(lb, 0, 4), R("lt", 0, 128, 32))
         if r == 0:
             while_the_columns_leave()
         if WHOLE[r]:
             send(d, "arrl%d" % r, [(R(lb), R(ll))], gone)
         else:
-            pick(R(lq, 0, H), R(lsc, 0, H), R(qn), R(sn), R(lb))
+            if FLAGS[r]:
+                for k in range(2):
+                    move(R("pr", 128 * k, 128 * k + 128), ps(mm(("fq", "fs", 0, 128), (qn, sn, 128 * k, 128)), 0, 128))
+                framed(R("pr"), LA, "e", "db", "sk", False)
+                tt(R("tmp", 0, 8), R("sk", 7, 64, 8), R("sk", 71, 128, 8), ALU.add)
+                ts(R(lb, 4, 12), R("tmp", 0, 8), -9.0, ALU.add)
+                send(d, "arra%d" % r, [(R(lb), R(ll))])
+            pick(R(lq, 0, H), R(lsc, 0, H), R(qn), R(sn), R(lb, 0, 4))
             send(d, "arrl%d" % r, [(R(lq, 0, H), border[0]), (R(lsc, 0, H), border[1])], gone)
         if r == 0:
             while_the_list_leaves()
 
-        for j, (b, h) in enumerate([(b, h) for b in range(4) for h in range(2 if b < TWO[r] else 4)] + [("m", h) for h in range(1, 9)]):
+        values, marks = [(b, h) for b in range(4) for h in range(MADE[r][b])], [("m", h) for h in range(0 if FLAGS[r] else 1, MARKS[r])]
+        for j, (b, h) in enumerate(values + marks if MARKS[r] == 8 else marks + values):
             if r and j < EARLY:
                 for k in range(2):
-                    unpack(b, h, (qn, sn, 128 * k, 128), 128 * k, 128)
+                    unpack(b, h, (qn, sn, 128 * k, 128), 128 * k, 128, MARKS[r] == 8)
             else:
-                unpack(b, h, own, 0, C)
-        for b in range(TWO[r]):
-            inside("Y", "sv%d%d" % (r, b), [(R("win", PL * b + 512, PL * b + 1024, 1, p0, p1),
-                                            R("win", PL * b, PL * b + 512, 1, (p0 + 32) % 128, (p1 + 31) % 128 + 1), [left])
-                                           for p0, p1 in ((0, 96), (96, 128))])
+                unpack(b, h, own, 0, C, MARKS[r] == 8)
+        if not FLAGS[r]:
+            for k in range(2):
+                unpack("m", 0, (qn, sn, 128 * k, 128), 128 * k, 128, MARKS[r] == 8)
+        if MARKS[r] == 2:
+            token = [{"l": left, "g": gone}[FIRSTLY[r]]]
+            inside("Y", "sm%d" % r, [(R("mk", H + 512 * j, H + 512 * j + 512, 1, p0, p1, 4), R("mk", H, H + 512, 1, p0 + up, p1 + up, 4), token)
+                                     for j in (1, 2, 3) for p0, p1, up in ((0, 112, 4 * j), (112, 128, 4 * j - 16))]
+                   + [(R("mk", H + 2048, H + 2304, 1, 0, 128, 4), R("mk", H, H + C, 1, 0, 128, 4), token)])
         for b in range(4):
-            inside("Y", "sw%d%d" % (r, b), [(R("win", PL * b + 1024, PL * b + 2048, 1, 64 * k, 64 * k + 64),
-                                            R("win", PL * b, PL * b + 1024, 1, 64 - 64 * k, 128 - 64 * k), [left if b < SOON[r] else gone])
-                                           for k in range(2)])
+            if MADE[r][b] == 2:
+                inside("Y", "sv%d%d" % (r, b), [(R("win", PL * b + 512, PL * b + 1024, 1, p0, p1),
+                                                R("win", PL * b, PL * b + 512, 1, (p0 + 32) % 128, (p1 + 31) % 128 + 1), [left])
+                                               for p0, p1 in ((0, 96), (96, 128))])
+        for b in range(4):
+            lo, hi = PL * b + C * max(0, MADE[r][b] - 4), PL * b + C * (4 - MOVED[r][b])
+            if lo < hi:
+                inside("Y", "sw%d%d" % (r, b), [(R("win", lo + 1024, hi + 1024, 1, 64 * k, 64 * k + 64),
+                                                R("win", lo, hi, 1, 64 - 64 * k, 128 - 64 * k), [left if b < SOON[r] else gone])
+                                               for k in range(2)])
+            for k in range(2 if MOVED[r][b] else 0):
+                carry(R("win", hi + 1024, PL * b + 2048, 1, 64 * k, 64 * k + 64), R("win", hi, PL * b + 1024, 1, 64 - 64 * k, 128 - 64 * k))
         if r == 0:
             inside("Y", "db", [(R("bq", 192, 256), R("q0", 0, H), []), (R("bs", 192, 256), R("s0", 0, H), [])])
-            dmas("Y", "dw", [(T.wq[:].bitcast(dt.uint8), T.wc[:], [R("win", 3 * PL + 2047, 3 * PL + 2048)], [R("wq")]),
-                             (T.wsc[:], T.ws[:], [], [R("wsc")])], 5 << 16)
+            if LATE:
+                dmas("Y", "dw", [(T.wq[:].bitcast(dt.uint8), T.wc[:], [left], [R("wq")]),
+                                 (T.wsc[:], T.ws[:], [], [R("wsc")])], 5 << 16)
         if r == 1:
             dmas("Y", "dv", [(T.vin[:], T.v[:], [R("win", 3 * PL + 2047, 3 * PL + 2048)], [R("vin")])], 1 << 17)
             quant(R("vq"), R("vs"), R("vin"))
-        for k in range(2):
-            products((qn, sn, 128 * k, 128), R("mk", H + 128 * k, H + 128 * k + 128))
-        framed(R("mk", H, H + C), LA, "a", "da", "sa")
+        if FLAGS[r]:
+            for k in range(2):
+                flagged((qn, sn, 128 * k, 128), "a", k, R("kt", H + 128 * k, H + 128 * k + 128))
+            looked(R("kt", H, H + C), LA, "a", "da", "sa")
+        else:
+            framed(R("mk", H, H + C), LA, "a", "da", "sa")
         ts(R("offa"), R("sa", 7, 128, 8), -1.0, ALU.mult)
-        tt(R("pre"), (R("cand"), LP), R("ib"), ALU.add)
+        tt(R("pre"), (R("cw"), LP), R("ib"), ALU.add)
         tt(R("wi"), (R("sa"), LKI), R("pre"), ALU.add)
         ts(R("wr"), R("wi"), MASK, ALU.bitwise_and)
         ts(R("wy"), R("wi"), 1792, ALU.bitwise_and)
-        ts(R("ad", 7, 128, 8), R("wr"), 1 / 2048, ALU.mult)
-        tt(R("wf"), (R("wy"), LX8), R("pat"), ALU.is_equal)
-        tt(R("dk"), R("wf"), R("ad"), ALU.add)
+        tt(R("wf"), (R("wy"), LX8), R("pat"), ALU.subtract)
+        ts(R("dk"), R("wf"), 0.0, ALU.is_equal, -0.125, ALU.add)
+        ts(R("dk", 7, 128, 8), R("wr"), 1 / 2048, ALU.mult)
         for b in range(4):
             move(R("ah", C * b, C * b + C), (R("win", PL * b, PL * b + 2048), R("offa")))
             move(R("af", C * b, C * b + C), R("ah", C * b, C * b + C), 2.0)
 
         if WHOLE[r]:
             for k in range(2):
-                products((lq, lsc, 128 * k, 128), R("pr", 128 * k, 128 * k + 128))
-            move(R("mk", 0, H), (R("pr"), R(ll)))
+                if FLAGS[r]:
+                    flagged((lq, lsc, 128 * k, 128), "e", k, R("kt", H + C + 128 * k, H + C + 128 * k + 128))
+                else:
+                    products((lq, lsc, 128 * k, 128), R("pr", 128 * k, 128 * k + 128))
+            if FLAGS[r]:
+                move(R("kt", 0, H), (R("kt", H + C, H + 2 * C), R(ll)))
+            else:
+                move(R("mk", 0, H), (R("pr"), R(ll)))
             pick(border[0], border[1], R(lq), R(lsc), R(ll))
+        elif FLAGS[r]:
+            for k in range(2):
+                move(R("kt", H + C + 128 * k, H + C + 128 * k + 128), (R("kt", H + 2 * C + H * k, H + 2 * C + H * k + H), R(ll, 4, 12)))
+            move(R("kt", 0, H), (R("kt", H + C, H + 2 * C), R(ll, 0, 4)))
         else:
             products(came, R("mk", 0, H))
         for b in ("m", 0, 1, 2, 3):
-            for h in range(9 if b == "m" else 8):
+            for h in range(8 if b == "m" or BORDER[r][b] == "P" else 4):
                 unpack(b, h, came, FAR, H)
+            if b != "m" and BORDER[r][b] != "P":
+                lo = PL * b + NEAR
+                pairs = [(R("win", lo + C, lo + 2 * C, 1, 64 * k, 64 * k + 64), R("win", lo, lo + C, 1, 64 - 64 * k, 128 - 64 * k), []) for k in range(2)]
+                if BORDER[r][b] == "Y":
+                    inside("Y", "sb%d%d" % (r, b), pairs)
+                for o, i, more in pairs:
+                    if BORDER[r][b] == "G":
+                        carry(o, i)
+                    if BORDER[r][b] == "V":
+                        move(o, i)
 
-        framed(R("mk", 0, H + C), R("lk"), "e", "dk", "sk")
+        if r == TELL and FLAGS[2]:
+            send(STEP[2], "arru", [(R("uaq", 0, 16), R("fuq")), (R("uas", 0, 16), R("fus", 0, 16))])
+            listed(R("l2", 8, 16), R("six", 0, 8), 0.0, "m")
+            pick(R("fq"), R("fs"), R("fuq"), R("fus", 0, 16), R("l2", 8, 16))
+            lin(R("up", 5, 6), F["h"], 256.0, -256.0)
+            lin(R("up", 6, 7), F["h"], -16.0, 112.0)
+            ts(R("kt", H + 2 * C, 2 * H + 2 * C), R("pat", 0, H), R("up", 5, 6), ALU.is_lt)
+            ts(R("kt", 2 * H + 2 * C), (R("rows", 0, 16), R("ls", 0, 4)), R("up", 6, 7), ALU.is_gt)
+            for k in range(2):
+                fill(R("db", H * k, H * k + H), 8.0 ** k)
+
+        if FLAGS[r]:
+            looked(R("kt", 0, H + C), R("lk"), "e", "dk", "sk")
+        else:
+            framed(R("mk", 0, H + C), R("lk"), "e", "dk", "sk")
         for k in range(2):
             ts(R("offm", k, 16, 2), R("sk", 7, 64, 8), 2048.0, ALU.mult, 256.0 * k, ALU.add)
-        ts(R("cand"), (R("sk"), LX7), 2048.0, ALU.mult)
-        c0, c2, c1, c3 = [R("cand", 16 * k, 16 * k + 16) for k in range(4)]
+        move(R("cw", 0, 128, 2), (R("sk"), LX7), 2048.0)
+        scan(R("cv"), R("sg"), R("cw"), ALU.mult, ALU.add)
+        c0, c2, c1, c3 = [R("cv", 32 * k + 1, 32 * k + 32, 2) for k in range(4)]
         tt(R("dc", 0, 64, 4), c0, c1, ALU.subtract)
         tt(R("dc", 1, 64, 4), c3, c2, ALU.subtract)
         tt(R("dc", 2, 64, 4), c1, c0, ALU.subtract)
         tt(R("d1", 0, 128, 8), c2, c0, ALU.subtract)
-        copy(R("d1", 4, 128, 8), c0)
+        move(R("d1", 4, 128, 8), c0)
         for k in range(2):
             lo, hi = 128 * k, 128 * k + 128
             move(R("gm", lo, hi), (R("mk", H), R("offm", 8 * k, 8 * k + 8)))
@@ -781,7 +924,8 @@ def rank_program(g, core, T, topo):
             quant(R("q%d" % (r + 1), 128 * k, 128 * k + 128), R("s%d" % (r + 1), 128 * k, 128 * k + 128), R("xn", 512 * k, 512 * k + 512))
         line[0] = None
 
-    ts(R("sj", 0, 16), R("cand", 0, 64, 4), 8, ALU.arith_shift_right, 7, ALU.bitwise_and)
+    copy(R("cand"), R("cw", 0, 128, 8))
+    ts(R("sj", 0, 16), R("cand"), 8, ALU.arith_shift_right, 7, ALU.bitwise_and)
     copy(R("og"), (R("sj"), LOE))
     turn(R("ot"), R("og"))
     dmas("Y", "oute", [(T.oe[c, :], ap(R("ot", 0, 16, 1, c, 128, 8)), [R("ot")], []) for c in range(4)], 0)

from concourse.mybir import dt, AluOpType as ALU, ActivationFunctionType as ACT

F32, BF, I32, U16, MX, U8 = "float32", "bfloat16", "int32", "uint16", "float8_e4m3fn_x4", "uint8"
STEP = [1, 2, 4]
C, H = 256, 64
FAR, MASK = 4096, 4096 + 2047
NEAR, PL = 2048, 2560
WHOLE = [True, True, False]
FOUR = [False, True, True]
BOTH = False
ALL = True
MADE = [[2, 2, 4, 4], [4, 4, 4, 4], [4, 4, 4, 4]]
TELL = 0
FLAGS = [True, True, True]
LATE = False
MOVED = [[0, 0, 0, 4], [0, 0, 0, 4], [0, 0, 0, 4]]
BORDER = ["YYYP", "YYGP", "YYYP"]
MARKS, FIRSTLY = [8, 2, 8], "lll"
BIG = 1e29
POLISH, WARM = 24000, 0.03
URGENT = 0.3
SPINE = ("dd", "fo", "fd", "rk", "oh", "ohq", "lt", "lb0", "lb1", "lb2", "lq2", "lsc2", "gb", "tb", "kt", "ge", "te", "me", "ke", "sk", "offm", "gm", "tm", "e2", "fl", "d0", "d1", "e5",
         "offb", "ob", "bh", "z", "zq", "rl", "xn", "q1", "q2", "q3", "bq", "bs")
SOON = [0, 0, 1]
EARLY = 6
FUSED = 4
BULK = 4
CYC, PECYC, HOP, LOCAL, REMOTE, ROWS, FIRST = 0.83e-3, 0.6e-3, 0.21, 1.1, 0.9, 0.3, 1.5
WRITE, PORT = 160e3, [300e3, 300e3, 110e3]
AGAIN = 0
PASSES, SLACK, MARGIN, SHAKE = 12, 0.04, 0.05, 0.15
MACHINES = [(0.21, 1.0, 1.0, 1.0), (0.23, 1.12, 0.7, 0.8), (0.18, 1.25, 1.35, 1.0), (0.2, 1.45, 1.2, 1.2), (0.24, 1.3, 1.0, 1.4)]
FIELDS = [
    ("lnb", [([[1, 2], [2, 2], [8, 4]], 0)] * 2, 0),
    ("lki", [([[8, 2], [0, 4], [16, 2]], 7), ([[-8, 2], [0, 4], [16, 2]], 15)], 1),
    ("lp", [([[8, 2], [16, 8]], 0), ([[-8, 2], [16, 8]], 8)], 0),
    ("ib0", [([[16, 2], [1, 16]], 0)], 2), ("ib1", [([[-16, 2], [1, 16]], 16)], 2),
    ("lu2", [([[4, 4], [1, 2]], 0), ([[4, 4], [-1, 2]], 1), ([[4, 4], [1, 2]], 2), ([[4, 4], [-1, 2]], 3)], 0),
    ("lx7", [([[8, 2], [64, 2], [0, 4]], 7), ([[8, 2], [-64, 2], [0, 4]], 71)], 0),
    ("lfl", [([[1, 4], [0, 2], [16, 2]], 0)] * 2, 0), ("loe", [([[1, 2], [4, 4], [8, 2]], 0)] * 2, 0)]
GROUPS = [(0, 3), (3, 6), (6, 9)]
BITS = [("m", 0, 15), ("p112", 0, 112), ("h", 1, 7), ("p1", 0, 1), ("p31", 0, 31), ("m3", 3, 1)]


def _s(n, d):
    return ("sbuf", [128, n], d)


SCRATCH = {
    "ps": ("psum", [128, 4096], F32),
    "xin": _s(1024, BF), "uin": _s(512, BF), "vin": _s(512, BF),
    "wq": _s(512, MX), "wsc": _s(512, U8), "uq": _s(128, MX), "us": _s(128, U8), "vq": _s(128, MX), "vs": _s(128, U8),
    "u2q": _s(128, MX), "u2s": _s(128, U8), "uaq": _s(144, MX), "uas": _s(144, U8),
    "et": _s(1040, BF), "eq": _s(1024, MX), "es": _s(1024, U8),
    "wt": _s(1024, BF), "cq": _s(256, MX), "cs": _s(256, U8),
    "jm": _s(128, BF), "tri": _s(128, BF), "cn": _s(128, BF),
    "fi": _s(32 * len(FIELDS), F32), "ft": _s(32 * len(FIELDS), F32), "rows": _s(32, F32), "up": _s(8, F32),
    "pi": _s(8, I32), "pf": _s(8, F32), "six": _s(16, F32),
    "l2": _s(16, U16), "ls": _s(64, U16), "lk": _s(16, U16),
    "ni": _s(32, I32), "n0": _s(32, F32), "nf": _s(64, F32), "nt": _s(64, F32), "n16": _s(16, F32), "tmp": _s(128, F32),
    "dd": _s(256, BF), "fo": _s(256, BF), "fd": _s(256, BF), "rk": _s(256, BF), "oh": _s(512, BF), "ohq": _s(128, MX), "ohs": _s(128, U8),
    "lt": _s(128, F32),
    "sa": _s(128, F32), "pr": _s(256, F32), "cap": _s(64, F32),
    "ta": _s(256, F32), "ma": _s(144, F32),
    "ge": _s(256, F32), "te": _s(256, F32), "me": _s(144, F32), "ke": _s(128, F32),
    "sk": _s(128, F32), "kp": _s(512, BF), "kt": _s(3 * H + 2 * C, BF),
    "fuq": _s(16, MX), "fus": _s(32, U8), "fq": _s(128, MX), "fs": _s(128, U8), "db": _s(128, F32), "gb": _s(512, BF), "tb": _s(512, BF),
    "offa": _s(16, U16), "pre": _s(16, F32), "wi": _s(16, I32), "wr": _s(16, I32), "wy": _s(16, I32), "ib": _s(16, F32),
    "da": _s(128, F32), "pat": _s(128, F32), "wf": _s(128, F32), "dk": _s(128, F32),
    "offm": _s(32, U16), "sj": _s(32, I32),
    "cand": _s(16, I32), "cv": _s(128, F32), "gm": _s(256, F32), "tm": _s(256, F32),
    "e2": _s(32, F32), "fl": _s(32, F32), "dc": _s(64, F32), "e5": _s(128, F32), "d0": _s(128, F32), "d1": _s(128, F32),
    "offb": _s(16, U16), "ob": _s(16, F32),
    "win": _s(4 * PL, BF), "mk": _s(H + FAR + 9 * C, F32), "sg": _s(128, F32), "cw": _s(128, F32),
    "bq": _s(256, MX), "bs": _s(256, U8),
    "ah": _s(1024, BF), "bh": _s(1024, BF), "af": _s(1024, BF), "z": _s(1024, BF), "zq": _s(256, MX), "zs": _s(256, U8),
    "rl": _s(1024, F32), "xn": _s(1024, BF),
    "og": _s(32, F32), "ot": _s(32, F32), "yb": _s(256, F32),
}
for _r in range(4):
    SCRATCH["q%d" % _r] = _s(256, MX)
    SCRATCH["s%d" % _r] = _s(256, U8)
for _r in range(3):
    SCRATCH["lq%d" % _r] = _s(256, MX)
    SCRATCH["lsc%d" % _r] = _s(256, U8)
    SCRATCH["lb%d" % _r] = SCRATCH["ll%d" % _r] = _s(4 if WHOLE[_r] else 12, U16)
SIZE = {F32: 4, BF: 2, I32: 4, U16: 2, MX: 4, U8: 1}

SEMAPHORES = (["V", "S", "P", "G", "dx0", "dx1", "du", "dw", "dv", "dn", "db", "dz0", "dz1", "dz2", "sent", "go", "arru", "out", "outa", "outy", "oute"]
              + ["%s%d%d" % (a, r, b) for r in range(3) for b in range(4) for a in ("sv", "sw", "sb")]
              + ["%s%d" % (a, r) for r in range(3) for a in ("arra", "arrb", "arrl", "sm")])


def R(name, c0=0, c1=None, step=1, p0=0, p1=128, pstep=1):
    return (name, c0, SCRATCH[name][1][1] if c1 is None else c1, step, p0, p1, pstep)


def size(r):
    return len(range(r[1], r[2], r[3]))


def meets(a, b):
    if a[0] != b[0] or a[5] <= b[4] or b[5] <= a[4] or a[2] <= b[1] or b[2] <= a[1]:
        return False
    if a[3] == b[3]:
        return (a[1] - b[1]) % a[3] == 0
    if a[3] == 1 or b[3] == 1:
        return True
    return bool(set(range(a[1], a[2], a[3])) & set(range(b[1], b[2], b[3])))


def link(calls):
    log = {}
    for i, c in enumerate(calls):
        c["pred"] = dict(c["after"])
        for regs, w in ((c["reads"], False), (c["writes"], True)):
            for r in regs:
                for (o, ow, j) in log.get(r[0] if r[0] != "ps" else r[1] // 512, []):
                    other = list(calls[j]["ways"])
                    if j != i and (((w or ow) and meets(r, o)) or (r[0] == "ps" and (other != list(c["ways"]) or len(other) > 1))):
                        c["pred"][j] = 0.0 if other == ["P"] == list(c["ways"]) else HOP - calls[j]["lat"] * (r[0] not in SCRATCH)
        for regs, w in ((c["reads"], False), (c["writes"], True)):
            for r in regs:
                old = log.setdefault(r[0] if r[0] != "ps" else r[1] // 512, [])
                if w:
                    old[:] = [e for e in old if e[0] != r]
                old.append((r, w, i))


def lay(calls, pred, succ, chain, forward):
    n = len(calls)
    ways, lat = [c["ways"] for c in calls], [c["lat"] for c in calls]
    free, idle = {q: 0.0 for q in "VSPGYA"}, {q: 0 for q in "VSPGYA"}
    lack = [set(p) for p in pred]
    at = [0.0 if forward else lat[i] for i in range(n)]
    ready = {q: {i for i in range(n) if q in ways[i] and not lack[i]} for q in free}
    todo = {q: sorted((i for i in range(n) if [q] == list(ways[i])), key=lambda i: -chain[i]) for q in free}
    left = {}
    for c in calls:
        for v in c["bank"]:
            left[v] = left.get(v, 0) + 1
    banks, last, bulk, place = {b: 0.0 for b in range(8)}, {}, set(), {}
    seq, end, engines = [], [0.0] * n, 0.0

    def when(i):
        if forward and "P" in ways[i] and calls[i]["bank"][0] not in place:
            if not banks or (calls[i]["bulk"] and len(bulk) >= BULK):
                return 1e9
            return max(at[i], min(banks.values()))
        return at[i]

    def guess(i, depth):
        if len(lack[i]) > 3 or (lack[i] and not depth):
            return 1e9
        return max([at[i]] + [max(guess(j, depth - 1), min(free[q] for q in ways[j])) + max(ways[j].values()) + lat[j] + pred[i][j]
                              for j in lack[i]])

    while len(seq) < n:
        t, q = min((max(free[q], min(map(when, ready[q]))), q) for q in free if ready[q])
        now = sorted((i for i in ready[q] if when(i) <= t + 1e-9), key=lambda i: -chain[i])
        if q == "V" and forward:
            now = [i for i in now if len(ways[i]) == 1 or at[i] + MARGIN <= t or not calls[i]["bank"]]
            if not now:
                free[q] = t + 0.03
                continue
        soon = [(max(guess(h, 3), t), h) for h in todo[q][:30] if h not in now and chain[h] > chain[now[-1]]]
        hold = 1e9
        for i in now[:8]:
            dur = ways[i][q]
            late = [e for e, h in soon if chain[h] > chain[i] and e < t + dur - 1e-6
                    and max(e + chain[h], e + ways[h][q] + chain[i]) < max(t + dur + chain[h], t + chain[i]) - SLACK]
            if not late:
                break
            hold = min(hold, min(late))
        else:
            idle[q] += 1
            if idle[q] < 12:
                free[q] = max(hold, t + 0.02)
                continue
            i = now[0]
        idle[q] = 0
        if forward and q == "P" and calls[i]["bank"][0] not in place:
            v = calls[i]["bank"][0]
            place[v] = min(banks, key=lambda b: (banks[b], b))
            del banks[place[v]]
            if calls[i]["bulk"]:
                bulk.add(v)
        end[i] = t + ways[i][q] + (lat[i] if forward else 0.0)
        if calls[i]["busy"] and forward:
            end[i] = engines = max(end[i] - calls[i]["busy"], engines) + calls[i]["busy"]
        if q != "A":
            free[q] = t + ways[i][q]
        for k in ways[i]:
            ready[k].discard(i)
        if len(ways[i]) == 1:
            todo[q].remove(i)
        seq.append((i, q))
        for v in calls[i]["bank"] if forward else []:
            left[v] -= 1
            last[v] = max(last.get(v, 0.0), end[i])
            if not left[v]:
                banks[place[v]] = last[v] + HOP
                bulk.discard(v)
        for k, d in succ[i].items():
            lack[k].discard(i)
            at[k] = max(at[k], end[i] + d + (0.0 if forward else lat[k]))
            if not lack[k]:
                for w in ways[k]:
                    ready[w].add(k)
    return end, seq, place


def replay(calls, seq, place, hop, compute, tensor, dma, same=0, earlier=None):
    n = len(calls)
    if same < 64:
        free, issued, end, why = {q: (0.0, None) for q in "VSPGYA"}, [0.0] * n, [0.0] * n, [None] * n
        bank, engines, kept, at = [(0.0, None)] * 8, 0.0, [], 0
    else:
        why, issued, end, kept, at = list(earlier[2]), list(earlier[3]), list(earlier[4]), earlier[5][:same // 64], same // 64 * 64
        free, bank, engines = dict(earlier[5][same // 64][0]), list(earlier[5][same // 64][1]), earlier[5][same // 64][2]
    for p in range(at, n):
        if not p % 64:
            kept.append((dict(free), list(bank), engines))
        i, q = seq[p]
        needs, banks, ways, lat, busy = calls[i]["short"]
        t, w = free[q]
        for j, landed, waits in needs:
            e = (end[j] if landed else issued[j]) + hop * waits
            if e > t:
                t, w = e, j
        if q == "P":
            if bank[place[banks[0]]][0] > t:
                t, w = bank[place[banks[0]]]
            issued[i] = end[i] = t = t + ways[q] * tensor
            free[q] = (t, i)
        elif lat:
            issued[i] = t = t + ways[q] * dma
            end[i] = engines = max(t + lat - busy, engines) + busy * dma
            free[q] = (t, i)
        else:
            issued[i] = end[i] = t = t + ways[q] * compute
            if q != "A":
                free[q] = (t, i)
            for v in banks:
                if bank[place[v]][0] < t + hop:
                    bank[place[v]] = (t + hop, i)
        why[i] = w
    return max(end), end.index(max(end)), why, issued, end, kept


def polish(calls, seq, place):
    hard, users = [set(c["pred"]) for c in calls], {}
    for i, q in seq:
        for v in calls[i]["bank"]:
            before = users.setdefault(place[v], [])
            hard[i].update(j for j, w in before if w != v)
            before[:] = [e for e in before if e[1] == v] + [(i, v)] if q == "P" else before + [(i, v)]
    now, seed, at = [replay(calls, seq, place, *m) for m in MACHINES], 7, {j: p for p, (j, q) in enumerate(seq)}
    for k in range(POLISH):
        took, i, why = now[k % len(MACHINES)][:3]
        pairs = []
        while why[i] is not None:
            if why[i] not in hard[i]:
                pairs.append((why[i], i))
            i = why[i]
        seed = seed * 48271 % 2147483647
        j, i = pairs[seed % len(pairs)]
        new, kind = list(seq), seed // 4096 % 4
        if kind >= 2:
            who = (j, i)[kind - 2]
            other = [q for q in calls[who]["ways"] if q != seq[at[who]][1]]
            if not other:
                kind -= 2
            else:
                new[at[who]] = (who, other[0])
        if kind == 0:
            if any(at[h] > at[j] for h in hard[i]):
                continue
            new.insert(at[j], new.pop(at[i]))
        if kind == 1:
            if any(j in hard[h] for h, q in seq[at[j] + 1:at[i]]):
                continue
            new.insert(at[i], new.pop(at[j]))
        same, one = min(at[i], at[j]), k % len(MACHINES)
        first = replay(calls, new, place, *MACHINES[one], same, now[one])
        if first[0] <= took + WARM:
            then = [first if h == one else replay(calls, new, place, *m, same, now[h]) for h, m in enumerate(MACHINES)]
            if sum(a[0] for a in then) <= sum(a[0] for a in now) + WARM * (1 - k / POLISH):
                now, seq, at = then, new, {j: p for p, (j, q) in enumerate(new)}
    return seq


def arrange(calls):
    link(calls)
    pred, succ = [c["pred"] for c in calls], [{} for c in calls]
    for i, c in enumerate(calls):
        c["bank"] = sorted({r[1] // 512 for r in c["reads"] + c["writes"] if r[0] == "ps"})
        c["needs"] = [(j, d in (0.0, HOP), d > 0 if d in (0.0, HOP) else d + calls[j]["lat"] > 0) for j, d in c["pred"].items()
                      if not any(calls[k]["pred"].get(j) == HOP and e == HOP for k, e in c["pred"].items())]
        c["short"] = (c["needs"], c["bank"], c["ways"], c["lat"], c["busy"])
        for j, d in c["pred"].items():
            succ[j][i] = d
    chain, line, best = [0.0] * len(calls), {}, None
    for i in reversed(range(len(calls))):
        c = calls[i]
        span = max(c["ways"].values()) + c["lat"]
        chain[i] = span + max([0.0] + [d + chain[k] for k, d in succ[i].items()])
        if c["line"]:
            chain[i] = line[c["line"]] = max(chain[i], span + line.get(c["line"], 0.0))
    seed, tried = 1, []
    for k in range(PASSES):
        shaken = []
        for a, c in zip(chain, calls):
            seed = seed * 48271 % 2147483647
            shaken.append(a + SHAKE * seed / 2147483647 + URGENT * (k % 3) * (c["writes"][:1] != [] and c["writes"][0][0] in SPINE))
        end, seq, place = lay(calls, pred, succ, shaken, True)
        took = sum(replay(calls, seq, place, *m)[0] for m in MACHINES)
        if best is None or took < best[0]:
            best = (took, seq, place, shaken)
        tried.append(shaken)
        chain = [(a + b) / 2 for a, b in zip(lay(calls, succ, pred, end, False)[0], chain)]
    for k in range(AGAIN):
        seed = seed * 48271 % 2147483647
        other, mine = tried[seed % len(tried)], [i for i, c in enumerate(calls) if c["round"] == k % len(STEP)]
        shift = sum(best[3][i] - other[i] for i in mine) / len(mine)
        shaken = list(best[3])
        for i in mine:
            seed = seed * 48271 % 2147483647
            shaken[i] = other[i] + shift if k // len(STEP) % 2 == 0 else shaken[i] + SHAKE * (seed / 2147483647 - 0.5)
        end, seq, place = lay(calls, pred, succ, shaken, True)
        took = sum(replay(calls, seq, place, *m)[0] for m in MACHINES)
        if took < best[0]:
            best = (took, seq, place, shaken)
    return polish(calls, best[1], best[2]), best[2]


ARRANGED = []


def rank_program(g, core, T, topo):
    rank = T.rank_of(core)
    if rank is None:
        return
    n = len(T.cores)
    Q = {"V": g.vector, "S": g.scalar, "P": g.tensor, "G": g, "Y": g.sync}
    calls, place = [], {}
    count = {k: 0 for k in SEMAPHORES}
    known = {k: {} for k in Q}
    clock = {}
    log = {}

    def real(r):
        if r[0] != "ps":
            return r
        shift = 512 * (place[r[1] // 512] - r[1] // 512)
        return (r[0], r[1] + shift, r[2] + shift) + r[3:]

    def ap(r):
        r = real(r)
        if r[6] != 1:
            return T[r[0]][r[4]:r[5]:r[6], r[1]:r[2]]
        if r[3] != 1:
            return T[r[0]][r[4]:r[5], r[1]:r[2]:r[3]]
        return T[r[0]][r[4]:r[5], r[1]:r[2]]

    def wait(q, sem, val):
        if known[q].get(sem, 0) >= val:
            return
        Q[q].wait_ge(T.sem[sem], val)
        known[q][sem] = val
        for s, v in clock.get((sem, val), {}).items():
            if known[q].get(s, 0) < v:
                known[q][s] = v

    def order(q, reads, writes):
        need = {}
        for regs, w in ((reads, False), (writes, True)):
            for r in map(real, regs):
                for (o, ow, oq, sem, val) in log.get(r[0], []):
                    if oq == "P" and q == "P":
                        continue
                    hit = (w or ow) and meets(r, o)
                    if r[0] == "ps" and oq != q and r[1] // 512 == o[1] // 512:
                        hit = True
                    if hit and need.get(sem, 0) < val:
                        need[sem] = val
        for sem in sorted(need, key=lambda s: (s == q, s)):
            wait(q, sem, need[sem])

    def note(q, reads, writes, sem, val):
        clock[(sem, val)] = dict(known[q])
        for regs, w in ((reads, False), (writes, True)):
            for r in map(real, regs):
                old = log.setdefault(r[0], [])
                if w:
                    old[:] = [e for e in old if e[0] != r]
                old.append((r, w, q, sem, val))

    now = [0]
    line = [None]

    def record(ways, issue, reads, writes, lat=0.0, busy=0.0, after=None, bulk=False):
        calls.append(dict(ways=ways, issue=issue, reads=reads, writes=writes, lat=lat + busy, busy=busy, after=after or {}, bulk=bulk,
                          line=line[0] and (line[0], list(ways)[0]), round=now[0]))
        return len(calls) - 1

    def op(forms, reads, writes, bulk=False):
        def issue(q):
            order(q, reads, writes)
            forms[q][1]().then_inc(T.sem[q], 1)
            count[q] += 1
            note(q, reads, writes, q, count[q])
        return record({q: f[0] for q, f in forms.items()}, issue, reads, writes, bulk=bulk)

    def dmas(q, sem, items, nbytes, after=None):
        def issue(q):
            for (o, i, rd, wr) in items:
                order(q, rd, wr)
                Q[q].dma_start(o, i).then_inc(T.sem[sem], 16)
                count[sem] += 16
            for (o, i, rd, wr) in items:
                note(q, rd, wr, sem, count[sem])
        return record({q: 0.05 * len(items)}, issue, [r for i in items for r in i[2]], [r for i in items for r in i[3]],
                      LOCAL, 0.05 + nbytes / 250e3, {} if after is None else {after: -calls[after]["lat"]})

    def inside(q, sem, pairs):
        def view(r):
            return ap(r).bitcast(dt.uint8) if SCRATCH[r[0]][2] == MX else ap(r)
        dmas(q, sem, [(view(o), view(i), [i] + more, [o]) for o, i, more in pairs],
             sum(len(range(*o[4:])) * size(o) * SIZE[SCRATCH[o[0]][2]] for o, i, more in pairs))

    def regs(a):
        return [a[0], a[1]] if len(a) == 2 else [a]

    def src(a):
        return ap(a[0]).indirect(ap(a[1])) if len(a) == 2 else ap(a)

    def plain(o, *ins, twice=False, scalar=False):
        if len(ins[0]) == 2:
            return (0.065 if scalar else 0.05) + 1.5 * CYC * size(o)
        narrow = not scalar and all(SIZE[SCRATCH[r[0]][2]] == 2 for r in (o,) + ins)
        return CYC * max(64, size(o) * ((1.5 if narrow else 2) if twice else 0.5 if narrow else 1))

    def val(s):
        return ap(s) if isinstance(s, tuple) else s

    def v_copy(o, a):
        return plain(o, a), lambda: g.vector.tensor_copy(ap(o), src(a))

    def v_ts(o, a, s1, op0, s2=None, op1=None):
        if op1 is None:
            return plain(o, a), lambda: g.vector.tensor_scalar(ap(o), src(a), val(s1), None, op0)
        return plain(o, a), lambda: g.vector.tensor_scalar(ap(o), src(a), val(s1), val(s2), op0, op1)

    def s_act(o, a, func, scale=None, bias=None):
        kw = {k: s for k, s in (("scale", scale), ("bias", bias)) if s is not None}
        return plain(o, a, scalar=True), lambda: g.scalar.activation(ap(o), src(a), func, **{k: val(s) for k, s in kw.items()})

    def cols(*s):
        return [c for c in s if isinstance(c, tuple)]

    def copy(o, a):
        op({"V": v_copy(o, a)}, regs(a), [o])

    def ts(o, a, s1, op0, s2=None, op1=None):
        op({"V": v_ts(o, a, s1, op0, s2, op1)}, regs(a) + cols(s1, s2), [o])

    def act(o, a, func=ACT.Copy, scale=None, bias=None):
        op({"S": s_act(o, a, func, scale, bias)}, regs(a) + cols(scale, bias), [o])

    def lin(o, a, scale=None, bias=None):
        op({"S": s_act(o, a, ACT.Identity, scale, bias), "V": v_ts(o, a, scale or 1.0, ALU.mult, bias or 0.0, ALU.add)},
           [a] + cols(scale, bias), [o])

    def move(o, a, scale=None):
        op({"S": s_act(o, a, ACT.Copy, scale), "V": v_copy(o, a) if scale is None else v_ts(o, a, scale, ALU.mult)}, regs(a), [o])

    def tt(o, a, b, alu):
        op({"V": (plain(o, a, b, twice=a[0] != "ps"), lambda: g.vector.tensor_tensor(ap(o), src(a), ap(b), alu))}, regs(a) + [b], [o])

    def memset(o, c):
        op({"V": (plain(o, o), lambda: g.vector.memset(ap(o), c))}, [], [o])

    def zeros(k):
        return R("et", 0, 4 * k, 4)

    def fill(o, c):
        op({"S": s_act(o, zeros(size(o)), ACT.Identity, None, c), "V": (plain(o, o), lambda: g.vector.memset(ap(o), c))}, [zeros(size(o))], [o])

    def turn(o, a):
        op({"V": (plain(o, a), lambda: g.vector.transpose(ap(o), ap(a)))}, [a], [o])

    def scan(o, a, b, op0, op1, first=0.0):
        op({"V": (plain(o, a, b), lambda: g.vector.tensor_tensor_scan(ap(o), ap(a), ap(b), first, op0, op1))}, [a, b], [o])

    def quant(oq, osc, a):
        op({"V": (0.012 + 0.22e-3 * size(a), lambda: g.vector.quantize_mx(ap(oq), ap(osc), ap(a)))}, [a], [oq, osc])

    def pick(oq, osc, wq, ws, off):
        op({"V": (plain(oq, (wq, off)), lambda: g.vector.tensor_copy(ap(oq).bitcast(dt.uint32), ap(wq).bitcast(dt.uint32).indirect(ap(off))))},
           [wq, off], [oq])
        move(osc, (ws, off))

    results = [0]

    def mm(w, x, into=None, stop=True, bulk=False):
        if into is None:
            results[0] += 1
        v = results[0] if into is None else into
        rs = [R(w[0], w[2], w[2] + w[3]), R(w[1], w[2], w[2] + w[3]), R(x[0], x[2], x[2] + x[3]), R(x[1], x[2], x[2] + x[3])]
        o = ps(v, 0, x[3])
        op({"P": (PECYC * (x[3] + 16), lambda: g.tensor.matmul_mx(ap(o), ap(rs[0]), ap(rs[1]), ap(rs[2]), ap(rs[3]), into is None, stop))},
           rs, [o], bulk)
        return v

    def ps(v, c0, c1, p0=0, p1=128):
        return R("ps", 512 * v + c0, 512 * v + c1, 1, p0, p1)

    ahead = []

    def iota(o, pattern, base, cm):
        k = op({"G": (0.13 + 2 * CYC * size(o), lambda: g.iota(ap(o), pattern, base, cm, allow_small_or_imprecise_dtypes=True))}, [], [o])
        calls[k]["after"] = {j: -calls[j]["lat"] for j in ahead[-1:]}
        ahead.append(k)

    def carry(o, a):
        def call():
            if count["G"]:
                wait("G", "G", count["G"])
            return g.affine_select(ap(o), ap(a), [[0, size(o)]], ALU.is_gt, 0.0, 1, 0)
        k = op({"G": (0.17 + 2 * CYC * size(o), call)}, [a], [o])
        calls[k]["after"] = {j: -calls[j]["lat"] for j in ahead[-1:]}
        calls[k]["after"].update({j: HOP for j in [j for j in ahead if not calls[j]["lat"]][-1:]})
        ahead.append(k)

    def engines(k, d):
        each = [set(topo.engines(T.cores[k], T.cores[(k - d) % n])) for d in STEP]
        return sorted(each[STEP.index(d)] if ALL else each[0] & each[1] & each[2])

    def moving(d, nbytes):
        ports = [(topo.chip(c), topo.die(c)) for j, c in enumerate(T.cores) if topo.chip(c) != topo.chip(T.cores[(j - d) % n])]
        return max(ROWS + nbytes / WRITE, 0.1 + nbytes * max(map(ports.count, ports)) / PORT[STEP.index(d)])

    def send(d, sem, pieces, token=None):
        rid, pid, _ = topo.addr(T.cores[(rank - d) % n])
        sent = []
        for a, o in pieces:
            last = token and (a, o) == pieces[-1]

            def issue(q, a=a, o=o, last=last):
                order("G", [a], [])
                cast = [ap(k).bitcast(dt.uint8) if SCRATCH[k[0]][2] == MX else ap(k) for k in (o, a)]
                g.remote_dma(cast[0], cast[1], T.sem[sem], T.sem.sent, pid, rid, sum(1 << e for e in engines(rank, d)))
                count["sent"] += len(engines(rank, d))
                if last:
                    g.sem_inc(T.sem.go, 1)
                    count["go"] += 1
                    note("G", [], [token], "go", count["go"])
            sent.append(record({"G": 0.3 if any(calls[k]["busy"] for k in ahead) else FIRST}, issue, [a], [token] if last else [], REMOTE,
                               moving(d, 128 * size(a) * SIZE[SCRATCH[a[0]][2]]), {k: -calls[k]["lat"] for k in ahead[-1:]}))
            ahead.append(sent[-1])

        def arrive(q):
            count[sem] = len(pieces) * len(engines((rank + d) % n, d))
            note("G", [], [o for a, o in pieces], sem, count[sem])
            clock[(sem, count[sem])] = {}
        record({"A": 0.0}, arrive, [], [o for a, o in pieces], after={k: 0.0 for k in sent})

    U2, WHI, WLO = ("u2q", "u2s", 0, 128), ("cq", "cs", 0, 128), ("cq", "cs", 128, 128)
    LX8, LUM, LNB, LKI, LP, LU2, LOE, LA, LX7, LF = [R("ls", a, b) for a, b in (
        (0, 8), (16, 25), (26, 27), (28, 29), (30, 31), (32, 33), (38, 40), (40, 56), (56, 60), (60, 64))]
    F = {f[0]: R("ft", 32 * k, 32 * k + 1) for k, f in enumerate(FIELDS)}
    F.update({f[0]: R("pf", k, k + 1) for k, f in enumerate(BITS)})

    def fields(lo, hi):
        for k in range(lo, hi):
            name, pieces, cm = FIELDS[k]
            many = 32 // len(pieces)
            for j, (pattern, base) in enumerate(pieces):
                iota(R("fi", 32 * k + many * j, 32 * k + many * j + many), pattern, base, cm)
        turn(R("ft", 32 * lo, 32 * hi), R("fi", 32 * lo, 32 * hi))

    load = None
    for sem, to, piece in (("dx0", R("xin", 0, 512), T.x[:, 0:512]), ("du", R("uin"), T.u[:]), ("dx1", R("xin", 512, 1024), T.x[:, 512:1024])):
        load = dmas("Y", sem, [(ap(to), piece, [], [to])], 1 << 17, load)
    memset(R("ni"), 0)
    memset(R("et"), 0.0)
    memset(R("l2", 0, 8), 2)
    memset(R("sj"), 0)
    load = dmas("Y", "dn", [(ap(R("ni", 0, 16, 1, c, 128, 8)), T.nb[c, :], [], [R("ni")]) for c in range(4)]
                + [(ap(R("ni", 16, 32, 1, c, 128, 8)), T.e[c, :], [], [R("ni")]) for c in range(4)], 1 << 14, load)
    if not LATE:
        dmas("Y", "dw", [(T.wq[:].bitcast(dt.uint8), T.wc[:], [], [R("wq")]), (T.wsc[:], T.ws[:], [], [R("wsc")])], 5 << 16, load)
    iota(R("jm"), [[1, 128]], 0, -1)
    iota(R("pi", 7, 8), [[0, 1]], 0, 1)
    iota(R("rows", 0, 16), [[16, 16]], 0, 0)
    iota(R("cn"), [[16, 4], [0, 2], [1, 16]], 0, 0)
    fields(*GROUPS[0])
    for k, (name, shift, mask) in enumerate(BITS):
        ts(R("pi", k, k + 1), R("pi", 7, 8), shift, ALU.arith_shift_right, mask, ALU.bitwise_and)
    copy(R("pf", 0, 4), R("pi", 0, 4))
    copy(R("pf", 4, 6), R("pi", 4, 6))
    fill(R("six"), 16.0)
    for k in range(2):
        fill(R("oh", 256 * k, 256 * k + 256), 0.0)
        ts(R("et", 3 + 512 * k, 512 + 512 * k, 4), R("jm"), 0.0, ALU.is_equal)
    ts(R("tri"), R("jm"), 0.0, ALU.is_lt, 2.0 ** -100, ALU.mult)
    for b in range(4):
        k = 112 + 16 * max([m[b] for m in MADE] + [8 if w[b] == "P" else 4 for w in BORDER])
        quant(R("eq", 256 * b, 256 * b + k), R("es", 256 * b, 256 * b + k), R("et", 3 - b, 3 - b + 4 * k))
    lin(R("wt", 0, 512, 2), zeros(256), None, F["p112"])
    lin(R("up", 0, 1), F["p112"], None, 128.0)
    lin(R("wt", 1, 512, 2), zeros(256), None, R("up", 0, 1))
    lin(R("wt", 512, 1024, 2), zeros(256), None, F["m"])
    lin(R("wt", 513, 1024, 2), zeros(256), None, F["m"])
    quant(R("cq", 0, 256), R("cs", 0, 256), R("wt", 0, 1024))
    fill(R("da"), 256.0)
    lin(R("up", 2, 3), F["m"], -1.0, -1792.0)
    lin(R("da", 7, 128, 8), R("rows", 0, 16), -1.0, R("up", 2, 3))

    def listed(to, a, scale, field):
        ts(to, a, scale, ALU.mult, F[field], ALU.add)

    ts(LUM, R("six", 0, 9), F["h"], ALU.mult, F["p1"], ALU.add)
    quant(R("uq"), R("us"), R("uin"))
    pick(R("u2q"), R("u2s"), R("uq"), R("us"), R("l2", 0, 8))
    fill(R("cap"), BIG)
    fill(R("cap", 7, 64, 8), -BIG)
    fill(R("ma", 0, 144, 72), -BIG)
    fill(R("me", 0, 144, 72), -BIG)
    fill(R("cw", 0, 128, 2), 0.0)
    fill(R("sg", 0, 128, 2), 0.0)
    fill(R("kp", 0, 512, 2), 0.0)
    for h in range(MARKS[0], 9 if MARKS[0] < 8 else 0):
        fill(R("mk", H + C * h, H + C * h + C), 0.0)
    copy(R("n0"), R("ni"))
    for k in range(4):
        move(R("nf", 16 * k, 16 * k + 16), R("n0", 16 * (k // 2), 16 * (k // 2) + 16))
    turn(R("nt"), R("nf"))

    pick(R("uaq"), R("uas"), R("uq"), R("us"), LUM)
    for k in range(2):
        listed(R("ls", 40 + k, 56, 2), R("rows", 0, 8), 2.0, "p31")
    listed(LX8, R("rows", 0, 8), 0.125, "m3")
    copy(R("ls", 26, 32, 2), R("ft", 0, 96, 32))
    copy(R("n16"), (R("nt", 0, 32), LNB))
    ts(R("tmp", 0, 16), (R("nt", 32, 64), LNB), 256.0, ALU.mult)
    ts(R("tmp", 16, 32), R("n16"), float(C), ALU.is_ge, float(FAR - C), ALU.mult)
    tt(R("tmp", 32, 48), R("tmp", 0, 16), R("n16"), ALU.add)
    tt(R("cw", 0, 128, 8), R("tmp", 32, 48), R("tmp", 16, 32), ALU.add)
    ts(R("tmp", 48, 64), R("n16"), float(C), ALU.is_ge, -float(C + H), ALU.mult)
    tt(R("tmp", 64, 80), R("tmp", 48, 64), R("n16"), ALU.add)

    def while_the_columns_leave():
        iota(R("rows", 16, 24), [[0, 4], [32, 2]], 1792, 0)
        fields(*GROUPS[1])
        iota(R("pat"), [[0, 16], [-256, 8]], 1536, 0)
        for k in range(2):
            lin(R("ib", 8 * k, 8 * k + 8), R("rows", 16, 24), None, F["ib%d" % k])
        copy(LU2, F["lu2"])
        ts(R("lk"), (R("tmp", 64, 80), LU2), float(H), ALU.add)
        ts(R("tmp", 96, 112), R("n16"), float(C), ALU.is_ge)
        lin(R("tmp", 112, 128), R("n16"), 0.75, NEAR - FAR / 4 - 0.75 * C)
        tt(R("tmp", 80, 96), R("tmp", 96, 112), R("tmp", 112, 128), ALU.mult)
        for k in range(4):
            move(R("cw", 2 * k + 1, 128, 8), R("tmp", 80, 96))
            lin(R("sg", 2 * k + 1, 128, 8), R("tmp", 96, 112), -0.75, 1.0)

    def while_the_list_leaves():
        fields(*GROUPS[2])
        for name, c in (("dc", 0.0), ("d1", 0.0), ("d0", 1.0)):
            fill(R(name), c)
        fill(R("d0", 0, 128, 8), 0.0)
        listed(LX7, R("rows", 0, 4), 1.0, "lx7")
        listed(LF, R("rows", 0, 4), 0.25, "lfl")
        listed(LOE, R("rows", 0, 2), 0.125, "loe")

    def unpack(b, h, x, lo, k, ninth=True):
        line[0] = "unpack"
        v = mm(("uaq", "uas", 2 * h, 128) if b == "m" else ("eq", "es", 256 * b + 16 * h, 128), x, bulk=True)
        line[0] = None
        if b == "m":
            for at in ((0, 8) if h == 0 and ninth else (h,)):
                move(R("mk", H + lo + C * at, H + lo + C * at + k), ps(v, 0, k))
        else:
            at = PL * b + (NEAR + H * h if lo == FAR else lo + C * h)
            move(R("win", at, at + k), ps(v, 0, k), 0.5)

    def products(x, out):
        move(out, ps(mm(("uaq", "uas", 0, 128), x), 0, size(out)))

    def framed(table, off, name, steps, out, urgent=True):
        for k in range(2):
            lo, hi, half = 128 * k, 128 * k + 128, (64 * k, 64 * k + 64)
            for j in ((0, 4) if (name, k, urgent) == ("e", 0, True) else (0,)):
                many = 4 if (name, k, urgent) == ("e", 0, True) else 8
                move(R("g" + name, lo + 16 * j, lo + 16 * (j + many)), (table, R(off[0], off[1] + 8 * k + j, off[1] + 8 * k + j + many)))
            turn(R("t" + name, lo, hi), R("g" + name, lo, hi))
            scan(R("m" + name, 72 * k + 1, 72 * k + 65), R("t" + name, lo + 1, hi, 2), R("cap"), ALU.max, ALU.min, -BIG)
            tt(R("k" + name, *half), R("t" + name, lo + 1, hi, 2), R("m" + name, 72 * k, 72 * k + 64), ALU.is_le)
            scan(R(out, *half), R("k" + name, *half), R(steps, *half), ALU.mult, ALU.add)

    def flagged(x, name, k, out):
        lo, at = 128 * k, 128 * k + (C if name == "e" else 0)
        turn(R("t" + name, lo, lo + 128), ps(mm(("uaq", "uas", 0, 128), x), 0, 128))
        scan(R("m" + name, 72 * k + 1, 72 * k + 65), R("t" + name, lo + 1, lo + 128, 2), R("cap"), ALU.max, ALU.min, -BIG)
        tt(R("kp", at + 1, at + 128, 2), R("t" + name, lo + 1, lo + 128, 2), R("m" + name, 72 * k, 72 * k + 64), ALU.is_le)
        turn(out, R("kp", at, at + 128))

    def looked(table, off, name, steps, out):
        for k in range(2):
            lo = 128 * k + (C if name == "e" else 0)
            for j in ((0, 4) if (name, k) == ("e", 0) else (0,)):
                many = 4 if (name, k) == ("e", 0) else 8
                move(R("gb", lo + 16 * j, lo + 16 * (j + many)), (table, R(off[0], off[1] + 8 * k + j, off[1] + 8 * k + j + many)))
            turn(R("tb", lo, lo + 128), R("gb", lo, lo + 128))
            scan(R(out, 64 * k, 64 * k + 64), R("tb", lo + 1, lo + 128, 2), R(steps, 64 * k, 64 * k + 64), ALU.mult, ALU.add)

    for r, d in enumerate(STEP):
        qn, sn, lq, lsc, lb, ll = [k + str(r) for k in ("q", "s", "lq", "lsc", "lb", "ll")]
        own, left, gone = (qn, sn, 0, C), ("left%d" % r, 0, 1, 1, 0, 128, 1), ("gone%d" % r, 0, 1, 1, 0, 128, 1)
        now[0] = r
        came = ("bq", "bs", 128 - H * r, 128)
        border = [R(k, 128 - H * r, 128 - H * r + H) for k in ("bq", "bs")]

        along, down = [], []
        for k in range(2):
            half = (qn, sn, 128 * k, 128)
            hq, hs = R(qn, 128 * k, 128 * k + 128), R(sn, 128 * k, 128 * k + 128)
            if r == 0:
                quant(hq, hs, R("xin", 512 * k, 512 * k + 512))
            if WHOLE[r]:
                send(d, "arr%s%d" % ("ab"[k], r), [(hq, R(lq, 128 * k, 128 * k + 128))]
                     + ([(hs, R(lsc, 128 * k, 128 * k + 128))] if FOUR[r] else [(R(sn), R(lsc))] if k else []), left if k else None)
            down.append(ps(mm(half, U2), 0, 1))
            along.append(ps(mm(U2, half), 0, 128))
        if r or not BOTH:
            act(R("up", 4, 5), down[0])
            down[0] = R("up", 4, 5)
            act(R("dd", 0, 128), along[0], ACT.Identity, -1.0, down[0])
        else:
            ts(R("dd", 0, 128), along[0], down[0], ALU.subtract, -1.0, ALU.mult)
        ts(R("dd", 128, 256), along[1], down[1], ALU.subtract, -1.0, ALU.mult)
        ts(R("fo", 0, 128), along[1], down[0], ALU.is_gt)
        ts(R("fo", 128, 256), along[0], down[1], ALU.is_ge)
        for k in range(2):
            lo, hi = 128 * k, 128 * k + 128
            tt(R("fd", lo, hi), R("dd", lo, hi), R("tri"), ALU.is_lt)
            scan(R("rk", lo, hi), R("fd", lo, hi), R("fo", lo, hi), ALU.add, ALU.add)
            ts(R("oh", k, 512, 4), R("cn"), R("rk", hi - 1, hi), ALU.is_equal)
        quant(R("ohq"), R("ohs"), R("oh"))
        v = mm(WHI, ("ohq", "ohs", 0, 128), stop=False)
        mm(WLO, ("ohq", "ohs", 0, 128), into=v)
        turn(R("lt"), ps(v, 0, 128))
        copy(R(lb, 0, 4), R("lt", 0, 128, 32))
        if r == 0:
            while_the_columns_leave()
        if WHOLE[r]:
            send(d, "arrl%d" % r, [(R(lb), R(ll))], gone)
        else:
            if FLAGS[r]:
                for k in range(2):
                    move(R("pr", 128 * k, 128 * k + 128), ps(mm(("fq", "fs", 0, 128), (qn, sn, 128 * k, 128)), 0, 128))
                framed(R("pr"), LA, "e", "db", "sk", False)
                tt(R("tmp", 0, 8), R("sk", 7, 64, 8), R("sk", 71, 128, 8), ALU.add)
                ts(R(lb, 4, 12), R("tmp", 0, 8), -9.0, ALU.add)
                send(d, "arra%d" % r, [(R(lb), R(ll))])
            pick(R(lq, 0, H), R(lsc, 0, H), R(qn), R(sn), R(lb, 0, 4))
            send(d, "arrl%d" % r, [(R(lq, 0, H), border[0]), (R(lsc, 0, H), border[1])], gone)
        if r == 0:
            while_the_list_leaves()

        values, marks = [(b, h) for b in range(4) for h in range(MADE[r][b])], [("m", h) for h in range(0 if FLAGS[r] else 1, MARKS[r])]
        for j, (b, h) in enumerate(values + marks if MARKS[r] == 8 else marks + values):
            if r and j < EARLY:
                for k in range(2):
                    unpack(b, h, (qn, sn, 128 * k, 128), 128 * k, 128, MARKS[r] == 8)
            else:
                unpack(b, h, own, 0, C, MARKS[r] == 8)
        if not FLAGS[r]:
            for k in range(2):
                unpack("m", 0, (qn, sn, 128 * k, 128), 128 * k, 128, MARKS[r] == 8)
        if MARKS[r] == 2:
            token = [{"l": left, "g": gone}[FIRSTLY[r]]]
            inside("Y", "sm%d" % r, [(R("mk", H + 512 * j, H + 512 * j + 512, 1, p0, p1, 4), R("mk", H, H + 512, 1, p0 + up, p1 + up, 4), token)
                                     for j in (1, 2, 3) for p0, p1, up in ((0, 112, 4 * j), (112, 128, 4 * j - 16))]
                   + [(R("mk", H + 2048, H + 2304, 1, 0, 128, 4), R("mk", H, H + C, 1, 0, 128, 4), token)])
        for b in range(4):
            if MADE[r][b] == 2:
                inside("Y", "sv%d%d" % (r, b), [(R("win", PL * b + 512, PL * b + 1024, 1, p0, p1),
                                                R("win", PL * b, PL * b + 512, 1, (p0 + 32) % 128, (p1 + 31) % 128 + 1), [left])
                                               for p0, p1 in ((0, 96), (96, 128))])
        for b in range(4):
            lo, hi = PL * b + C * max(0, MADE[r][b] - 4), PL * b + C * (4 - MOVED[r][b])
            if lo < hi:
                inside("Y", "sw%d%d" % (r, b), [(R("win", lo + 1024, hi + 1024, 1, 64 * k, 64 * k + 64),
                                                R("win", lo, hi, 1, 64 - 64 * k, 128 - 64 * k), [left if b < SOON[r] else gone])
                                               for k in range(2)])
            for k in range(2 if MOVED[r][b] else 0):
                carry(R("win", hi + 1024, PL * b + 2048, 1, 64 * k, 64 * k + 64), R("win", hi, PL * b + 1024, 1, 64 - 64 * k, 128 - 64 * k))
        if r == 0:
            inside("Y", "db", [(R("bq", 192, 256), R("q0", 0, H), []), (R("bs", 192, 256), R("s0", 0, H), [])])
            if LATE:
                dmas("Y", "dw", [(T.wq[:].bitcast(dt.uint8), T.wc[:], [left], [R("wq")]),
                                 (T.wsc[:], T.ws[:], [], [R("wsc")])], 5 << 16)
        if r == 1:
            dmas("Y", "dv", [(T.vin[:], T.v[:], [R("win", 3 * PL + 2047, 3 * PL + 2048)], [R("vin")])], 1 << 17)
            quant(R("vq"), R("vs"), R("vin"))
        if FLAGS[r]:
            for k in range(2):
                flagged((qn, sn, 128 * k, 128), "a", k, R("kt", H + 128 * k, H + 128 * k + 128))
            looked(R("kt", H, H + C), LA, "a", "da", "sa")
        else:
            framed(R("mk", H, H + C), LA, "a", "da", "sa")
        ts(R("offa"), R("sa", 7, 128, 8), -1.0, ALU.mult)
        tt(R("pre"), (R("cw"), LP), R("ib"), ALU.add)
        tt(R("wi"), (R("sa"), LKI), R("pre"), ALU.add)
        ts(R("wr"), R("wi"), MASK, ALU.bitwise_and)
        ts(R("wy"), R("wi"), 1792, ALU.bitwise_and)
        tt(R("wf"), (R("wy"), LX8), R("pat"), ALU.subtract)
        ts(R("dk"), R("wf"), 0.0, ALU.is_equal, -0.125, ALU.add)
        ts(R("dk", 7, 128, 8), R("wr"), 1 / 2048, ALU.mult)
        for b in range(4):
            move(R("ah", C * b, C * b + C), (R("win", PL * b, PL * b + 2048), R("offa")))
            move(R("af", C * b, C * b + C), R("ah", C * b, C * b + C), 2.0)

        if WHOLE[r]:
            for k in range(2):
                if FLAGS[r]:
                    flagged((lq, lsc, 128 * k, 128), "e", k, R("kt", H + C + 128 * k, H + C + 128 * k + 128))
                else:
                    products((lq, lsc, 128 * k, 128), R("pr", 128 * k, 128 * k + 128))
            if FLAGS[r]:
                move(R("kt", 0, H), (R("kt", H + C, H + 2 * C), R(ll)))
            else:
                move(R("mk", 0, H), (R("pr"), R(ll)))
            pick(border[0], border[1], R(lq), R(lsc), R(ll))
        elif FLAGS[r]:
            for k in range(2):
                move(R("kt", H + C + 128 * k, H + C + 128 * k + 128), (R("kt", H + 2 * C + H * k, H + 2 * C + H * k + H), R(ll, 4, 12)))
            move(R("kt", 0, H), (R("kt", H + C, H + 2 * C), R(ll, 0, 4)))
        else:
            products(came, R("mk", 0, H))
        for b in ("m", 0, 1, 2, 3):
            for h in range(8 if b == "m" or BORDER[r][b] == "P" else 4):
                unpack(b, h, came, FAR, H)
            if b != "m" and BORDER[r][b] != "P":
                lo = PL * b + NEAR
                pairs = [(R("win", lo + C, lo + 2 * C, 1, 64 * k, 64 * k + 64), R("win", lo, lo + C, 1, 64 - 64 * k, 128 - 64 * k), []) for k in range(2)]
                if BORDER[r][b] == "Y":
                    inside("Y", "sb%d%d" % (r, b), pairs)
                for o, i, more in pairs:
                    if BORDER[r][b] == "G":
                        carry(o, i)
                    if BORDER[r][b] == "V":
                        move(o, i)

        if r == TELL and FLAGS[2]:
            send(STEP[2], "arru", [(R("uaq", 0, 16), R("fuq")), (R("uas", 0, 16), R("fus", 0, 16))])
            listed(R("l2", 8, 16), R("six", 0, 8), 0.0, "m")
            pick(R("fq"), R("fs"), R("fuq"), R("fus", 0, 16), R("l2", 8, 16))
            lin(R("up", 5, 6), F["h"], 256.0, -256.0)
            lin(R("up", 6, 7), F["h"], -16.0, 112.0)
            ts(R("kt", H + 2 * C, 2 * H + 2 * C), R("pat", 0, H), R("up", 5, 6), ALU.is_lt)
            ts(R("kt", 2 * H + 2 * C), (R("rows", 0, 16), R("ls", 0, 4)), R("up", 6, 7), ALU.is_gt)
            for k in range(2):
                fill(R("db", H * k, H * k + H), 8.0 ** k)

        if FLAGS[r]:
            looked(R("kt", 0, H + C), R("lk"), "e", "dk", "sk")
        else:
            framed(R("mk", 0, H + C), R("lk"), "e", "dk", "sk")
        for k in range(2):
            ts(R("offm", k, 16, 2), R("sk", 7, 64, 8), 2048.0, ALU.mult, 256.0 * k, ALU.add)
        move(R("cw", 0, 128, 2), (R("sk"), LX7), 2048.0)
        scan(R("cv"), R("sg"), R("cw"), ALU.mult, ALU.add)
        c0, c2, c1, c3 = [R("cv", 32 * k + 1, 32 * k + 32, 2) for k in range(4)]
        tt(R("dc", 0, 64, 4), c0, c1, ALU.subtract)
        tt(R("dc", 1, 64, 4), c3, c2, ALU.subtract)
        tt(R("dc", 2, 64, 4), c1, c0, ALU.subtract)
        tt(R("d1", 0, 128, 8), c2, c0, ALU.subtract)
        move(R("d1", 4, 128, 8), c0)
        for k in range(2):
            lo, hi = 128 * k, 128 * k + 128
            move(R("gm", lo, hi), (R("mk", H), R("offm", 8 * k, 8 * k + 8)))
            turn(R("tm", lo, hi), R("gm", lo, hi))
        even, odd = R("tm", 0, 128, 4), R("tm", 128, 256, 4)
        tt(R("e2"), odd, even, ALU.max)
        tt(R("fl"), odd, even, ALU.is_gt)
        tt(R("d0", 4, 128, 8), R("e2", 16, 32), R("e2", 0, 16), ALU.is_gt)
        tt(R("d1", 1, 128, 2), (R("fl"), LF), R("dc"), ALU.mult)
        scan(R("e5"), R("d0"), R("d1"), ALU.mult, ALU.add)
        line[0] = "tail"
        for a in range(4):
            for k in range(4):
                i = R("e5", 8 * k + 5, 128, 32, 32 * a, 32 * a + 32)
                if a >= 2:
                    act(R("ob", 4 * a, 4 * a + 4, 1, 32 * k, 32 * k + 32), i)
                else:
                    copy(R("offb", 4 * a, 4 * a + 4, 1, 32 * k, 32 * k + 32), i)
        line[0] = "tail"
        for k in range(2):
            for b in range(4):
                lo = 256 * b + 128 * k
                parts = (R("win", PL * b, PL * b + PL), R("offb", 8 * k, 8 * k + 8))
                if 4 * k + b >= FUSED:
                    act(R("bh", lo, lo + 128), parts)
                    parts = R("bh", lo, lo + 128)
                if (k, b) == (0, 0):
                    for j in range(2):
                        tt(R("z", 256 * j, 256 * j + 256, 4), (parts[0], R("offb", 4 * j, 4 * j + 4)), R("ah", 64 * j, 64 * j + 64), ALU.add)
                    copy(R("offb", 8, 16), R("ob", 8, 16))
                else:
                    tt(R("z", 512 * k + b, 512 * k + 512, 4), parts, R("ah", lo, lo + 128), ALU.add)
            quant(R("zq", 128 * k, 128 * k + 128), R("zs", 128 * k, 128 * k + 128), R("z", 512 * k, 512 * k + 512))
            for b in range(4):
                lo = 256 * b + 128 * k
                v = mm(("wq", "wsc", 128 * b, 128), ("zq", "zs", 128 * k, 128))
                act(R("rl", lo, lo + 128), ps(v, 0, 128), ACT.Relu, 0.03125)
        for k in range(2):
            for b in range(4):
                lo = 256 * b + 128 * k
                tt(R("xn", 512 * k + b, 512 * k + 512, 4), R("rl", lo, lo + 128), R("af", lo, lo + 128), ALU.add)
            quant(R("q%d" % (r + 1), 128 * k, 128 * k + 128), R("s%d" % (r + 1), 128 * k, 128 * k + 128), R("xn", 512 * k, 512 * k + 512))
        line[0] = None

    copy(R("cand"), R("cw", 0, 128, 8))
    ts(R("sj", 0, 16), R("cand"), 8, ALU.arith_shift_right, 7, ALU.bitwise_and)
    copy(R("og"), (R("sj"), LOE))
    turn(R("ot"), R("og"))
    dmas("Y", "oute", [(T.oe[c, :], ap(R("ot", 0, 16, 1, c, 128, 8)), [R("ot")], []) for c in range(4)], 0)
    for k in range(2):
        lo, hi = 128 * k, 128 * k + 128
        v = mm(("vq", "vs", 0, 128), ("q3", "s3", lo, 128))
        act(R("yb", lo, hi), ps(v, 0, 128))
        codes = [(T.oc[:, 4 * lo:4 * hi], T.q3[:, lo:hi].bitcast(dt.uint8), [R("q3", lo, hi)], [])]
        if k == 0:
            dmas("Y", "outa", codes + [(T.y[:, lo:hi], T.yb[:, lo:hi], [R("yb", lo, hi)], [])], 1 << 17)
        else:
            dmas("S", "outy", [(T.y[:, lo:hi], T.yb[:, lo:hi], [R("yb", lo, hi)], [])], 1 << 16)
            dmas("Y", "out", codes + [(T.osc[4 * j:4 * j + 4, :], T.s3[32 * j:32 * j + 4, :], [R("s3")], []) for j in range(4)], 1 << 16)

    if not ARRANGED:
        ARRANGED.extend(arrange(calls))
    place.update(ARRANGED[1])
    for i, q in ARRANGED[0]:
        calls[i]["issue"](q)
    for sem in SEMAPHORES:
        if count[sem]:
            known["G"].pop(sem, None)
            wait("G", sem, count[sem])
